import numpy as np
import ml_dtypes


def mxq(x, axis, fmt="e4m3"):
    dtype, down = {"e4m3": (ml_dtypes.float8_e4m3fn, 7), "e5m2": (ml_dtypes.float8_e5m2, 14)}[fmt]
    v = np.moveaxis(np.asarray(x, np.float32).astype(ml_dtypes.bfloat16).astype(np.float64), axis, -1)
    blocks = v.reshape(v.shape[:-1] + (-1, 32))
    amax = np.abs(blocks).max(-1, keepdims=True)
    byte = np.maximum(np.where(amax > 0, np.frexp(amax)[1] - 1 + 127, 0) - down, 1)
    scale = np.exp2(byte - 127.0)
    codes = (blocks / scale).astype(np.float32).astype(dtype).astype(np.float64)
    return np.moveaxis((codes * scale).reshape(v.shape), -1, axis)


WIDE = False


def mx_kscale(k):
    if not WIDE:
        return np.ones(k)
    levels = np.array([10, -10, 5, -5, 0])
    if k % 512:
        return np.exp2(np.random.permutation(np.resize(levels, k // 32))).repeat(32)
    a = np.empty((k // 512, 16))
    for p in range(k // 512):
        a[p, :8] = np.random.permutation(np.resize(levels, 8))
        for g in range(8):
            far = levels[np.abs(levels - a[p, g]) >= 10]
            a[p, g + 8] = far[np.random.randint(len(far))]
    return np.exp2(a.ravel()).repeat(32)


def f64(x):
    return np.asarray(x).astype(np.float64)


def striped(idx):
    return np.tile(idx.reshape(-1, 16).T, (8, 1)).astype(np.uint16)


def unstriped(offs):
    return offs[:16].T.reshape(-1).astype(np.int64)


def relu(v):
    return np.maximum(v, 0.0)


K, T, E, C, H, N = 1024, 512, 6, 256, 512, 256
TOP = 3


def by_expert(wq, xq):
    return np.concatenate([wq[e].T @ xq[:, e * C:(e + 1) * C] for e in range(E)], axis=1)


def setup_inputs():
    n = np.random.standard_normal
    s = mx_kscale(K)[:, None]
    u = mx_kscale(H)
    deal = np.repeat(np.arange(E), C).reshape(TOP, T)[:, np.random.permutation(T)]
    deal = np.take_along_axis(deal, np.argsort(np.random.rand(TOP, T), axis=0), axis=0)
    for _ in range(8):
        s_, t_ = np.random.permutation(T).reshape(2, -1); r = np.random.randint(TOP, size=T // 2); x, y = deal[r, s_].copy(), deal[r, t_].copy()
        ok = ~((deal[:, s_] == y).any(0) | (deal[:, t_] == x).any(0)); deal[r[ok], s_[ok]] = y[ok]; deal[r[ok], t_[ok]] = x[ok]
    order = np.lexsort((np.random.rand(TOP * T), deal.reshape(-1)))
    slot_token = order % T; pos = np.empty(TOP * T, np.int64); pos[order] = np.arange(TOP * T); pos = pos.reshape(TOP, T)
    g = np.random.uniform(0.5, 1.5, (TOP, T)); g = g / g.sum(0)
    return {
        "xT": (n((K, T)) * s).astype(np.float32),
        "w1": (n((E, K, H)) / np.sqrt(K) / s[None]).astype(np.float32),
        "w3": (n((E, K, H)) / np.sqrt(K) / s[None] * u[None, None, :]).astype(np.float32),
        "w2": (n((E, H, N)) / np.sqrt(H) / u[None, :, None]).astype(np.float32),
        "gate": np.stack([np.tile(r, (N, 1)) for r in g]).astype(np.float32),
        "offs": striped(slot_token),
        "pos1": striped(pos[0]),
        "pos2": striped(pos[1]),
        "pos3": striped(pos[2]),
    }


def reference(xT, w1, w3, w2, gate, offs, pos1, pos2, pos3):
    idx = unstriped(offs)
    xq = mxq(f64(xT)[:, idx], 0, "e4m3")
    h = relu(by_expert(mxq(f64(w1), 1, "e4m3"), xq))
    h = h * by_expert(mxq(f64(w3), 1, "e4m3"), xq)
    y = by_expert(mxq(f64(w2), 1, "e4m3"), mxq(h, 0, "e4m3"))
    return sum(f64(gate[r]) * y[:, unstriped(p)] for r, p in enumerate((pos1, pos2, pos3)))

@@ -1,0 +1,318 @@
+from contextlib import ExitStack
+
+import concourse.mybir as mybir
+
+K, T, E, C, H, N = 1024, 512, 6, 256, 512, 256
+TOP = 3
+SLOTS = E * C
+FLOPS = 2 * SLOTS * (2 * K * H + H * N)
+
+F32 = mybir.dt.float32
+BF16 = mybir.dt.bfloat16
+U32 = mybir.dt.uint32
+U16 = mybir.dt.uint16
+U8 = mybir.dt.uint8
+FP8X4 = mybir.dt.float8_e4m3fn_x4
+MULT = mybir.AluOpType.mult
+ADD = mybir.AluOpType.add
+RELU = mybir.ActivationFunctionType.Relu
+
+P = 128
+PACK = 4
+PASS = P * PACK
+PASSES = K // PASS
+HALVES = 2
+QUAD = 4
+SCALE_STEP = 4
+
+AHEAD = 7
+RAW_BUFS = AHEAD + 2
+EARLY_W2 = 2
+LATE = range(EARLY_W2, E)
+LAST = E - 1
+X_QUADS_ON_VECTOR = 64
+LAST_W3_QUADS_ON_VECTOR = 32
+
+
+def chunk_order():
+    order = [("x", 0, s) for s in range(PASSES)]
+    for e in range(E):
+        order += [(kind, e, s) for kind in ("w1", "w3") for s in range(PASSES)]
+        if e < EARLY_W2:
+            order.append(("w2", e, 0))
+    return order + [("w2", e, 0) for e in LATE]
+
+
+def quads_on_vector(kind, e, s):
+    if kind == "x":
+        return X_QUADS_ON_VECTOR if s == 0 else 0
+    if kind == "w2":
+        return N // QUAD if e < EARLY_W2 or e == LAST else 0
+    if s == 1:
+        return H // QUAD
+    return LAST_W3_QUADS_ON_VECTOR if (kind, e) == ("w3", LAST) else 0
+
+
+def tile_moe_tk_glu_relu_kernel(tc, xT, w1, w3, w2, gate, offs, pos1, pos2, pos3, out):
+    nc = tc.nc
+    with ExitStack() as ctx:
+        keep = ctx.enter_context(tc.tile_pool(name="keep", bufs=1))
+        raws = ctx.enter_context(tc.tile_pool(name="raws", bufs=RAW_BUFS))
+        raws2 = ctx.enter_context(tc.tile_pool(name="raws2", bufs=4))
+        groups = ctx.enter_context(tc.tile_pool(name="groups", bufs=3))
+        codes = ctx.enter_context(tc.tile_pool(name="codes", bufs=4))
+        codes2 = ctx.enter_context(tc.tile_pool(name="codes2", bufs=E))
+        slots = ctx.enter_context(tc.tile_pool(name="slots", bufs=E))
+        hidden = ctx.enter_context(tc.tile_pool(name="hidden", bufs=2))
+        hidden_codes = ctx.enter_context(tc.tile_pool(name="hidden_codes", bufs=E))
+        psum = ctx.enter_context(tc.psum_pool(name="psum", bufs=HALVES))
+        psum_y = ctx.enter_context(tc.psum_pool(name="psum_y", bufs=4))
+
+        offs_sb = keep.tile([P, SLOTS // 16], U16, name="offs_sb")
+        pos_sb = [keep.tile([P, T // 16], U16, name=f"pos_sb{r}") for r in range(TOP)]
+        x_codes = [keep.tile([P, T], U32, name=f"x_codes{s}", align_bytes=64) for s in range(PASSES)]
+        x_scales = keep.tile([P, T], U8, name="x_scales", align_bytes=64)
+        nc.gpsimd.memset(x_scales[:], 0)
+        y_sb = [keep.tile([P, SLOTS], F32, name=f"y_sb{n}") for n in range(HALVES)]
+        gate_sb = [keep.tile([P, TOP, T], F32, name=f"gate_sb{n}") for n in range(HALVES)]
+
+        chunks = chunk_order()
+        raw, grouped, packed = {}, {}, {}
+        slot_codes, relu_a, h_bf, h_packed = {}, {}, {}, {}
+        a_banks, b_banks, y_banks = {}, {}, {}
+
+        def load(chunk):
+            kind, e, s = chunk
+            if kind == "w2":
+                tile = raws2.tile([P, PACK, N], F32, name="raw2")
+                rows = w2[e]
+            else:
+                tile = raws.tile([P, PACK, PASS], F32, name="raw")
+                rows = {"x": xT, "w1": w1[e], "w3": w3[e]}[kind][s * PASS : (s + 1) * PASS, :]
+            nc.sync.dma_start(out=tile[:], in_=rows.rearrange("(p j) w -> p j w", j=PACK))
+            raw[chunk] = tile
+
+        def interleave(chunk):
+            kind, e, s = chunk
+            tile = raw.pop(chunk)
+            if kind == "w2":
+                target = groups.tile([P, PACK * N], BF16, name="grouped2", align_bytes=64)
+                flat = target[:]
+            else:
+                if s == 0:
+                    target = groups.tile([P, PASSES, PACK * PASS], BF16, name="grouped", align_bytes=64)
+                else:
+                    target = grouped[kind, e, 0]
+                flat = target[:, s, :]
+            grouped[chunk] = target
+            source = tile[:].rearrange("p j (m i) -> p m j i", i=QUAD)
+            if kind in ("w1", "w3"):
+                flat = flat.rearrange("p (i m j) -> p m j i", i=QUAD, j=PACK)
+            else:
+                flat = flat.rearrange("p (m i j) -> p m j i", i=QUAD, j=PACK)
+
+            if kind == "w1" and s == 1 and e > 0:
+                h_bf[e - 1] = hidden.tile([P, C, PACK], BF16, name="h_bf", align_bytes=64)
+                nc.vector.tensor_copy(h_bf[e - 1][:, 0:C:P, 0:2], tile[:, 0:2, 0:2])
+            cut = quads_on_vector(kind, e, s)
+            if cut > 0:
+                nc.vector.tensor_copy(out=flat[:, :cut], in_=source[:, :cut])
+            if cut < source.shape[1]:
+                nc.scalar.copy(out=flat[:, cut:], in_=source[:, cut:])
+            if kind == "w3" and s == 1:
+                relu_a[e] = hidden.tile([P, HALVES, P, PACK], F32, name="relu_a")
+                nc.scalar.copy(relu_a[e][:, :, 0, 0], tile[:, 0:HALVES, 0])
+                if 1 <= e <= EARLY_W2:
+                    for n in range(HALVES):
+                        nc.scalar.copy(y_sb[n][:, (e - 1) * C : (e - 1) * C + 1], tile[:, 0, 0:1])
+            if chunk == chunks[-1]:
+                nc.scalar.copy(y_sb[0][:, LATE[0] * C : LAST * C : C], tile[:, 0, 0 : LAST - LATE[0]])
+
+        def quantise(chunk):
+            kind, e, s = chunk
+            source = grouped[chunk]
+            if kind == "x":
+                nc.vector.quantize_mx(
+                    out=x_codes[s][:].bitcast(FP8X4), scales=x_scales[SCALE_STEP * s : P, :], in_=source[:, s, :]
+                )
+                return
+            if kind == "w2":
+                words = codes2.tile([P, N], U32, name="w2_codes", align_bytes=64)
+                scales = codes2.tile([P, N], U8, name="w2_scales", align_bytes=64)
+                nc.vector.quantize_mx(out=words[:].bitcast(FP8X4), scales=scales[:], in_=source[:])
+                packed[kind, e] = (words, scales)
+                return
+            if s == 0:
+                words = codes.tile([P, PASSES, H], U32, name="w_codes", align_bytes=64)
+                scales = codes.tile([P, PASSES, H], U8, name="w_scales", align_bytes=64)
+                packed[kind, e] = (words, scales)
+            words, scales = packed[kind, e]
+            if (kind, e) == ("w3", LAST):
+                nc.vector.quantize_mx(out=words[:, s, :].bitcast(FP8X4), scales=scales[:, s, :], in_=source[:, s, :])
+            elif s == PASSES - 1:
+                nc.vector.quantize_mx(
+                    out=words[:].rearrange("p s w -> p (s w)").bitcast(FP8X4),
+                    scales=scales[:].rearrange("p s w -> p (s w)"),
+                    in_=source[:].rearrange("p s w -> p (s w)"),
+                )
+
+        def gather_tokens(e):
+            entries = offs_sb[:, e * C // 16 : (e + 1) * C // 16]
+            words = []
+            for s in range(PASSES):
+                tile = slots.tile([P, C], U32, name=f"slot_codes{s}", align_bytes=64)
+                nc.vector.tensor_copy(tile[:], x_codes[s][:].indirect(entries))
+                words.append(tile)
+            scales = slots.tile([P, C], U8, name="slot_scales", align_bytes=64)
+            nc.vector.tensor_copy(scales[:], x_scales[:].indirect(entries))
+            slot_codes[e] = (words, scales)
+
+        def first_product(kind, e):
+            banks = []
+            words, scales = packed[kind, e]
+            x_words, slot_scales = slot_codes[e]
+            for half in range(HALVES):
+                bank = psum.tile([P, PACK, P], F32, name="bank_a" if kind == "w1" else "bank_b")
+                cols = slice(half * P, (half + 1) * P)
+                for t in range(PACK):
+                    rows = slice(t * P, (t + 1) * P)
+                    for s in range(PASSES):
+                        nc.tensor.matmul_mx(
+                            out=bank[:, t, :],
+                            lhsT=words[:, s, rows].bitcast(FP8X4),
+                            lhsT_scale=scales[:, s, rows],
+                            rhs=x_words[s][:, cols].bitcast(FP8X4),
+                            rhs_scale=slot_scales[SCALE_STEP * s : P, cols],
+                            start=(s == 0),
+                            stop=(s == PASSES - 1),
+                        )
+                banks.append(bank)
+            return banks
+
+        def take_relu(e):
+            for half in range(HALVES):
+                nc.scalar.activation(
+                    relu_a[e][:, half, :, :], a_banks[e][half][:].rearrange("p t c -> p c t"), RELU
+                )
+
+        def take_h(e):
+            if e not in h_bf:
+                h_bf[e] = hidden.tile([P, C, PACK], BF16, name="h_bf", align_bytes=64)
+            for half in range(HALVES):
+                nc.vector.tensor_tensor(
+                    h_bf[e][:, half * P : (half + 1) * P, :],
+                    b_banks[e][half][:].rearrange("p t c -> p c t"),
+                    relu_a[e][:, half, :, :],
+                    MULT,
+                )
+
+        def quantise_h(e):
+            words = hidden_codes.tile([P, C], U32, name="h_codes", align_bytes=64)
+            scales = hidden_codes.tile([P, C], U8, name="h_scales", align_bytes=64)
+            nc.vector.quantize_mx(
+                out=words[:].bitcast(FP8X4), scales=scales[:], in_=h_bf[e][:].rearrange("p c t -> p (c t)")
+            )
+            h_packed[e] = (words, scales)
+
+        def second_product(e):
+            words, scales = packed["w2", e]
+            h_words, h_scales = h_packed[e]
+            bank = psum_y.tile([P, HALVES, C], F32, name="bank_y")
+            for n in range(HALVES):
+                rows = slice(n * P, (n + 1) * P)
+                nc.tensor.matmul_mx(
+                    out=bank[:, n, :],
+                    lhsT=words[:, rows].bitcast(FP8X4),
+                    lhsT_scale=scales[:, rows],
+                    rhs=h_words[:].bitcast(FP8X4),
+                    rhs_scale=h_scales[:],
+                    start=True,
+                    stop=True,
+                )
+            y_banks[e] = bank
+
+        def copy_y(e, halves):
+            for n in halves:
+                nc.scalar.copy(out=y_sb[n][:, e * C : (e + 1) * C], in_=y_banks[e][:, n, :])
+
+        agenda = {}
+
+        def put_off(step, action, *args):
+            agenda.setdefault(step, []).append((action, args))
+
+        def finish(e, step):
+            if e in h_packed and ("w2", e) in packed and e not in y_banks:
+                second_product(e)
+                if e < EARLY_W2:
+                    put_off(max(step, chunks.index(("w3", e + 1, 1))) + 1, copy_y, e, range(HALVES))
+                else:
+                    put_off(max(step, 0 if e == LAST else len(chunks) - 1) + 1, copy_y, e, (0,))
+
+        def follow(chunk, step):
+            kind, e, s = chunk
+            if kind == "w1" and s == PASSES - 1:
+                a_banks[e] = first_product(kind, e)
+            if kind == "w3" and s == PASSES - 1:
+                take_relu(e)
+                b_banks[e] = first_product(kind, e)
+                put_off(step + 2, take_h, e)
+                put_off(step + 2, quantise_h, e)
+                put_off(step + 2, finish, e, step + 2)
+            if kind == "w2":
+                put_off(step, finish, e, step)
+
+        for e in range(E):
+            put_off(max(PASSES + 1, 4 * e + 1), gather_tokens, e)
+        loaded = 0
+        step = 0
+        while step <= len(chunks) or agenda:
+            while loaded < min(step + AHEAD + 1, len(chunks)):
+                load(chunks[loaded])
+                loaded += 1
+                if loaded == 1:
+                    nc.sync.dma_start(offs_sb[:], offs)
+                if loaded == len(chunks):
+                    for r, pos in enumerate((pos1, pos2, pos3)):
+                        nc.sync.dma_start(pos_sb[r][:], pos)
+                    for n in range(HALVES):
+                        rows = slice(n * P, (n + 1) * P)
+                        nc.sync.dma_start(out=gate_sb[n][:], in_=gate[:, rows, :].rearrange("r p t -> p r t"))
+            if step < len(chunks):
+                interleave(chunks[step])
+            if 1 <= step <= len(chunks):
+                quantise(chunks[step - 1])
+                follow(chunks[step - 1], step)
+            for action, args in agenda.pop(step, []):
+                action(*args)
+            step += 1
+
+        nc.scalar.copy(y_sb[1][:, LATE[0] * C : E * C : C], gate_sb[0][:, 0, 0 : E - LATE[0]])
+        for e in LATE:
+            copy_y(e, (1,))
+
+        def fetch(n, r, cols):
+            part = keep.tile([P, cols.stop - cols.start], F32, name=f"part{n}_{r}_{cols.start}")
+            entries = pos_sb[r][:, cols.start // 16 : cols.stop // 16]
+            nc.vector.tensor_tensor(part[:], y_sb[n][:].indirect(entries), gate_sb[n][:, r, cols], MULT)
+            return part
+
+        def add(name, first, second):
+            total = keep.tile([P, second.shape[1]], F32, name=name)
+            nc.vector.tensor_tensor(total[:], first, second[:], ADD)
+            return total
+
+        tokens = slice(0, T)
+        part0 = fetch(0, 0, tokens)
+        part1 = fetch(0, 1, tokens)
+        part2 = fetch(0, 2, tokens)
+        pair = add("pair0", part0[:], part1)
+        next0 = fetch(1, 0, tokens)
+        result = add("result0", pair[:], part2)
+        nc.sync.dma_start(out=out[0:P, :], in_=result[:])
+        next1 = fetch(1, 1, tokens)
+        pair = add("pair1", next0[:], next1)
+        token_halves = [slice(q * T // 2, (q + 1) * T // 2) for q in range(2)]
+        ends = [fetch(1, 2, cols) for cols in token_halves]
+        for cols, end in zip(token_halves, ends):
+            result = add(f"result1_{cols.start}", pair[:, cols], end)
+            nc.sync.dma_start(out=out[P : 2 * P, cols], in_=result[:])

@@ -1,6 +1,7 @@
 from contextlib import ExitStack
 
 import concourse.mybir as mybir
+from concourse.masks import make_identity
 
 K, T, E, C, H, N = 1024, 512, 6, 256, 512, 256
 TOP = 3
@@ -25,69 +26,79 @@ HALVES = 2
 QUAD = 4
 SCALE_STEP = 4
 
-AHEAD = 7
-RAW_BUFS = AHEAD + 2
-EARLY_W2 = 2
-LATE = range(EARLY_W2, E)
+RING = 12
+AHEAD = RING - 3
+EARLY_W2 = 1
 LAST = E - 1
-X_QUADS_ON_VECTOR = 64
-LAST_W3_QUADS_ON_VECTOR = 32
+X_QUADS_ON_VECTOR = 84
+W_QUADS_ON_VECTOR = 96
+LAST_QUADS_ON_VECTOR = {("w1", 0): 96, ("w1", 1): 32, ("w3", 0): 38, ("w3", 1): 84}
+SLOT_BUFS = 3
 
 
 def chunk_order():
     order = [("x", 0, s) for s in range(PASSES)]
     for e in range(E):
-        order += [(kind, e, s) for kind in ("w1", "w3") for s in range(PASSES)]
-        if e < EARLY_W2:
-            order.append(("w2", e, 0))
-    return order + [("w2", e, 0) for e in LATE]
+        order += [("w1", e, 0), ("w1", e, 1), ("w3", e, 0)]
+        if 1 <= e <= EARLY_W2:
+            order.append(("w2", e - 1, 0))
+        order.append(("w3", e, 1))
+    order += [("w2", e, 0) for e in range(EARLY_W2, E)]
+    return order + [("gate", r, 0) for r in range(TOP)]
 
 
 def quads_on_vector(kind, e, s):
     if kind == "x":
         return X_QUADS_ON_VECTOR if s == 0 else 0
     if kind == "w2":
-        return N // QUAD if e < EARLY_W2 or e == LAST else 0
-    if s == 1:
-        return H // QUAD
-    return LAST_W3_QUADS_ON_VECTOR if (kind, e) == ("w3", LAST) else 0
+        return 0
+    if (kind, e, s) == ("w3", LAST - 1, 1):
+        return 64
+    if e == LAST:
+        return LAST_QUADS_ON_VECTOR[kind, s]
+    return W_QUADS_ON_VECTOR if s == 0 else 0
 
 
 def tile_moe_tk_glu_relu_kernel(tc, xT, w1, w3, w2, gate, offs, pos1, pos2, pos3, out):
     nc = tc.nc
     with ExitStack() as ctx:
         keep = ctx.enter_context(tc.tile_pool(name="keep", bufs=1))
-        raws = ctx.enter_context(tc.tile_pool(name="raws", bufs=RAW_BUFS))
-        raws2 = ctx.enter_context(tc.tile_pool(name="raws2", bufs=4))
+        ring = ctx.enter_context(tc.tile_pool(name="ring", bufs=1))
         groups = ctx.enter_context(tc.tile_pool(name="groups", bufs=3))
         codes = ctx.enter_context(tc.tile_pool(name="codes", bufs=4))
-        codes2 = ctx.enter_context(tc.tile_pool(name="codes2", bufs=E))
-        slots = ctx.enter_context(tc.tile_pool(name="slots", bufs=E))
-        hidden = ctx.enter_context(tc.tile_pool(name="hidden", bufs=2))
-        hidden_codes = ctx.enter_context(tc.tile_pool(name="hidden_codes", bufs=E))
-        psum = ctx.enter_context(tc.psum_pool(name="psum", bufs=HALVES))
-        psum_y = ctx.enter_context(tc.psum_pool(name="psum_y", bufs=4))
+        slots = ctx.enter_context(tc.tile_pool(name="slots", bufs=SLOT_BUFS))
+        psum = ctx.enter_context(tc.psum_pool(name="psum", bufs=1))
 
         offs_sb = keep.tile([P, SLOTS // 16], U16, name="offs_sb")
         pos_sb = [keep.tile([P, T // 16], U16, name=f"pos_sb{r}") for r in range(TOP)]
         x_codes = [keep.tile([P, T], U32, name=f"x_codes{s}", align_bytes=64) for s in range(PASSES)]
         x_scales = keep.tile([P, T], U8, name="x_scales", align_bytes=64)
         nc.gpsimd.memset(x_scales[:], 0)
+        identity = keep.tile([P, P], F32, name="identity")
+        make_identity(nc, identity[:])
         y_sb = [keep.tile([P, SLOTS], F32, name=f"y_sb{n}") for n in range(HALVES)]
-        gate_sb = [keep.tile([P, TOP, T], F32, name=f"gate_sb{n}") for n in range(HALVES)]
 
         chunks = chunk_order()
         raw, grouped, packed = {}, {}, {}
-        slot_codes, relu_a, h_bf, h_packed = {}, {}, {}, {}
-        a_banks, b_banks, y_banks = {}, {}, {}
+        slot_words, slot_scales, relu_a, h_bf, h_packed = {}, {}, {}, {}, {}
+        banks = {}
+
+        def in_buffer_of(chunk, shape, dtype, name):
+            return ring.tile(shape, dtype, name=name, tag=f"ring{chunks.index(chunk) % RING}", align_bytes=64)
 
         def load(chunk):
             kind, e, s = chunk
+            if kind == "gate":
+                nc.sync.dma_start(pos_sb[e][:], (pos1, pos2, pos3)[e])
+                tile = in_buffer_of(chunk, [P, T], F32, "gate_sb")
+                nc.sync.dma_start(out=tile[:], in_=gate[e, 0:P, :])
+                raw[chunk] = tile
+                return
             if kind == "w2":
-                tile = raws2.tile([P, PACK, N], F32, name="raw2")
+                tile = in_buffer_of(chunk, [P, PACK, N], F32, "raw2")
                 rows = w2[e]
             else:
-                tile = raws.tile([P, PACK, PASS], F32, name="raw")
+                tile = in_buffer_of(chunk, [P, PACK, PASS], F32, "raw")
                 rows = {"x": xT, "w1": w1[e], "w3": w3[e]}[kind][s * PASS : (s + 1) * PASS, :]
             nc.sync.dma_start(out=tile[:], in_=rows.rearrange("(p j) w -> p j w", j=PACK))
             raw[chunk] = tile
@@ -110,23 +121,23 @@ def tile_moe_tk_glu_relu_kernel(tc, xT, w1, w3, w2, gate, offs, pos1, pos2, pos3
                 flat = flat.rearrange("p (i m j) -> p m j i", i=QUAD, j=PACK)
             else:
                 flat = flat.rearrange("p (m i j) -> p m j i", i=QUAD, j=PACK)
-
-            if kind == "w1" and s == 1 and e > 0:
-                h_bf[e - 1] = hidden.tile([P, C, PACK], BF16, name="h_bf", align_bytes=64)
-                nc.vector.tensor_copy(h_bf[e - 1][:, 0:C:P, 0:2], tile[:, 0:2, 0:2])
             cut = quads_on_vector(kind, e, s)
             if cut > 0:
                 nc.vector.tensor_copy(out=flat[:, :cut], in_=source[:, :cut])
             if cut < source.shape[1]:
                 nc.scalar.copy(out=flat[:, cut:], in_=source[:, cut:])
-            if kind == "w3" and s == 1:
-                relu_a[e] = hidden.tile([P, HALVES, P, PACK], F32, name="relu_a")
-                nc.scalar.copy(relu_a[e][:, :, 0, 0], tile[:, 0:HALVES, 0])
-                if 1 <= e <= EARLY_W2:
-                    for n in range(HALVES):
-                        nc.scalar.copy(y_sb[n][:, (e - 1) * C : (e - 1) * C + 1], tile[:, 0, 0:1])
-            if chunk == chunks[-1]:
-                nc.scalar.copy(y_sb[0][:, LATE[0] * C : LAST * C : C], tile[:, 0, 0 : LAST - LATE[0]])
+
+        def interleave_half(e, n, target, engine_copy):
+            source = raw["w2", e, 0][:, :, n * P : (n + 1) * P].rearrange("p j (m i) -> p m j i", i=QUAD)
+            engine_copy(out=target.rearrange("p (m i j) -> p m j i", i=QUAD, j=PACK), in_=source)
+
+        def quantise_halves(experts, n, source):
+            words = keep.tile([P, len(experts) * P], U32, name=f"w2_codes{experts[0]}_{n}", align_bytes=64)
+            scales = keep.tile([P, len(experts) * P], U8, name=f"w2_scales{experts[0]}_{n}", align_bytes=64)
+            nc.vector.quantize_mx(out=words[:].bitcast(FP8X4), scales=scales[:], in_=source)
+            for place, e in enumerate(experts):
+                cols = slice(place * P, (place + 1) * P)
+                packed["w2", e, n] = (words[:, cols], scales[:, cols])
 
         def quantise(chunk):
             kind, e, s = chunk
@@ -137,10 +148,11 @@ def tile_moe_tk_glu_relu_kernel(tc, xT, w1, w3, w2, gate, offs, pos1, pos2, pos3
                 )
                 return
             if kind == "w2":
-                words = codes2.tile([P, N], U32, name="w2_codes", align_bytes=64)
-                scales = codes2.tile([P, N], U8, name="w2_scales", align_bytes=64)
+                words = keep.tile([P, N], U32, name=f"w2_codes{e}", align_bytes=64)
+                scales = keep.tile([P, N], U8, name=f"w2_scales{e}", align_bytes=64)
                 nc.vector.quantize_mx(out=words[:].bitcast(FP8X4), scales=scales[:], in_=source[:])
-                packed[kind, e] = (words, scales)
+                for n in range(HALVES):
+                    packed[kind, e, n] = (words[:, n * P : (n + 1) * P], scales[:, n * P : (n + 1) * P])
                 return
             if s == 0:
                 words = codes.tile([P, PASSES, H], U32, name="w_codes", align_bytes=64)
@@ -156,23 +168,23 @@ def tile_moe_tk_glu_relu_kernel(tc, xT, w1, w3, w2, gate, offs, pos1, pos2, pos3
                     in_=source[:].rearrange("p s w -> p (s w)"),
                 )
 
-        def gather_tokens(e):
-            entries = offs_sb[:, e * C // 16 : (e + 1) * C // 16]
-            words = []
-            for s in range(PASSES):
-                tile = slots.tile([P, C], U32, name=f"slot_codes{s}", align_bytes=64)
-                nc.vector.tensor_copy(tile[:], x_codes[s][:].indirect(entries))
-                words.append(tile)
-            scales = slots.tile([P, C], U8, name="slot_scales", align_bytes=64)
-            nc.vector.tensor_copy(scales[:], x_scales[:].indirect(entries))
-            slot_codes[e] = (words, scales)
+        def entries_of(e):
+            return offs_sb[:, e * C // 16 : (e + 1) * C // 16]
+
+        def gather_words(e, s):
+            tile = slots.tile([P, C], U32, name=f"slot_codes{s}", align_bytes=64)
+            nc.vector.tensor_copy(tile[:], x_codes[s][:].indirect(entries_of(e)))
+            slot_words[e, s] = tile
+
+        def gather_scales(e):
+            tile = slots.tile([P, C], U8, name="slot_scales", align_bytes=64)
+            nc.vector.tensor_copy(tile[:], x_scales[:].indirect(entries_of(e)))
+            slot_scales[e] = tile
 
         def first_product(kind, e):
-            banks = []
             words, scales = packed[kind, e]
-            x_words, slot_scales = slot_codes[e]
             for half in range(HALVES):
-                bank = psum.tile([P, PACK, P], F32, name="bank_a" if kind == "w1" else "bank_b")
+                bank = psum.tile([P, PACK, P], F32, name="bank", tag=f"{kind}_{half}")
                 cols = slice(half * P, (half + 1) * P)
                 for t in range(PACK):
                     rows = slice(t * P, (t + 1) * P)
@@ -181,119 +193,139 @@ def tile_moe_tk_glu_relu_kernel(tc, xT, w1, w3, w2, gate, offs, pos1, pos2, pos3
                             out=bank[:, t, :],
                             lhsT=words[:, s, rows].bitcast(FP8X4),
                             lhsT_scale=scales[:, s, rows],
-                            rhs=x_words[s][:, cols].bitcast(FP8X4),
-                            rhs_scale=slot_scales[SCALE_STEP * s : P, cols],
+                            rhs=slot_words[e, s][:, cols].bitcast(FP8X4),
+                            rhs_scale=slot_scales[e][SCALE_STEP * s : P, cols],
                             start=(s == 0),
                             stop=(s == PASSES - 1),
                         )
-                banks.append(bank)
-            return banks
+                banks[kind, e, half] = bank
 
-        def take_relu(e):
+        def take_relu(e, chunk):
+            relu_a[e] = in_buffer_of(chunk, [P, HALVES, P, PACK], F32, "relu_a")
             for half in range(HALVES):
                 nc.scalar.activation(
-                    relu_a[e][:, half, :, :], a_banks[e][half][:].rearrange("p t c -> p c t"), RELU
+                    relu_a[e][:, half, :, :], banks["w1", e, half][:].rearrange("p t c -> p c t"), RELU
                 )
 
-        def take_h(e):
-            if e not in h_bf:
-                h_bf[e] = hidden.tile([P, C, PACK], BF16, name="h_bf", align_bytes=64)
+        def take_h(e, chunk):
+            if e == LAST:
+                h_bf[e] = keep.tile([P, C, PACK], BF16, name="h_last", align_bytes=64)
+            else:
+                h_bf[e] = in_buffer_of(chunk, [P, C, PACK], BF16, "h_bf")
             for half in range(HALVES):
                 nc.vector.tensor_tensor(
                     h_bf[e][:, half * P : (half + 1) * P, :],
-                    b_banks[e][half][:].rearrange("p t c -> p c t"),
+                    banks["w3", e, half][:].rearrange("p t c -> p c t"),
                     relu_a[e][:, half, :, :],
                     MULT,
                 )
 
         def quantise_h(e):
-            words = hidden_codes.tile([P, C], U32, name="h_codes", align_bytes=64)
-            scales = hidden_codes.tile([P, C], U8, name="h_scales", align_bytes=64)
+            words = keep.tile([P, C], U32, name=f"h_codes{e}", align_bytes=64)
+            scales = keep.tile([P, C], U8, name=f"h_scales{e}", align_bytes=64)
             nc.vector.quantize_mx(
                 out=words[:].bitcast(FP8X4), scales=scales[:], in_=h_bf[e][:].rearrange("p c t -> p (c t)")
             )
             h_packed[e] = (words, scales)
 
-        def second_product(e):
-            words, scales = packed["w2", e]
+        def second_product(e, n, target):
+            words, scales = packed["w2", e, n]
             h_words, h_scales = h_packed[e]
-            bank = psum_y.tile([P, HALVES, C], F32, name="bank_y")
+            nc.tensor.matmul_mx(
+                out=target,
+                lhsT=words.bitcast(FP8X4),
+                lhsT_scale=scales,
+                rhs=h_words[:].bitcast(FP8X4),
+                rhs_scale=h_scales[:],
+                start=True,
+                stop=True,
+            )
+
+        def early_y(e):
+            bank = psum.tile([P, HALVES, C], F32, name="bank_y", tag="w1_0")
             for n in range(HALVES):
-                rows = slice(n * P, (n + 1) * P)
-                nc.tensor.matmul_mx(
-                    out=bank[:, n, :],
-                    lhsT=words[:, rows].bitcast(FP8X4),
-                    lhsT_scale=scales[:, rows],
-                    rhs=h_words[:].bitcast(FP8X4),
-                    rhs_scale=h_scales[:],
-                    start=True,
-                    stop=True,
-                )
-            y_banks[e] = bank
+                second_product(e, n, bank[:, n, :])
+            for n in range(HALVES):
+                nc.scalar.copy(out=y_sb[n][:, e * C : (e + 1) * C], in_=bank[:, n, :])
 
-        def copy_y(e, halves):
-            for n in halves:
-                nc.scalar.copy(out=y_sb[n][:, e * C : (e + 1) * C], in_=y_banks[e][:, n, :])
+        def late_y(experts, n, tag, engine_copy=nc.scalar.copy):
+            bank = psum.tile([P, len(experts) * C], F32, name="bank_y", tag=tag)
+            for place, e in enumerate(experts):
+                second_product(e, n, bank[:, place * C : (place + 1) * C])
+            engine_copy(out=y_sb[n][:, experts[0] * C : (experts[-1] + 1) * C], in_=bank[:])
 
-        agenda = {}
+        def late_w2(e):
+            first = keep.tile([P, PACK * P], BF16, name=f"w2_first{e}", tag=f"w2_first{e}", align_bytes=64)
+            interleave_half(e, 0, first[:], nc.vector.tensor_copy if e in (EARLY_W2, LAST - 1, LAST) else nc.scalar.copy)
+            if e == EARLY_W2:
+                take_h(LAST, None)
+            quantise_halves([e], 0, first[:])
+            if e == EARLY_W2 + 1:
+                quantise_h(LAST)
+                late_y([e - 1, e], 0, "y0")
+            if e == LAST - 1:
+                late_y([e - 1, e], 0, "y1")
+            if e == LAST:
+                late_y([e], 0, "y2", nc.vector.tensor_copy)
+                width = PACK * P
+                for experts, tag in (([e - 4, e - 3], "w2_second"), ([e - 2, e - 1, e], f"w2_first{e}")):
+                    second = keep.tile([P, len(experts) * width], BF16, name="w2_second", tag=tag, align_bytes=64)
+                    for place, other in enumerate(experts):
+                        interleave_half(other, 1, second[:, place * width : (place + 1) * width], nc.scalar.copy)
+                    quantise_halves(experts[:2], 1, second[:, : 2 * width])
+                    if len(experts) > 2:
+                        quantise_halves(experts[2:], 1, second[:, 2 * width :])
+                late_y([e - 4, e - 3], 1, "y2")
+                late_y([e - 2, e - 1], 1, "y3")
+                late_y([e], 1, "y0")
 
-        def put_off(step, action, *args):
-            agenda.setdefault(step, []).append((action, args))
-
-        def finish(e, step):
-            if e in h_packed and ("w2", e) in packed and e not in y_banks:
-                second_product(e)
-                if e < EARLY_W2:
-                    put_off(max(step, chunks.index(("w3", e + 1, 1))) + 1, copy_y, e, range(HALVES))
-                else:
-                    put_off(max(step, 0 if e == LAST else len(chunks) - 1) + 1, copy_y, e, (0,))
-
-        def follow(chunk, step):
+        def work(chunk):
             kind, e, s = chunk
-            if kind == "w1" and s == PASSES - 1:
-                a_banks[e] = first_product(kind, e)
-            if kind == "w3" and s == PASSES - 1:
-                take_relu(e)
-                b_banks[e] = first_product(kind, e)
-                put_off(step + 2, take_h, e)
-                put_off(step + 2, quantise_h, e)
-                put_off(step + 2, finish, e, step + 2)
-            if kind == "w2":
-                put_off(step, finish, e, step)
+            if kind == "w2" and e >= EARLY_W2:
+                late_w2(e)
+                return
+            interleave(chunk)
+            if kind == "x":
+                quantise(chunk)
+                for other in range(SLOT_BUFS):
+                    gather_words(other, s)
+                    if s == PASSES - 1:
+                        gather_scales(other)
+            elif kind == "w1":
+                if e > 0 and s == 0:
+                    take_h(e - 1, chunk)
+                    quantise_h(e - 1)
+                    if e - 1 + SLOT_BUFS < E:
+                        for other_pass in range(PASSES):
+                            gather_words(e - 1 + SLOT_BUFS, other_pass)
+                        gather_scales(e - 1 + SLOT_BUFS)
+                quantise(chunk)
+                if s == 1:
+                    first_product(kind, e)
+            elif kind == "w3":
+                quantise(chunk)
+                if s == 1:
+                    take_relu(e, chunk)
+                    if 1 <= e <= EARLY_W2:
+                        early_y(e - 1)
+                    first_product(kind, e)
+            else:
+                quantise(chunk)
 
-        for e in range(E):
-            put_off(max(PASSES + 1, 4 * e + 1), gather_tokens, e)
-        loaded = 0
-        step = 0
-        while step <= len(chunks) or agenda:
-            while loaded < min(step + AHEAD + 1, len(chunks)):
-                load(chunks[loaded])
-                loaded += 1
-                if loaded == 1:
+        for step in range(-AHEAD, len(chunks) - TOP):
+            if step + AHEAD < len(chunks):
+                load(chunks[step + AHEAD])
+                if step + AHEAD == 0:
                     nc.sync.dma_start(offs_sb[:], offs)
-                if loaded == len(chunks):
-                    for r, pos in enumerate((pos1, pos2, pos3)):
-                        nc.sync.dma_start(pos_sb[r][:], pos)
-                    for n in range(HALVES):
-                        rows = slice(n * P, (n + 1) * P)
-                        nc.sync.dma_start(out=gate_sb[n][:], in_=gate[:, rows, :].rearrange("r p t -> p r t"))
-            if step < len(chunks):
-                interleave(chunks[step])
-            if 1 <= step <= len(chunks):
-                quantise(chunks[step - 1])
-                follow(chunks[step - 1], step)
-            for action, args in agenda.pop(step, []):
-                action(*args)
-            step += 1
+            if step >= 0:
+                work(chunks[step])
 
-        nc.scalar.copy(y_sb[1][:, LATE[0] * C : E * C : C], gate_sb[0][:, 0, 0 : E - LATE[0]])
-        for e in LATE:
-            copy_y(e, (1,))
+        gate_sb = [raw["gate", r, 0] for r in range(TOP)]
 
         def fetch(n, r, cols):
             part = keep.tile([P, cols.stop - cols.start], F32, name=f"part{n}_{r}_{cols.start}")
             entries = pos_sb[r][:, cols.start // 16 : cols.stop // 16]
-            nc.vector.tensor_tensor(part[:], y_sb[n][:].indirect(entries), gate_sb[n][:, r, cols], MULT)
+            nc.vector.tensor_tensor(part[:], y_sb[n][:].indirect(entries), gate_sb[r][:, cols], MULT)
             return part
 
         def add(name, first, second):
@@ -302,12 +334,28 @@ def tile_moe_tk_glu_relu_kernel(tc, xT, w1, w3, w2, gate, offs, pos1, pos2, pos3
             return total
 
         tokens = slice(0, T)
-        part0 = fetch(0, 0, tokens)
-        part1 = fetch(0, 1, tokens)
-        part2 = fetch(0, 2, tokens)
-        pair = add("pair0", part0[:], part1)
+        parts = [fetch(0, r, tokens) for r in range(TOP)]
         next0 = fetch(1, 0, tokens)
-        result = add("result0", pair[:], part2)
+        blocks = range(T // P)
+        free_banks = [f"{kind}_{half}" for kind in ("w1", "w3") for half in range(HALVES)]
+        turned = [psum.tile([P, P], F32, name="turned", tag=free_banks[block]) for block in blocks]
+        for r in range(TOP):
+            for block in blocks:
+                nc.tensor.matmul(
+                    turned[block][:],
+                    lhsT=parts[r][:, block * P : (block + 1) * P],
+                    rhs=identity[:],
+                    is_transpose=True,
+                    start=(r == 0),
+                    stop=(r == TOP - 1),
+                )
+        upright = psum.tile([P, T // P, P], F32, name="upright", tag="y1")
+        for block in blocks:
+            turned_sb = keep.tile([P, P], F32, name=f"turned_sb{block}")
+            nc.scalar.copy(out=turned_sb[:], in_=turned[block][:])
+            nc.tensor.transpose(upright[:, block, :], turned_sb[:], identity[:])
+        result = keep.tile([P, T], F32, name="result0")
+        nc.scalar.copy(out=result[:], in_=upright[:].rearrange("p b t -> p (b t)"))
         nc.sync.dma_start(out=out[0:P, :], in_=result[:])
         next1 = fetch(1, 1, tokens)
         pair = add("pair1", next0[:], next1)

@@ -29,6 +29,7 @@ SCALE_STEP = 4
 RING = 12
 AHEAD = RING - 3
 EARLY_W2 = 1
+SPLIT_W2 = 3
 LAST = E - 1
 X_QUADS_ON_VECTOR = 84
 W_QUADS_ON_VECTOR = 96
@@ -43,8 +44,10 @@ def chunk_order():
         if 1 <= e <= EARLY_W2:
             order.append(("w2", e - 1, 0))
         order.append(("w3", e, 1))
-    order += [("w2", e, 0) for e in range(EARLY_W2, E)]
-    return order + [("gate", r, 0) for r in range(TOP)]
+    order += [("w2", e, 0) for e in range(EARLY_W2, SPLIT_W2)]
+    order += [("half", e, 0) for e in range(SPLIT_W2, E)] + [("gate", 0, 0)]
+    order += [("half", SPLIT_W2, 1), ("gate", 1, 0)] + [("half", e, 1) for e in range(SPLIT_W2 + 1, E)]
+    return order + [("gate", 2, 0)]
 
 
 def quads_on_vector(kind, e, s):
@@ -97,6 +100,12 @@ def tile_moe_tk_glu_relu_kernel(tc, xT, w1, w3, w2, gate, offs, pos1, pos2, pos3
             if kind == "w2":
                 tile = in_buffer_of(chunk, [P, PACK, N], F32, "raw2")
                 rows = w2[e]
+            elif kind == "half":
+                if e == LAST:
+                    tile = y_sb[s][:, 2 * C : 4 * C].rearrange("p (j w) -> p j w", j=PACK)
+                else:
+                    tile = in_buffer_of(chunk, [P, PACK, P], F32, "raw_half")
+                rows = w2[e][:, s * P : (s + 1) * P]
             else:
                 tile = in_buffer_of(chunk, [P, PACK, PASS], F32, "raw")
                 rows = {"x": xT, "w1": w1[e], "w3": w3[e]}[kind][s * PASS : (s + 1) * PASS, :]
@@ -128,7 +137,8 @@ def tile_moe_tk_glu_relu_kernel(tc, xT, w1, w3, w2, gate, offs, pos1, pos2, pos3
                 nc.scalar.copy(out=flat[:, cut:], in_=source[:, cut:])
 
         def interleave_half(e, n, target, engine_copy):
-            source = raw["w2", e, 0][:, :, n * P : (n + 1) * P].rearrange("p j (m i) -> p m j i", i=QUAD)
+            columns = raw["half", e, n][:] if e >= SPLIT_W2 else raw["w2", e, 0][:, :, n * P : (n + 1) * P]
+            source = columns.rearrange("p j (m i) -> p m j i", i=QUAD)
             engine_copy(out=target.rearrange("p (m i j) -> p m j i", i=QUAD, j=PACK), in_=source)
 
         def quantise_halves(experts, n, source):
@@ -221,7 +231,8 @@ def tile_moe_tk_glu_relu_kernel(tc, xT, w1, w3, w2, gate, offs, pos1, pos2, pos3
                 )
 
         def quantise_h(e):
-            words = keep.tile([P, C], U32, name=f"h_codes{e}", align_bytes=64)
+            tag = "w2_first2" if e == LAST else f"h_codes{e}"
+            words = keep.tile([P, C], U32, name=f"h_codes{e}", tag=tag, align_bytes=64)
             scales = keep.tile([P, C], U8, name=f"h_scales{e}", align_bytes=64)
             nc.vector.quantize_mx(
                 out=words[:].bitcast(FP8X4), scales=scales[:], in_=h_bf[e][:].rearrange("p c t -> p (c t)")
@@ -254,34 +265,46 @@ def tile_moe_tk_glu_relu_kernel(tc, xT, w1, w3, w2, gate, offs, pos1, pos2, pos3
                 second_product(e, n, bank[:, place * C : (place + 1) * C])
             engine_copy(out=y_sb[n][:, experts[0] * C : (experts[-1] + 1) * C], in_=bank[:])
 
+        width = PACK * P
+        first = {}
+
         def late_w2(e):
-            first = keep.tile([P, PACK * P], BF16, name=f"w2_first{e}", tag=f"w2_first{e}", align_bytes=64)
-            interleave_half(e, 0, first[:], nc.vector.tensor_copy if e in (EARLY_W2, LAST - 1, LAST) else nc.scalar.copy)
             if e == EARLY_W2:
+                alone = keep.tile([P, width], BF16, name="w2_first1", align_bytes=64)
+                interleave_half(e, 0, alone[:], nc.vector.tensor_copy)
+                quantise_halves([e], 0, alone[:])
                 take_h(LAST, None)
-            quantise_halves([e], 0, first[:])
-            if e == EARLY_W2 + 1:
+                return
+            pair, place = e - e % 2, e % 2
+            if place == 0:
+                first[pair] = keep.tile([P, 2 * width], BF16, name=f"w2_first{pair}", tag=f"w2_first{pair}", align_bytes=64)
+            interleave_half(e, 0, first[pair][:, place * width : (place + 1) * width], nc.scalar.copy)
+            if place == 1:
+                quantise_halves([pair, e], 0, first[pair][:])
+            if e == 3:
                 quantise_h(LAST)
-                late_y([e - 1, e], 0, "y0")
-            if e == LAST - 1:
-                late_y([e - 1, e], 0, "y1")
             if e == LAST:
-                late_y([e], 0, "y2", nc.vector.tensor_copy)
-                width = PACK * P
-                for experts, tag in (([e - 4, e - 3], "w2_second"), ([e - 2, e - 1, e], f"w2_first{e}")):
-                    second = keep.tile([P, len(experts) * width], BF16, name="w2_second", tag=tag, align_bytes=64)
-                    for place, other in enumerate(experts):
-                        interleave_half(other, 1, second[:, place * width : (place + 1) * width], nc.scalar.copy)
-                    quantise_halves(experts[:2], 1, second[:, : 2 * width])
-                    if len(experts) > 2:
-                        quantise_halves(experts[2:], 1, second[:, 2 * width :])
-                late_y([e - 4, e - 3], 1, "y2")
-                late_y([e - 2, e - 1], 1, "y3")
-                late_y([e], 1, "y0")
+                late_y([1, 2], 0, "y0")
+                late_y([3], 0, "y1")
+                late_y([4, 5], 0, "y2", nc.vector.tensor_copy)
+                whole = keep.tile([P, 2 * width], BF16, name="w2_second1", tag="w2_first4", align_bytes=64)
+                for place, other in enumerate((1, 2)):
+                    interleave_half(other, 1, whole[:, place * width : (place + 1) * width], nc.vector.tensor_copy)
+                quantise_halves([1, 2], 1, whole[:])
+                split = keep.tile([P, 3 * width], BF16, name="w2_second3", tag="w2_second3", align_bytes=64)
+                for place, other in enumerate((3, 4, 5)):
+                    interleave_half(other, 1, split[:, place * width : (place + 1) * width], nc.scalar.copy)
+                late_y([1, 2], 1, "y3")
+                quantise_halves([3, 4], 1, split[:, : 2 * width])
+                late_y([3, 4], 1, "y0")
+                quantise_halves([5], 1, split[:, 2 * width :])
+                late_y([5], 1, "y2")
 
         def work(chunk):
             kind, e, s = chunk
-            if kind == "w2" and e >= EARLY_W2:
+            if kind == "gate" or (kind, s) == ("half", 1):
+                return
+            if kind in ("w2", "half") and e >= EARLY_W2:
                 late_w2(e)
                 return
             interleave(chunk)
@@ -312,7 +335,7 @@ def tile_moe_tk_glu_relu_kernel(tc, xT, w1, w3, w2, gate, offs, pos1, pos2, pos3
             else:
                 quantise(chunk)
 
-        for step in range(-AHEAD, len(chunks) - TOP):
+        for step in range(-AHEAD, len(chunks)):
             if step + AHEAD < len(chunks):
                 load(chunks[step + AHEAD])
                 if step + AHEAD == 0:
@@ -323,7 +346,9 @@ def tile_moe_tk_glu_relu_kernel(tc, xT, w1, w3, w2, gate, offs, pos1, pos2, pos3
         gate_sb = [raw["gate", r, 0] for r in range(TOP)]
 
         def fetch(n, r, cols):
-            part = keep.tile([P, cols.stop - cols.start], F32, name=f"part{n}_{r}_{cols.start}")
+            name = f"part{n}_{r}_{cols.start}"
+            tag = "w2_second3" if (n, r) == (0, 1) else name
+            part = keep.tile([P, cols.stop - cols.start], F32, name=name, tag=tag, align_bytes=64)
             entries = pos_sb[r][:, cols.start // 16 : cols.stop // 16]
             nc.vector.tensor_tensor(part[:], y_sb[n][:].indirect(entries), gate_sb[r][:, cols], MULT)
             return part

@@ -33,7 +33,7 @@ SPLIT_W2 = 3
 LAST = E - 1
 X_QUADS_ON_VECTOR = 84
 W_QUADS_ON_VECTOR = 96
-LAST_QUADS_ON_VECTOR = {("w1", 0): 96, ("w1", 1): 32, ("w3", 0): 38, ("w3", 1): 84}
+LAST_QUADS_ON_VECTOR = {("w1", 0): 96, ("w1", 1): 32, ("w3", 0): 38, ("w3", 1): 128}
 SLOT_BUFS = 3
 
 
@@ -101,7 +101,7 @@ def tile_moe_tk_glu_relu_kernel(tc, xT, w1, w3, w2, gate, offs, pos1, pos2, pos3
                 tile = in_buffer_of(chunk, [P, PACK, N], F32, "raw2")
                 rows = w2[e]
             elif kind == "half":
-                if e == LAST:
+                if (e, s) in ((LAST - 1, 0), (LAST, 1)):
                     tile = y_sb[s][:, 2 * C : 4 * C].rearrange("p (j w) -> p j w", j=PACK)
                 else:
                     tile = in_buffer_of(chunk, [P, PACK, P], F32, "raw_half")
@@ -141,8 +141,8 @@ def tile_moe_tk_glu_relu_kernel(tc, xT, w1, w3, w2, gate, offs, pos1, pos2, pos3
             source = columns.rearrange("p j (m i) -> p m j i", i=QUAD)
             engine_copy(out=target.rearrange("p (m i j) -> p m j i", i=QUAD, j=PACK), in_=source)
 
-        def quantise_halves(experts, n, source):
-            words = keep.tile([P, len(experts) * P], U32, name=f"w2_codes{experts[0]}_{n}", align_bytes=64)
+        def quantise_halves(experts, n, source, tag=""):
+            words = keep.tile([P, len(experts) * P], U32, name=f"w2_codes{experts[0]}_{n}", tag=tag, align_bytes=64)
             scales = keep.tile([P, len(experts) * P], U8, name=f"w2_scales{experts[0]}_{n}", align_bytes=64)
             nc.vector.quantize_mx(out=words[:].bitcast(FP8X4), scales=scales[:], in_=source)
             for place, e in enumerate(experts):
@@ -266,31 +266,35 @@ def tile_moe_tk_glu_relu_kernel(tc, xT, w1, w3, w2, gate, offs, pos1, pos2, pos3
             engine_copy(out=y_sb[n][:, experts[0] * C : (experts[-1] + 1) * C], in_=bank[:])
 
         width = PACK * P
-        first = {}
+        staged = {}
+
+        def stage(name, experts, tag):
+            staged[name] = keep.tile([P, experts * width], BF16, name=name, tag=tag, align_bytes=64)
+            return staged[name]
 
         def late_w2(e):
-            if e == EARLY_W2:
-                alone = keep.tile([P, width], BF16, name="w2_first1", align_bytes=64)
-                interleave_half(e, 0, alone[:], nc.vector.tensor_copy)
-                quantise_halves([e], 0, alone[:])
+            if e == 1:
+                interleave_half(e, 0, stage("first1", 1, "first1")[:], nc.vector.tensor_copy)
+                quantise_halves([e], 0, staged["first1"][:])
                 take_h(LAST, None)
-                return
-            pair, place = e - e % 2, e % 2
-            if place == 0:
-                first[pair] = keep.tile([P, 2 * width], BF16, name=f"w2_first{pair}", tag=f"w2_first{pair}", align_bytes=64)
-            interleave_half(e, 0, first[pair][:, place * width : (place + 1) * width], nc.scalar.copy)
-            if place == 1:
-                quantise_halves([pair, e], 0, first[pair][:])
+                interleave_half(e, 1, stage("second1", 2, "second1")[:, :width], nc.scalar.copy)
+            if e == 2:
+                interleave_half(e, 0, stage("first2", 2, "w2_first2")[:, :width], nc.scalar.copy)
+                interleave_half(e, 1, staged["second1"][:, width:], nc.scalar.copy)
             if e == 3:
+                interleave_half(e, 0, staged["first2"][:, width:], nc.scalar.copy)
+                quantise_halves([2, 3], 0, staged["first2"][:])
                 quantise_h(LAST)
-            if e == LAST:
+            if e == 4:
+                interleave_half(e, 0, stage("first4", 1, "first4")[:], nc.scalar.copy)
+                quantise_halves([e], 0, staged["first4"][:])
                 late_y([1, 2], 0, "y0")
-                late_y([3], 0, "y1")
-                late_y([4, 5], 0, "y2", nc.vector.tensor_copy)
-                whole = keep.tile([P, 2 * width], BF16, name="w2_second1", tag="w2_first4", align_bytes=64)
-                for place, other in enumerate((1, 2)):
-                    interleave_half(other, 1, whole[:, place * width : (place + 1) * width], nc.vector.tensor_copy)
-                quantise_halves([1, 2], 1, whole[:])
+                late_y([3, 4], 0, "y1")
+            if e == LAST:
+                interleave_half(e, 0, stage("first5", 1, "first5")[:], nc.vector.tensor_copy)
+                quantise_halves([e], 0, staged["first5"][:])
+                late_y([e], 0, "y2", nc.vector.tensor_copy)
+                quantise_halves([1, 2], 1, staged["second1"][:], "first5")
                 split = keep.tile([P, 3 * width], BF16, name="w2_second3", tag="w2_second3", align_bytes=64)
                 for place, other in enumerate((3, 4, 5)):
                     interleave_half(other, 1, split[:, place * width : (place + 1) * width], nc.scalar.copy)
@@ -327,8 +331,9 @@ def tile_moe_tk_glu_relu_kernel(tc, xT, w1, w3, w2, gate, offs, pos1, pos2, pos3
                     first_product(kind, e)
             elif kind == "w3":
                 quantise(chunk)
-                if s == 1:
+                if s == (0 if e == LAST else 1):
                     take_relu(e, chunk)
+                if s == 1:
                     if 1 <= e <= EARLY_W2:
                         early_y(e - 1)
                     first_product(kind, e)

@@ -45,9 +45,7 @@ def chunk_order():
             order.append(("w2", e - 1, 0))
         order.append(("w3", e, 1))
     order += [("w2", e, 0) for e in range(EARLY_W2, SPLIT_W2)]
-    order += [("half", e, 0) for e in range(SPLIT_W2, E)] + [("gate", 0, 0)]
-    order += [("half", SPLIT_W2, 1), ("gate", 1, 0)] + [("half", e, 1) for e in range(SPLIT_W2 + 1, E)]
-    return order + [("gate", 2, 0)]
+    return order + [("half", e, n) for n in range(HALVES) for e in range(SPLIT_W2, E)]
 
 
 def quads_on_vector(kind, e, s):
@@ -79,6 +77,9 @@ def tile_moe_tk_glu_relu_kernel(tc, xT, w1, w3, w2, gate, offs, pos1, pos2, pos3
         nc.gpsimd.memset(x_scales[:], 0)
         identity = keep.tile([P, P], F32, name="identity")
         make_identity(nc, identity[:])
+        gate_columns = keep.tile([P, TOP, QUAD], F32, name="gate_columns")
+        nc.scalar.dma_start(out=gate_columns[:], in_=gate[:, 0, :].rearrange("r (p j) -> p r j", j=QUAD))
+        gate_sb = [keep.tile([P, T], F32, name=f"gate_sb{r}") for r in range(TOP)]
         y_sb = [keep.tile([P, SLOTS], F32, name=f"y_sb{n}") for n in range(HALVES)]
 
         chunks = chunk_order()
@@ -91,12 +92,6 @@ def tile_moe_tk_glu_relu_kernel(tc, xT, w1, w3, w2, gate, offs, pos1, pos2, pos3
 
         def load(chunk):
             kind, e, s = chunk
-            if kind == "gate":
-                nc.sync.dma_start(pos_sb[e][:], (pos1, pos2, pos3)[e])
-                tile = in_buffer_of(chunk, [P, T], F32, "gate_sb")
-                nc.sync.dma_start(out=tile[:], in_=gate[e, 0:P, :])
-                raw[chunk] = tile
-                return
             if kind == "w2":
                 tile = in_buffer_of(chunk, [P, PACK, N], F32, "raw2")
                 rows = w2[e]
@@ -111,6 +106,9 @@ def tile_moe_tk_glu_relu_kernel(tc, xT, w1, w3, w2, gate, offs, pos1, pos2, pos3
                 rows = {"x": xT, "w1": w1[e], "w3": w3[e]}[kind][s * PASS : (s + 1) * PASS, :]
             nc.sync.dma_start(out=tile[:], in_=rows.rearrange("(p j) w -> p j w", j=PACK))
             raw[chunk] = tile
+            if chunk == ("half", LAST, 0):
+                for r, pos in enumerate((pos1, pos2, pos3)):
+                    nc.sync.dma_start(pos_sb[r][:], pos)
 
         def interleave(chunk):
             kind, e, s = chunk
@@ -259,6 +257,13 @@ def tile_moe_tk_glu_relu_kernel(tc, xT, w1, w3, w2, gate, offs, pos1, pos2, pos3
             for n in range(HALVES):
                 nc.scalar.copy(out=y_sb[n][:, e * C : (e + 1) * C], in_=bank[:, n, :])
 
+        def spread_gates():
+            for r in range(TOP):
+                bank = psum.tile([P, QUAD, P], F32, name="gate_bank", tag=f"y{r}")
+                for j in range(QUAD):
+                    nc.tensor.transpose(bank[:, j, :], gate_columns[:, r, j : j + 1].to_broadcast([P, P]), identity[:])
+                nc.scalar.copy(out=gate_sb[r][:].rearrange("q (p j) -> q p j", j=QUAD), in_=bank[:].rearrange("q j p -> q p j"))
+
         def late_y(experts, n, tag, engine_copy=nc.scalar.copy):
             bank = psum.tile([P, len(experts) * C], F32, name="bank_y", tag=tag)
             for place, e in enumerate(experts):
@@ -306,7 +311,7 @@ def tile_moe_tk_glu_relu_kernel(tc, xT, w1, w3, w2, gate, offs, pos1, pos2, pos3
 
         def work(chunk):
             kind, e, s = chunk
-            if kind == "gate" or (kind, s) == ("half", 1):
+            if (kind, s) == ("half", 1):
                 return
             if kind in ("w2", "half") and e >= EARLY_W2:
                 late_w2(e)
@@ -314,6 +319,8 @@ def tile_moe_tk_glu_relu_kernel(tc, xT, w1, w3, w2, gate, offs, pos1, pos2, pos3
             interleave(chunk)
             if kind == "x":
                 quantise(chunk)
+                if s == 0:
+                    spread_gates()
                 for other in range(SLOT_BUFS):
                     gather_words(other, s)
                     if s == PASSES - 1:
@@ -348,12 +355,15 @@ def tile_moe_tk_glu_relu_kernel(tc, xT, w1, w3, w2, gate, offs, pos1, pos2, pos3
             if step >= 0:
                 work(chunks[step])
 
-        gate_sb = [raw["gate", r, 0] for r in range(TOP)]
+
+        later_parts = keep.tile([P, TOP - 1, T], F32, name="later_parts", tag="w2_second3", align_bytes=64)
 
         def fetch(n, r, cols):
             name = f"part{n}_{r}_{cols.start}"
-            tag = "w2_second3" if (n, r) == (0, 1) else name
-            part = keep.tile([P, cols.stop - cols.start], F32, name=name, tag=tag, align_bytes=64)
+            if n == 0 and r > 0:
+                part = later_parts[:, r - 1, :]
+            else:
+                part = keep.tile([P, cols.stop - cols.start], F32, name=name)
             entries = pos_sb[r][:, cols.start // 16 : cols.stop // 16]
             nc.vector.tensor_tensor(part[:], y_sb[n][:].indirect(entries), gate_sb[r][:, cols], MULT)
             return part

@@ -26,26 +26,26 @@ HALVES = 2
 QUAD = 4
 SCALE_STEP = 4
 
-RING = 12
-AHEAD = RING - 3
-EARLY_W2 = 1
-SPLIT_W2 = 3
+BUFFER = PACK * PASS * 4
+ROTATING = 9
+HELD = 3
+AHEAD = ROTATING - 3
 LAST = E - 1
+HALF = PACK * P * 4
 X_QUADS_ON_VECTOR = 84
 W_QUADS_ON_VECTOR = 96
-LAST_QUADS_ON_VECTOR = {("w1", 0): 96, ("w1", 1): 32, ("w3", 0): 38, ("w3", 1): 128}
-SLOT_BUFS = 3
+BEFORE_LAST_QUADS_ON_VECTOR = 64
+LAST_QUADS_ON_VECTOR = {("w1", 0): 96, ("w3", 0): 0, ("w1", 1): 84, ("w3", 1): 86}
 
 
 def chunk_order():
     order = [("x", 0, s) for s in range(PASSES)]
-    for e in range(E):
+    for e in range(LAST):
         order += [("w1", e, 0), ("w1", e, 1), ("w3", e, 0)]
-        if 1 <= e <= EARLY_W2:
-            order.append(("w2", e - 1, 0))
+        if e == 1:
+            order.append(("w2", 0, 0))
         order.append(("w3", e, 1))
-    order += [("w2", e, 0) for e in range(EARLY_W2, SPLIT_W2)]
-    return order + [("half", e, n) for n in range(HALVES) for e in range(SPLIT_W2, E)]
+    return order + [(kind, LAST, s) for s in range(PASSES) for kind in ("w1", "w3")]
 
 
 def quads_on_vector(kind, e, s):
@@ -54,7 +54,7 @@ def quads_on_vector(kind, e, s):
     if kind == "w2":
         return 0
     if (kind, e, s) == ("w3", LAST - 1, 1):
-        return 64
+        return BEFORE_LAST_QUADS_ON_VECTOR
     if e == LAST:
         return LAST_QUADS_ON_VECTOR[kind, s]
     return W_QUADS_ON_VECTOR if s == 0 else 0
@@ -67,7 +67,6 @@ def tile_moe_tk_glu_relu_kernel(tc, xT, w1, w3, w2, gate, offs, pos1, pos2, pos3
         ring = ctx.enter_context(tc.tile_pool(name="ring", bufs=1))
         groups = ctx.enter_context(tc.tile_pool(name="groups", bufs=3))
         codes = ctx.enter_context(tc.tile_pool(name="codes", bufs=4))
-        slots = ctx.enter_context(tc.tile_pool(name="slots", bufs=SLOT_BUFS))
         psum = ctx.enter_context(tc.psum_pool(name="psum", bufs=1))
 
         offs_sb = keep.tile([P, SLOTS // 16], U16, name="offs_sb")
@@ -87,28 +86,27 @@ def tile_moe_tk_glu_relu_kernel(tc, xT, w1, w3, w2, gate, offs, pos1, pos2, pos3
         slot_words, slot_scales, relu_a, h_bf, h_packed = {}, {}, {}, {}, {}
         banks = {}
 
-        def in_buffer_of(chunk, shape, dtype, name):
-            return ring.tile(shape, dtype, name=name, tag=f"ring{chunks.index(chunk) % RING}", align_bytes=64)
+        held = [("w3", e, 1) for e in range(HELD)]
+        in_turn = [chunk for chunk in chunks if chunk not in held]
+
+        def start_of(chunk):
+            if chunk in held:
+                return (ROTATING + held.index(chunk)) * BUFFER
+            return in_turn.index(chunk) % ROTATING * BUFFER
+
+        def placed(offset, shape, dtype, name):
+            return ring.tile(shape, dtype, name=name, tag=f"{name}_{offset}", align_bytes=64, offset=offset)
 
         def load(chunk):
             kind, e, s = chunk
             if kind == "w2":
-                tile = in_buffer_of(chunk, [P, PACK, N], F32, "raw2")
+                tile = placed(start_of(chunk), [P, PACK, N], F32, "raw2")
                 rows = w2[e]
-            elif kind == "half":
-                if (e, s) in ((LAST - 1, 0), (LAST, 1)):
-                    tile = y_sb[s][:, 2 * C : 4 * C].rearrange("p (j w) -> p j w", j=PACK)
-                else:
-                    tile = in_buffer_of(chunk, [P, PACK, P], F32, "raw_half")
-                rows = w2[e][:, s * P : (s + 1) * P]
             else:
-                tile = in_buffer_of(chunk, [P, PACK, PASS], F32, "raw")
+                tile = placed(start_of(chunk), [P, PACK, PASS], F32, "raw")
                 rows = {"x": xT, "w1": w1[e], "w3": w3[e]}[kind][s * PASS : (s + 1) * PASS, :]
             nc.sync.dma_start(out=tile[:], in_=rows.rearrange("(p j) w -> p j w", j=PACK))
             raw[chunk] = tile
-            if chunk == ("half", LAST, 0):
-                for r, pos in enumerate((pos1, pos2, pos3)):
-                    nc.sync.dma_start(pos_sb[r][:], pos)
 
         def interleave(chunk):
             kind, e, s = chunk
@@ -134,13 +132,8 @@ def tile_moe_tk_glu_relu_kernel(tc, xT, w1, w3, w2, gate, offs, pos1, pos2, pos3
             if cut < source.shape[1]:
                 nc.scalar.copy(out=flat[:, cut:], in_=source[:, cut:])
 
-        def interleave_half(e, n, target, engine_copy):
-            columns = raw["half", e, n][:] if e >= SPLIT_W2 else raw["w2", e, 0][:, :, n * P : (n + 1) * P]
-            source = columns.rearrange("p j (m i) -> p m j i", i=QUAD)
-            engine_copy(out=target.rearrange("p (m i j) -> p m j i", i=QUAD, j=PACK), in_=source)
-
-        def quantise_halves(experts, n, source, tag=""):
-            words = keep.tile([P, len(experts) * P], U32, name=f"w2_codes{experts[0]}_{n}", tag=tag, align_bytes=64)
+        def quantise_halves(experts, n, source):
+            words = keep.tile([P, len(experts) * P], U32, name=f"w2_codes{experts[0]}_{n}", align_bytes=64)
             scales = keep.tile([P, len(experts) * P], U8, name=f"w2_scales{experts[0]}_{n}", align_bytes=64)
             nc.vector.quantize_mx(out=words[:].bitcast(FP8X4), scales=scales[:], in_=source)
             for place, e in enumerate(experts):
@@ -162,45 +155,56 @@ def tile_moe_tk_glu_relu_kernel(tc, xT, w1, w3, w2, gate, offs, pos1, pos2, pos3
                 for n in range(HALVES):
                     packed[kind, e, n] = (words[:, n * P : (n + 1) * P], scales[:, n * P : (n + 1) * P])
                 return
-            if s == 0:
-                words = codes.tile([P, PASSES, H], U32, name="w_codes", align_bytes=64)
-                scales = codes.tile([P, PASSES, H], U8, name="w_scales", align_bytes=64)
-                packed[kind, e] = (words, scales)
-            words, scales = packed[kind, e]
-            if (kind, e) == ("w3", LAST):
-                nc.vector.quantize_mx(out=words[:, s, :].bitcast(FP8X4), scales=scales[:, s, :], in_=source[:, s, :])
-            elif s == PASSES - 1:
-                nc.vector.quantize_mx(
-                    out=words[:].rearrange("p s w -> p (s w)").bitcast(FP8X4),
-                    scales=scales[:].rearrange("p s w -> p (s w)"),
-                    in_=source[:].rearrange("p s w -> p (s w)"),
-                )
+            if e == LAST:
+                if (kind, s) == ("w3", 0):
+                    words = placed(start_of(("w1", e, 1)), [P, H], U32, "w_codes")
+                else:
+                    words = codes.tile([P, H], U32, name="w_codes", align_bytes=64)
+                scales = codes.tile([P, H], U8, name="w_scales", align_bytes=64)
+                nc.vector.quantize_mx(out=words[:].bitcast(FP8X4), scales=scales[:], in_=source[:, s, :])
+                packed[kind, e, s] = (words, scales)
+                return
+            words = codes.tile([P, PASSES, H], U32, name="w_codes", align_bytes=64)
+            scales = codes.tile([P, PASSES, H], U8, name="w_scales", align_bytes=64)
+            nc.vector.quantize_mx(
+                out=words[:].rearrange("p s w -> p (s w)").bitcast(FP8X4),
+                scales=scales[:].rearrange("p s w -> p (s w)"),
+                in_=source[:].rearrange("p s w -> p (s w)"),
+            )
+            for other in range(PASSES):
+                packed[kind, e, other] = (words[:, other, :], scales[:, other, :])
 
         def entries_of(e):
             return offs_sb[:, e * C // 16 : (e + 1) * C // 16]
 
         def gather_words(e, s):
-            tile = slots.tile([P, C], U32, name=f"slot_codes{s}", align_bytes=64)
+            if e < E - HELD:
+                tile = keep.tile([P, C], U32, name=f"slot_codes{e}_{s}", align_bytes=64)
+            else:
+                tile = placed(start_of(held[e - (E - HELD)]) + BUFFER // 2 + s * 4 * C, [P, C], U32, "slot_codes")
             nc.vector.tensor_copy(tile[:], x_codes[s][:].indirect(entries_of(e)))
             slot_words[e, s] = tile
 
         def gather_scales(e):
-            tile = slots.tile([P, C], U8, name="slot_scales", align_bytes=64)
+            if e < E - HELD:
+                tile = keep.tile([P, C], U8, name=f"slot_scales{e}", align_bytes=64)
+            else:
+                tile = placed(start_of(held[e - (E - HELD)]) + BUFFER // 2 + PASSES * 4 * C, [P, C], U8, "slot_scales")
             nc.vector.tensor_copy(tile[:], x_scales[:].indirect(entries_of(e)))
             slot_scales[e] = tile
 
         def first_product(kind, e):
-            words, scales = packed[kind, e]
             for half in range(HALVES):
                 bank = psum.tile([P, PACK, P], F32, name="bank", tag=f"{kind}_{half}")
                 cols = slice(half * P, (half + 1) * P)
                 for t in range(PACK):
                     rows = slice(t * P, (t + 1) * P)
                     for s in range(PASSES):
+                        words, scales = packed[kind, e, s]
                         nc.tensor.matmul_mx(
                             out=bank[:, t, :],
-                            lhsT=words[:, s, rows].bitcast(FP8X4),
-                            lhsT_scale=scales[:, s, rows],
+                            lhsT=words[:, rows].bitcast(FP8X4),
+                            lhsT_scale=scales[:, rows],
                             rhs=slot_words[e, s][:, cols].bitcast(FP8X4),
                             rhs_scale=slot_scales[e][SCALE_STEP * s : P, cols],
                             start=(s == 0),
@@ -208,18 +212,15 @@ def tile_moe_tk_glu_relu_kernel(tc, xT, w1, w3, w2, gate, offs, pos1, pos2, pos3
                         )
                 banks[kind, e, half] = bank
 
-        def take_relu(e, chunk):
-            relu_a[e] = in_buffer_of(chunk, [P, HALVES, P, PACK], F32, "relu_a")
+        def take_relu(e, offset):
+            relu_a[e] = placed(offset, [P, HALVES, P, PACK], F32, "relu_a")
             for half in range(HALVES):
                 nc.scalar.activation(
                     relu_a[e][:, half, :, :], banks["w1", e, half][:].rearrange("p t c -> p c t"), RELU
                 )
 
-        def take_h(e, chunk):
-            if e == LAST:
-                h_bf[e] = keep.tile([P, C, PACK], BF16, name="h_last", align_bytes=64)
-            else:
-                h_bf[e] = in_buffer_of(chunk, [P, C, PACK], BF16, "h_bf")
+        def take_h(e, offset):
+            h_bf[e] = placed(offset, [P, C, PACK], BF16, "h_bf")
             for half in range(HALVES):
                 nc.vector.tensor_tensor(
                     h_bf[e][:, half * P : (half + 1) * P, :],
@@ -229,8 +230,7 @@ def tile_moe_tk_glu_relu_kernel(tc, xT, w1, w3, w2, gate, offs, pos1, pos2, pos3
                 )
 
         def quantise_h(e):
-            tag = "w2_first2" if e == LAST else f"h_codes{e}"
-            words = keep.tile([P, C], U32, name=f"h_codes{e}", tag=tag, align_bytes=64)
+            words = keep.tile([P, C], U32, name=f"h_codes{e}", align_bytes=64)
             scales = keep.tile([P, C], U8, name=f"h_scales{e}", align_bytes=64)
             nc.vector.quantize_mx(
                 out=words[:].bitcast(FP8X4), scales=scales[:], in_=h_bf[e][:].rearrange("p c t -> p (c t)")
@@ -270,82 +270,44 @@ def tile_moe_tk_glu_relu_kernel(tc, xT, w1, w3, w2, gate, offs, pos1, pos2, pos3
                 second_product(e, n, bank[:, place * C : (place + 1) * C])
             engine_copy(out=y_sb[n][:, experts[0] * C : (experts[-1] + 1) * C], in_=bank[:])
 
-        width = PACK * P
-        staged = {}
-
-        def stage(name, experts, tag):
-            staged[name] = keep.tile([P, experts * width], BF16, name=name, tag=tag, align_bytes=64)
-            return staged[name]
-
-        def late_w2(e):
-            if e == 1:
-                interleave_half(e, 0, stage("first1", 1, "first1")[:], nc.vector.tensor_copy)
-                quantise_halves([e], 0, staged["first1"][:])
-                take_h(LAST, None)
-                interleave_half(e, 1, stage("second1", 2, "second1")[:, :width], nc.scalar.copy)
-            if e == 2:
-                interleave_half(e, 0, stage("first2", 2, "w2_first2")[:, :width], nc.scalar.copy)
-                interleave_half(e, 1, staged["second1"][:, width:], nc.scalar.copy)
-            if e == 3:
-                interleave_half(e, 0, staged["first2"][:, width:], nc.scalar.copy)
-                quantise_halves([2, 3], 0, staged["first2"][:])
-                quantise_h(LAST)
-            if e == 4:
-                interleave_half(e, 0, stage("first4", 1, "first4")[:], nc.scalar.copy)
-                quantise_halves([e], 0, staged["first4"][:])
-                late_y([1, 2], 0, "y0")
-                late_y([3, 4], 0, "y1")
-            if e == LAST:
-                interleave_half(e, 0, stage("first5", 1, "first5")[:], nc.vector.tensor_copy)
-                quantise_halves([e], 0, staged["first5"][:])
-                late_y([e], 0, "y2", nc.vector.tensor_copy)
-                quantise_halves([1, 2], 1, staged["second1"][:], "first5")
-                split = keep.tile([P, 3 * width], BF16, name="w2_second3", tag="w2_second3", align_bytes=64)
-                for place, other in enumerate((3, 4, 5)):
-                    interleave_half(other, 1, split[:, place * width : (place + 1) * width], nc.scalar.copy)
-                late_y([1, 2], 1, "y3")
-                quantise_halves([3, 4], 1, split[:, : 2 * width])
-                late_y([3, 4], 1, "y0")
-                quantise_halves([5], 1, split[:, 2 * width :])
-                late_y([5], 1, "y2")
-
         def work(chunk):
             kind, e, s = chunk
-            if (kind, s) == ("half", 1):
-                return
-            if kind in ("w2", "half") and e >= EARLY_W2:
-                late_w2(e)
-                return
             interleave(chunk)
             if kind == "x":
                 quantise(chunk)
                 if s == 0:
                     spread_gates()
-                for other in range(SLOT_BUFS):
+                for other in range(E - HELD):
                     gather_words(other, s)
                     if s == PASSES - 1:
                         gather_scales(other)
-            elif kind == "w1":
-                if e > 0 and s == 0:
-                    take_h(e - 1, chunk)
+            elif kind == "w2":
+                quantise(chunk)
+            elif e == LAST:
+                if (kind, s) != ("w3", 0):
+                    quantise(chunk)
+                if (kind, s) == ("w1", 0):
+                    take_h(e - 1, start_of(chunk))
                     quantise_h(e - 1)
-                    if e - 1 + SLOT_BUFS < E:
-                        for other_pass in range(PASSES):
-                            gather_words(e - 1 + SLOT_BUFS, other_pass)
-                        gather_scales(e - 1 + SLOT_BUFS)
-                quantise(chunk)
+                if (kind, s) == ("w1", 1):
+                    quantise(("w3", e, 0))
                 if s == 1:
                     first_product(kind, e)
-            elif kind == "w3":
-                quantise(chunk)
-                if s == (0 if e == LAST else 1):
-                    take_relu(e, chunk)
-                if s == 1:
-                    if 1 <= e <= EARLY_W2:
-                        early_y(e - 1)
-                    first_product(kind, e)
+            elif s == 0:
+                if kind == "w1" and e > 0:
+                    take_h(e - 1, start_of(chunk))
+                    quantise_h(e - 1)
             else:
                 quantise(chunk)
+                if kind == "w3":
+                    if chunk in held:
+                        for other_pass in range(PASSES):
+                            gather_words(e + E - HELD, other_pass)
+                        gather_scales(e + E - HELD)
+                    take_relu(e, start_of(chunk))
+                    if e == 1:
+                        early_y(0)
+                first_product(kind, e)
 
         for step in range(-AHEAD, len(chunks)):
             if step + AHEAD < len(chunks):
@@ -355,13 +317,70 @@ def tile_moe_tk_glu_relu_kernel(tc, xT, w1, w3, w2, gate, offs, pos1, pos2, pos3
             if step >= 0:
                 work(chunks[step])
 
+        width = PACK * P
+        first_free = len(in_turn) % ROTATING * BUFFER
+        second_free = (len(in_turn) + 1) % ROTATING * BUFFER
+        staging = start_of(held[0])
+        halves = {}
+        halves[1, 0] = placed(first_free, [P, PACK, P], F32, "raw_half")[:]
+        both = placed(first_free + 2 * HALF, [P, 2, PACK, P], F32, "raw_halves")
+        for e in (2, 3):
+            halves[e, 0] = both[:, e - 2]
+        halves[4, 0] = placed(second_free + 3 * HALF, [P, PACK, P], F32, "raw_half")[:]
+        halves[5, 0] = y_sb[0][:, C : 3 * C].rearrange("p (j w) -> p j w", j=PACK)
+        halves[1, 1] = y_sb[0][:, 3 * C : 5 * C].rearrange("p (j w) -> p j w", j=PACK)
+        for e in (2, 3, 4):
+            halves[e, 1] = placed(second_free + (e - 2) * HALF, [P, PACK, P], F32, "raw_half")[:]
+        halves[5, 1] = y_sb[1][:, C : 3 * C].rearrange("p (j w) -> p j w", j=PACK)
+        for n in range(HALVES):
+            for e in range(1, E):
+                rows = w2[e][:, n * P : (n + 1) * P]
+                nc.sync.dma_start(out=halves[e, n], in_=rows.rearrange("(p j) w -> p j w", j=PACK))
+            if n == 0:
+                for r, pos in enumerate((pos1, pos2, pos3)):
+                    nc.sync.dma_start(pos_sb[r][:], pos)
 
-        later_parts = keep.tile([P, TOP - 1, T], F32, name="later_parts", tag="w2_second3", align_bytes=64)
+        def interleave_half(e, n, target):
+            source = halves[e, n].rearrange("p j (m i) -> p m j i", i=QUAD)
+            nc.scalar.copy(out=target.rearrange("p (m i j) -> p m j i", i=QUAD, j=PACK), in_=source)
+
+        first = keep.tile([P, 4 * width], BF16, name="first", align_bytes=64)
+        first5 = keep.tile([P, width], BF16, name="first5", align_bytes=64)
+        second12 = placed(staging, [P, 2 * width], BF16, "second12")
+        second34 = placed(staging + 4 * width, [P, 2 * width], BF16, "second34")
+        second5 = placed(staging + 8 * width, [P, width], BF16, "second5")
+        interleave_half(1, 0, first[:, :width])
+        take_relu(LAST, first_free)
+        nc.vector.tensor_copy(
+            out=first[:, width : 3 * width].rearrange("p (e m i j) -> p e m j i", e=2, i=QUAD, j=PACK),
+            in_=both[:].rearrange("p e j (m i) -> p e m j i", i=QUAD),
+        )
+        quantise_halves([1, 2], 0, first[:, : 2 * width])
+        take_h(LAST, first_free + 2 * HALF)
+        interleave_half(4, 0, first[:, 3 * width :])
+        quantise_halves([3, 4], 0, first[:, 2 * width :])
+        quantise_h(LAST)
+        interleave_half(5, 0, first5[:])
+        quantise_halves([5], 0, first5[:])
+        late_y([1, 2], 0, "y0")
+        interleave_half(1, 1, second12[:, :width])
+        late_y([3, 4], 0, "y1")
+        late_y([5], 0, "y2", nc.vector.tensor_copy)
+        interleave_half(2, 1, second12[:, width:])
+        quantise_halves([1, 2], 1, second12[:])
+        for place, e in enumerate((3, 4)):
+            interleave_half(e, 1, second34[:, place * width : (place + 1) * width])
+        quantise_halves([3, 4], 1, second34[:])
+        interleave_half(5, 1, second5[:])
+        late_y([1, 2], 1, "y3")
+        quantise_halves([5], 1, second5[:])
+        late_y([3, 4], 1, "y0")
+        late_y([5], 1, "y2")
 
         def fetch(n, r, cols):
             name = f"part{n}_{r}_{cols.start}"
             if n == 0 and r > 0:
-                part = later_parts[:, r - 1, :]
+                part = placed(staging + (2 if r == 1 else 8) * width, [P, T], F32, name)
             else:
                 part = keep.tile([P, cols.stop - cols.start], F32, name=name)
             entries = pos_sb[r][:, cols.start // 16 : cols.stop // 16]
@@ -398,9 +417,10 @@ def tile_moe_tk_glu_relu_kernel(tc, xT, w1, w3, w2, gate, offs, pos1, pos2, pos3
         nc.scalar.copy(out=result[:], in_=upright[:].rearrange("p b t -> p (b t)"))
         nc.sync.dma_start(out=out[0:P, :], in_=result[:])
         next1 = fetch(1, 1, tokens)
-        pair = add("pair1", next0[:], next1)
         token_halves = [slice(q * T // 2, (q + 1) * T // 2) for q in range(2)]
-        ends = [fetch(1, 2, cols) for cols in token_halves]
+        ends = [fetch(1, 2, token_halves[0])]
+        pair = add("pair1", next0[:], next1)
+        ends.append(fetch(1, 2, token_halves[1]))
         for cols, end in zip(token_halves, ends):
             result = add(f"result1_{cols.start}", pair[:, cols], end)
             nc.sync.dma_start(out=out[P : 2 * P, cols], in_=result[:])

@@ -73,11 +73,12 @@ def tile_moe_tk_glu_relu_kernel(tc, xT, w1, w3, w2, gate, offs, pos1, pos2, pos3
         pos_sb = [keep.tile([P, T // 16], U16, name=f"pos_sb{r}") for r in range(TOP)]
         x_codes = [keep.tile([P, T], U32, name=f"x_codes{s}", align_bytes=64) for s in range(PASSES)]
         x_scales = keep.tile([P, T], U8, name="x_scales", align_bytes=64)
+        gate_rows = keep.tile([P, T], F32, name="gate_rows")
+        nc.gpsimd.memset(gate_rows[:], 0.0)
         nc.gpsimd.memset(x_scales[:], 0)
         identity = keep.tile([P, P], F32, name="identity")
         make_identity(nc, identity[:])
-        gate_columns = keep.tile([P, TOP, QUAD], F32, name="gate_columns")
-        nc.scalar.dma_start(out=gate_columns[:], in_=gate[:, 0, :].rearrange("r (p j) -> p r j", j=QUAD))
+        gate_columns = keep.tile([P, T // P, TOP], F32, name="gate_columns")
         gate_sb = [keep.tile([P, T], F32, name=f"gate_sb{r}") for r in range(TOP)]
         y_sb = [keep.tile([P, SLOTS], F32, name=f"y_sb{n}") for n in range(HALVES)]
 
@@ -258,11 +259,16 @@ def tile_moe_tk_glu_relu_kernel(tc, xT, w1, w3, w2, gate, offs, pos1, pos2, pos3
                 nc.scalar.copy(out=y_sb[n][:, e * C : (e + 1) * C], in_=bank[:, n, :])
 
         def spread_gates():
+            bank = psum.tile([P, T // P, P], F32, name="gate_bank", tag="y3")
+            for block in range(T // P):
+                nc.tensor.transpose(bank[:, block, :], gate_rows[:, block * P : (block + 1) * P], identity[:])
+            nc.scalar.copy(out=gate_columns[:], in_=bank[:, :, 0:TOP])
             for r in range(TOP):
-                bank = psum.tile([P, QUAD, P], F32, name="gate_bank", tag=f"y{r}")
-                for j in range(QUAD):
-                    nc.tensor.transpose(bank[:, j, :], gate_columns[:, r, j : j + 1].to_broadcast([P, P]), identity[:])
-                nc.scalar.copy(out=gate_sb[r][:].rearrange("q (p j) -> q p j", j=QUAD), in_=bank[:].rearrange("q j p -> q p j"))
+                bank = psum.tile([P, T // P, P], F32, name="gate_bank", tag=f"y{r}")
+                for block in range(T // P):
+                    column = gate_columns[:, block, r : r + 1].to_broadcast([P, P])
+                    nc.tensor.transpose(bank[:, block, :], column, identity[:])
+                nc.scalar.copy(out=gate_sb[r][:], in_=bank[:].rearrange("q b p -> q (b p)"))
 
         def late_y(experts, n, tag, engine_copy=nc.scalar.copy):
             bank = psum.tile([P, len(experts) * C], F32, name="bank_y", tag=tag)
@@ -275,7 +281,7 @@ def tile_moe_tk_glu_relu_kernel(tc, xT, w1, w3, w2, gate, offs, pos1, pos2, pos3
             interleave(chunk)
             if kind == "x":
                 quantise(chunk)
-                if s == 0:
+                if s == 1:
                     spread_gates()
                 for other in range(E - HELD):
                     gather_words(other, s)
@@ -314,6 +320,8 @@ def tile_moe_tk_glu_relu_kernel(tc, xT, w1, w3, w2, gate, offs, pos1, pos2, pos3
                 load(chunks[step + AHEAD])
                 if step + AHEAD == 0:
                     nc.sync.dma_start(offs_sb[:], offs)
+                if step + AHEAD == 1:
+                    nc.sync.dma_start(out=gate_rows[0:TOP, :], in_=gate[:, 0, :])
             if step >= 0:
                 work(chunks[step])
 
@@ -392,35 +400,45 @@ def tile_moe_tk_glu_relu_kernel(tc, xT, w1, w3, w2, gate, offs, pos1, pos2, pos3
             nc.vector.tensor_tensor(total[:], first, second[:], ADD)
             return total
 
-        tokens = slice(0, T)
-        parts = [fetch(0, r, tokens) for r in range(TOP)]
-        next0 = fetch(1, 0, tokens)
         blocks = range(T // P)
         free_banks = [f"{kind}_{half}" for kind in ("w1", "w3") for half in range(HALVES)]
-        turned = [psum.tile([P, P], F32, name="turned", tag=free_banks[block]) for block in blocks]
-        for r in range(TOP):
+
+        def sum_in_psum(n, parts, targets):
+            turned = [psum.tile([P, P], F32, name="turned", tag=free_banks[block]) for block in blocks]
+            for r, part in enumerate(parts):
+                for block in blocks:
+                    nc.tensor.matmul(
+                        turned[block][:],
+                        lhsT=part[block],
+                        rhs=identity[:],
+                        is_transpose=True,
+                        start=(r == 0),
+                        stop=(r == len(parts) - 1),
+                    )
             for block in blocks:
-                nc.tensor.matmul(
-                    turned[block][:],
-                    lhsT=parts[r][:, block * P : (block + 1) * P],
-                    rhs=identity[:],
-                    is_transpose=True,
-                    start=(r == 0),
-                    stop=(r == TOP - 1),
-                )
+                turned_sb = keep.tile([P, P], F32, name=f"turned_sb{n}_{block}")
+                nc.scalar.copy(out=turned_sb[:], in_=turned[block][:])
+                nc.tensor.transpose(targets[block], turned_sb[:], identity[:])
+
+        tokens = slice(0, T)
+        parts = [fetch(0, r, tokens) for r in range(TOP)]
         upright = psum.tile([P, T // P, P], F32, name="upright", tag="y1")
-        for block in blocks:
-            turned_sb = keep.tile([P, P], F32, name=f"turned_sb{block}")
-            nc.scalar.copy(out=turned_sb[:], in_=turned[block][:])
-            nc.tensor.transpose(upright[:, block, :], turned_sb[:], identity[:])
+        parts = [[part[:, block * P : (block + 1) * P] for block in blocks] for part in parts]
+        sum_in_psum(0, parts, [upright[:, block, :] for block in blocks])
         result = keep.tile([P, T], F32, name="result0")
         nc.scalar.copy(out=result[:], in_=upright[:].rearrange("p b t -> p (b t)"))
         nc.sync.dma_start(out=out[0:P, :], in_=result[:])
-        next1 = fetch(1, 1, tokens)
+
         token_halves = [slice(q * T // 2, (q + 1) * T // 2) for q in range(2)]
-        ends = [fetch(1, 2, token_halves[0])]
-        pair = add("pair1", next0[:], next1)
-        ends.append(fetch(1, 2, token_halves[1]))
-        for cols, end in zip(token_halves, ends):
-            result = add(f"result1_{cols.start}", pair[:, cols], end)
+        whole = fetch(1, 0, tokens)
+        cut = [fetch(1, 1, cols) for cols in token_halves]
+        parts = [
+            [whole[:, block * P : (block + 1) * P] for block in blocks],
+            [cut[block // 2][:, block % 2 * P : (block % 2 + 1) * P] for block in blocks],
+        ]
+        pairs = [psum.tile([P, T // 2], F32, name="pair", tag=tag) for tag in ("y0", "y2")]
+        sum_in_psum(1, parts, [pairs[block // 2][:, block % 2 * P : (block % 2 + 1) * P] for block in blocks])
+        ends = [fetch(1, TOP - 1, cols) for cols in token_halves]
+        for cols, pair, end in zip(token_halves, pairs, ends):
+            result = add(f"result1_{cols.start}", pair[:], end)
             nc.sync.dma_start(out=out[P : 2 * P, cols], in_=result[:])

@@ -92,7 +92,7 @@ def tile_moe_tk_glu_relu_kernel(tc, xT, w1, w3, w2, gate, offs, pos1, pos2, pos3
 
         def start_of(chunk):
             if chunk in held:
-                return (ROTATING + held.index(chunk)) * BUFFER
+                return ROTATING * BUFFER + held.index(chunk) * (BUFFER + C)
             return in_turn.index(chunk) % ROTATING * BUFFER
 
         def placed(offset, shape, dtype, name):
@@ -196,14 +196,17 @@ def tile_moe_tk_glu_relu_kernel(tc, xT, w1, w3, w2, gate, offs, pos1, pos2, pos3
 
         def first_product(kind, e):
             for half in range(HALVES):
-                bank = psum.tile([P, PACK, P], F32, name="bank", tag=f"{kind}_{half}")
-                cols = slice(half * P, (half + 1) * P)
-                for t in range(PACK):
+                if e == LAST:
+                    planes, cols = range(PACK), slice(half * P, (half + 1) * P)
+                else:
+                    planes, cols = range(2 * half, 2 * half + 2), slice(0, C)
+                bank = psum.tile([P, len(planes), cols.stop - cols.start], F32, name="bank", tag=f"{kind}_{half}")
+                for place, t in enumerate(planes):
                     rows = slice(t * P, (t + 1) * P)
                     for s in range(PASSES):
                         words, scales = packed[kind, e, s]
                         nc.tensor.matmul_mx(
-                            out=bank[:, t, :],
+                            out=bank[:, place, :],
                             lhsT=words[:, rows].bitcast(FP8X4),
                             lhsT_scale=scales[:, rows],
                             rhs=slot_words[e, s][:, cols].bitcast(FP8X4),
@@ -211,30 +214,36 @@ def tile_moe_tk_glu_relu_kernel(tc, xT, w1, w3, w2, gate, offs, pos1, pos2, pos3
                             start=(s == 0),
                             stop=(s == PASSES - 1),
                         )
-                banks[kind, e, half] = bank
+                banks[kind, e, half] = bank[:].rearrange("p t c -> p c t")
+
+        def like(flat, bank):
+            return flat.rearrange("p (c t) -> p c t", t=bank.shape[2])
 
         def take_relu(e, offset):
-            relu_a[e] = placed(offset, [P, HALVES, P, PACK], F32, "relu_a")
+            relu_a[e] = placed(offset, [P, HALVES, PASS], F32, "relu_a")
             for half in range(HALVES):
-                nc.scalar.activation(
-                    relu_a[e][:, half, :, :], banks["w1", e, half][:].rearrange("p t c -> p c t"), RELU
-                )
+                bank = banks["w1", e, half]
+                nc.scalar.activation(like(relu_a[e][:, half, :], bank), bank, RELU)
 
         def take_h(e, offset):
-            h_bf[e] = placed(offset, [P, C, PACK], BF16, "h_bf")
+            h_bf[e] = placed(offset, [P, HALVES, PASS], BF16, "h_bf")
             for half in range(HALVES):
-                nc.vector.tensor_tensor(
-                    h_bf[e][:, half * P : (half + 1) * P, :],
-                    banks["w3", e, half][:].rearrange("p t c -> p c t"),
-                    relu_a[e][:, half, :, :],
-                    MULT,
-                )
+                bank = banks["w3", e, half]
+                nc.vector.tensor_tensor(like(h_bf[e][:, half, :], bank), bank, like(relu_a[e][:, half, :], bank), MULT)
+
+        def weave_h(e, offset, engine_copy, words):
+            pairs = h_bf[e]
+            h_bf[e] = placed(offset, [P, HALVES, PASS], BF16, "h_woven")
+            engine_copy(
+                out=h_bf[e][:].rearrange("p a b -> p (a b)").bitcast(words).rearrange("p (c u) -> p c u", u=HALVES),
+                in_=pairs[:].bitcast(words).rearrange("p u c -> p c u"),
+            )
 
         def quantise_h(e):
             words = keep.tile([P, C], U32, name=f"h_codes{e}", align_bytes=64)
             scales = keep.tile([P, C], U8, name=f"h_scales{e}", align_bytes=64)
             nc.vector.quantize_mx(
-                out=words[:].bitcast(FP8X4), scales=scales[:], in_=h_bf[e][:].rearrange("p c t -> p (c t)")
+                out=words[:].bitcast(FP8X4), scales=scales[:], in_=h_bf[e][:].rearrange("p a b -> p (a b)")
             )
             h_packed[e] = (words, scales)
 
@@ -294,6 +303,7 @@ def tile_moe_tk_glu_relu_kernel(tc, xT, w1, w3, w2, gate, offs, pos1, pos2, pos3
                     quantise(chunk)
                 if (kind, s) == ("w1", 0):
                     take_h(e - 1, start_of(chunk))
+                    weave_h(e - 1, start_of(chunk) + BUFFER // 2, nc.vector.tensor_copy, mybir.dt.int32)
                     quantise_h(e - 1)
                 if (kind, s) == ("w1", 1):
                     quantise(("w3", e, 0))
@@ -302,7 +312,6 @@ def tile_moe_tk_glu_relu_kernel(tc, xT, w1, w3, w2, gate, offs, pos1, pos2, pos3
             elif s == 0:
                 if kind == "w1" and e > 0:
                     take_h(e - 1, start_of(chunk))
-                    quantise_h(e - 1)
             else:
                 quantise(chunk)
                 if kind == "w3":
@@ -310,8 +319,11 @@ def tile_moe_tk_glu_relu_kernel(tc, xT, w1, w3, w2, gate, offs, pos1, pos2, pos3
                         for other_pass in range(PASSES):
                             gather_words(e + E - HELD, other_pass)
                         gather_scales(e + E - HELD)
+                    if e > 0:
+                        weave_h(e - 1, start_of(chunk) + BUFFER // 2 + (9 * C if chunk in held else 0), nc.scalar.copy, U32)
+                        quantise_h(e - 1)
                     take_relu(e, start_of(chunk))
-                    if e == 1:
+                    if e == 2:
                         early_y(0)
                 first_product(kind, e)
 

@@ -31,6 +31,7 @@ ROTATING = 9
 HELD = 3
 AHEAD = ROTATING - 3
 LAST = E - 1
+EARLY_ENTRIES = 384
 HALF = PACK * P * 4
 X_QUADS_ON_VECTOR = 84
 W_QUADS_ON_VECTOR = 96
@@ -53,7 +54,7 @@ def quads_on_vector(kind, e, s):
         return X_QUADS_ON_VECTOR if s == 0 else 0
     if kind == "w2":
         return 0
-    if (kind, e, s) == ("w3", LAST - 1, 1):
+    if (kind, e) == ("w3", LAST - 1):
         return BEFORE_LAST_QUADS_ON_VECTOR
     if e == LAST:
         return LAST_QUADS_ON_VECTOR[kind, s]
@@ -175,28 +176,25 @@ def tile_moe_tk_glu_relu_kernel(tc, xT, w1, w3, w2, gate, offs, pos1, pos2, pos3
             for other in range(PASSES):
                 packed[kind, e, other] = (words[:, other, :], scales[:, other, :])
 
-        def entries_of(e):
-            return offs_sb[:, e * C // 16 : (e + 1) * C // 16]
+        def gather(tile, window, first, count):
+            nc.vector.tensor_copy(tile, window[:].indirect(offs_sb[:, first // 16 : (first + count) // 16]))
 
-        def gather_words(e, s):
-            if e < E - HELD:
-                tile = keep.tile([P, C], U32, name=f"slot_codes{e}_{s}", align_bytes=64)
-            else:
-                tile = placed(start_of(held[e - (E - HELD)]) + BUFFER // 2 + s * 4 * C, [P, C], U32, "slot_codes")
-            nc.vector.tensor_copy(tile[:], x_codes[s][:].indirect(entries_of(e)))
-            slot_words[e, s] = tile
+        def gather_early(window, dtype, name):
+            tile = keep.tile([P, (E - HELD) * C], dtype, name=name, align_bytes=64)
+            for first in range(0, (E - HELD) * C, EARLY_ENTRIES):
+                gather(tile[:, first : first + EARLY_ENTRIES], window, first, EARLY_ENTRIES)
+            return [tile[:, e * C : (e + 1) * C] for e in range(E - HELD)]
 
-        def gather_scales(e):
-            if e < E - HELD:
-                tile = keep.tile([P, C], U8, name=f"slot_scales{e}", align_bytes=64)
-            else:
-                tile = placed(start_of(held[e - (E - HELD)]) + BUFFER // 2 + PASSES * 4 * C, [P, C], U8, "slot_scales")
-            nc.vector.tensor_copy(tile[:], x_scales[:].indirect(entries_of(e)))
-            slot_scales[e] = tile
+        def gather_late(e, offset):
+            for s in range(PASSES):
+                slot_words[e, s] = placed(offset + s * 4 * C, [P, C], U32, "slot_codes")[:]
+                gather(slot_words[e, s], x_codes[s], e * C, C)
+            slot_scales[e] = placed(offset + PASSES * 4 * C, [P, C], U8, "slot_scales")[:]
+            gather(slot_scales[e], x_scales, e * C, C)
 
         def first_product(kind, e):
             for half in range(HALVES):
-                if e == LAST:
+                if kind == "w3" and e >= HELD:
                     planes, cols = range(PACK), slice(half * P, (half + 1) * P)
                 else:
                     planes, cols = range(2 * half, 2 * half + 2), slice(0, C)
@@ -229,7 +227,15 @@ def tile_moe_tk_glu_relu_kernel(tc, xT, w1, w3, w2, gate, offs, pos1, pos2, pos3
             h_bf[e] = placed(offset, [P, HALVES, PASS], BF16, "h_bf")
             for half in range(HALVES):
                 bank = banks["w3", e, half]
-                nc.vector.tensor_tensor(like(h_bf[e][:, half, :], bank), bank, like(relu_a[e][:, half, :], bank), MULT)
+                if e < HELD:
+                    nc.vector.tensor_tensor(like(h_bf[e][:, half, :], bank), bank, like(relu_a[e][:, half, :], bank), MULT)
+                else:
+                    nc.vector.tensor_tensor(
+                        h_bf[e][:, half, :].rearrange("p (c u t) -> p c u t", u=HALVES, t=2),
+                        bank.rearrange("p c (u t) -> p c u t", t=2),
+                        relu_a[e][:].rearrange("p u (c t) -> p c u t", t=2)[:, half * P : (half + 1) * P],
+                        MULT,
+                    )
 
         def weave_h(e, offset, engine_copy, words):
             pairs = h_bf[e]
@@ -292,10 +298,11 @@ def tile_moe_tk_glu_relu_kernel(tc, xT, w1, w3, w2, gate, offs, pos1, pos2, pos3
                 quantise(chunk)
                 if s == 1:
                     spread_gates()
-                for other in range(E - HELD):
-                    gather_words(other, s)
-                    if s == PASSES - 1:
-                        gather_scales(other)
+                for other, words in enumerate(gather_early(x_codes[s], U32, f"early_codes{s}")):
+                    slot_words[other, s] = words
+                if s == PASSES - 1:
+                    for other, scales in enumerate(gather_early(x_scales, U8, "early_scales")):
+                        slot_scales[other] = scales
             elif kind == "w2":
                 quantise(chunk)
             elif e == LAST:
@@ -303,7 +310,6 @@ def tile_moe_tk_glu_relu_kernel(tc, xT, w1, w3, w2, gate, offs, pos1, pos2, pos3
                     quantise(chunk)
                 if (kind, s) == ("w1", 0):
                     take_h(e - 1, start_of(chunk))
-                    weave_h(e - 1, start_of(chunk) + BUFFER // 2, nc.vector.tensor_copy, mybir.dt.int32)
                     quantise_h(e - 1)
                 if (kind, s) == ("w1", 1):
                     quantise(("w3", e, 0))
@@ -312,14 +318,14 @@ def tile_moe_tk_glu_relu_kernel(tc, xT, w1, w3, w2, gate, offs, pos1, pos2, pos3
             elif s == 0:
                 if kind == "w1" and e > 0:
                     take_h(e - 1, start_of(chunk))
+                    if e > HELD:
+                        quantise_h(e - 1)
             else:
                 quantise(chunk)
                 if kind == "w3":
                     if chunk in held:
-                        for other_pass in range(PASSES):
-                            gather_words(e + E - HELD, other_pass)
-                        gather_scales(e + E - HELD)
-                    if e > 0:
+                        gather_late(e + E - HELD, start_of(chunk) + BUFFER // 2)
+                    if 0 < e <= HELD:
                         weave_h(e - 1, start_of(chunk) + BUFFER // 2 + (9 * C if chunk in held else 0), nc.scalar.copy, U32)
                         quantise_h(e - 1)
                     take_relu(e, start_of(chunk))
@@ -400,7 +406,7 @@ def tile_moe_tk_glu_relu_kernel(tc, xT, w1, w3, w2, gate, offs, pos1, pos2, pos3
         def fetch(n, r, cols):
             name = f"part{n}_{r}_{cols.start}"
             if n == 0 and r > 0:
-                part = placed(staging + (2 if r == 1 else 8) * width, [P, T], F32, name)
+                part = placed(second_free + 2 * HALF if r == 1 else staging + 8 * width, [P, T], F32, name)
             else:
                 part = keep.tile([P, cols.stop - cols.start], F32, name=name)
             entries = pos_sb[r][:, cols.start // 16 : cols.stop // 16]
@@ -443,10 +449,10 @@ def tile_moe_tk_glu_relu_kernel(tc, xT, w1, w3, w2, gate, offs, pos1, pos2, pos3
 
         token_halves = [slice(q * T // 2, (q + 1) * T // 2) for q in range(2)]
         whole = fetch(1, 0, tokens)
-        cut = [fetch(1, 1, cols) for cols in token_halves]
+        cut = [fetch(1, 1, slice(start, stop)) for start, stop in ((0, 2 * P), (2 * P, 3 * P), (3 * P, T))]
         parts = [
             [whole[:, block * P : (block + 1) * P] for block in blocks],
-            [cut[block // 2][:, block % 2 * P : (block % 2 + 1) * P] for block in blocks],
+            [cut[0][:, :P], cut[0][:, P:], cut[1][:], cut[2][:]],
         ]
         pairs = [psum.tile([P, T // 2], F32, name="pair", tag=tag) for tag in ("y0", "y2")]
         sum_in_psum(1, parts, [pairs[block // 2][:, block % 2 * P : (block % 2 + 1) * P] for block in blocks])

@@ -31,6 +31,7 @@ ROTATING = 9
 HELD = 3
 AHEAD = ROTATING - 3
 LAST = E - 1
+WOVEN = E - 2
 EARLY_ENTRIES = 384
 HALF = PACK * P * 4
 X_QUADS_ON_VECTOR = 84
@@ -194,7 +195,7 @@ def tile_moe_tk_glu_relu_kernel(tc, xT, w1, w3, w2, gate, offs, pos1, pos2, pos3
 
         def first_product(kind, e):
             for half in range(HALVES):
-                if kind == "w3" and e >= HELD:
+                if kind == "w3" and e >= WOVEN:
                     planes, cols = range(PACK), slice(half * P, (half + 1) * P)
                 else:
                     planes, cols = range(2 * half, 2 * half + 2), slice(0, C)
@@ -227,7 +228,7 @@ def tile_moe_tk_glu_relu_kernel(tc, xT, w1, w3, w2, gate, offs, pos1, pos2, pos3
             h_bf[e] = placed(offset, [P, HALVES, PASS], BF16, "h_bf")
             for half in range(HALVES):
                 bank = banks["w3", e, half]
-                if e < HELD:
+                if e < WOVEN:
                     nc.vector.tensor_tensor(like(h_bf[e][:, half, :], bank), bank, like(relu_a[e][:, half, :], bank), MULT)
                 else:
                     nc.vector.tensor_tensor(
@@ -318,14 +319,12 @@ def tile_moe_tk_glu_relu_kernel(tc, xT, w1, w3, w2, gate, offs, pos1, pos2, pos3
             elif s == 0:
                 if kind == "w1" and e > 0:
                     take_h(e - 1, start_of(chunk))
-                    if e > HELD:
-                        quantise_h(e - 1)
             else:
                 quantise(chunk)
                 if kind == "w3":
                     if chunk in held:
                         gather_late(e + E - HELD, start_of(chunk) + BUFFER // 2)
-                    if 0 < e <= HELD:
+                    if e > 0:
                         weave_h(e - 1, start_of(chunk) + BUFFER // 2 + (9 * C if chunk in held else 0), nc.scalar.copy, U32)
                         quantise_h(e - 1)
                     take_relu(e, start_of(chunk))

@@ -20,24 +20,27 @@ RELU = mybir.ActivationFunctionType.Relu
 
 P = 128
 PACK = 4
+PAIR = 2
 PASS = P * PACK
 PASSES = K // PASS
 HALVES = 2
 QUAD = 4
 SCALE_STEP = 4
+LIST_ROWS = 16
+LAST = E - 1
 
 BUFFER = PACK * PASS * 4
 ROTATING = 9
-HELD = 3
 AHEAD = ROTATING - 3
-LAST = E - 1
-WOVEN = E - 2
+EARLY = 3
 EARLY_ENTRIES = 384
-HALF = PACK * P * 4
-X_QUADS_ON_VECTOR = 84
-W_QUADS_ON_VECTOR = 96
-BEFORE_LAST_QUADS_ON_VECTOR = 64
-LAST_QUADS_ON_VECTOR = {("w1", 0): 96, ("w3", 0): 0, ("w1", 1): 84, ("w3", 1): 86}
+HALF_BYTES = PACK * P * 4
+HALF_WIDTH = PACK * P
+
+X_QUADS = 84
+W_QUADS = 96
+BEFORE_LAST_QUADS = 64
+LAST_QUADS = {("w1", 0): W_QUADS, ("w3", 0): 0, ("w1", 1): 84, ("w3", 1): 86}
 
 
 def chunk_order():
@@ -52,27 +55,27 @@ def chunk_order():
 
 def quads_on_vector(kind, e, s):
     if kind == "x":
-        return X_QUADS_ON_VECTOR if s == 0 else 0
+        return X_QUADS if s == 0 else 0
     if kind == "w2":
         return 0
     if (kind, e) == ("w3", LAST - 1):
-        return BEFORE_LAST_QUADS_ON_VECTOR
+        return BEFORE_LAST_QUADS
     if e == LAST:
-        return LAST_QUADS_ON_VECTOR[kind, s]
-    return W_QUADS_ON_VECTOR if s == 0 else 0
+        return LAST_QUADS[kind, s]
+    return W_QUADS if s == 0 else 0
 
 
 def tile_moe_tk_glu_relu_kernel(tc, xT, w1, w3, w2, gate, offs, pos1, pos2, pos3, out):
     nc = tc.nc
     with ExitStack() as ctx:
         keep = ctx.enter_context(tc.tile_pool(name="keep", bufs=1))
-        ring = ctx.enter_context(tc.tile_pool(name="ring", bufs=1))
+        buffers = ctx.enter_context(tc.tile_pool(name="buffers", bufs=1))
         groups = ctx.enter_context(tc.tile_pool(name="groups", bufs=3))
         codes = ctx.enter_context(tc.tile_pool(name="codes", bufs=4))
         psum = ctx.enter_context(tc.psum_pool(name="psum", bufs=1))
 
-        offs_sb = keep.tile([P, SLOTS // 16], U16, name="offs_sb")
-        pos_sb = [keep.tile([P, T // 16], U16, name=f"pos_sb{r}") for r in range(TOP)]
+        offs_sb = keep.tile([P, SLOTS // LIST_ROWS], U16, name="offs_sb")
+        pos_sb = [keep.tile([P, T // LIST_ROWS], U16, name=f"pos_sb{r}") for r in range(TOP)]
         x_codes = [keep.tile([P, T], U32, name=f"x_codes{s}", align_bytes=64) for s in range(PASSES)]
         x_scales = keep.tile([P, T], U8, name="x_scales", align_bytes=64)
         gate_rows = keep.tile([P, T], F32, name="gate_rows")
@@ -85,20 +88,19 @@ def tile_moe_tk_glu_relu_kernel(tc, xT, w1, w3, w2, gate, offs, pos1, pos2, pos3
         y_sb = [keep.tile([P, SLOTS], F32, name=f"y_sb{n}") for n in range(HALVES)]
 
         chunks = chunk_order()
-        raw, grouped, packed = {}, {}, {}
+        raw, grouped, packed, banks = {}, {}, {}, {}
         slot_words, slot_scales, relu_a, h_bf, h_packed = {}, {}, {}, {}, {}
-        banks = {}
 
-        held = [("w3", e, 1) for e in range(HELD)]
+        held = [("w3", e, 1) for e in range(E - EARLY)]
         in_turn = [chunk for chunk in chunks if chunk not in held]
 
         def start_of(chunk):
             if chunk in held:
-                return ROTATING * BUFFER + held.index(chunk) * (BUFFER + C)
+                return (ROTATING + held.index(chunk)) * BUFFER
             return in_turn.index(chunk) % ROTATING * BUFFER
 
         def placed(offset, shape, dtype, name):
-            return ring.tile(shape, dtype, name=name, tag=f"{name}_{offset}", align_bytes=64, offset=offset)
+            return buffers.tile(shape, dtype, name=name, tag=f"{name}_{offset}", align_bytes=64, offset=offset)
 
         def load(chunk):
             kind, e, s = chunk
@@ -132,59 +134,47 @@ def tile_moe_tk_glu_relu_kernel(tc, xT, w1, w3, w2, gate, offs, pos1, pos2, pos3
             cut = quads_on_vector(kind, e, s)
             if cut > 0:
                 nc.vector.tensor_copy(out=flat[:, :cut], in_=source[:, :cut])
-            if cut < source.shape[1]:
-                nc.scalar.copy(out=flat[:, cut:], in_=source[:, cut:])
+            nc.scalar.copy(out=flat[:, cut:], in_=source[:, cut:])
 
-        def quantise_halves(experts, n, source):
-            words = keep.tile([P, len(experts) * P], U32, name=f"w2_codes{experts[0]}_{n}", align_bytes=64)
-            scales = keep.tile([P, len(experts) * P], U8, name=f"w2_scales{experts[0]}_{n}", align_bytes=64)
+        def quantise_w2(parts, source):
+            name = "%d_%d" % parts[0]
+            words = keep.tile([P, len(parts) * P], U32, name="w2_codes" + name, align_bytes=64)
+            scales = keep.tile([P, len(parts) * P], U8, name="w2_scales" + name, align_bytes=64)
             nc.vector.quantize_mx(out=words[:].bitcast(FP8X4), scales=scales[:], in_=source)
-            for place, e in enumerate(experts):
+            for place, (e, n) in enumerate(parts):
                 cols = slice(place * P, (place + 1) * P)
                 packed["w2", e, n] = (words[:, cols], scales[:, cols])
 
-        def quantise(chunk):
-            kind, e, s = chunk
-            source = grouped[chunk]
-            if kind == "x":
-                nc.vector.quantize_mx(
-                    out=x_codes[s][:].bitcast(FP8X4), scales=x_scales[SCALE_STEP * s : P, :], in_=source[:, s, :]
-                )
-                return
-            if kind == "w2":
-                words = keep.tile([P, N], U32, name=f"w2_codes{e}", align_bytes=64)
-                scales = keep.tile([P, N], U8, name=f"w2_scales{e}", align_bytes=64)
-                nc.vector.quantize_mx(out=words[:].bitcast(FP8X4), scales=scales[:], in_=source[:])
-                for n in range(HALVES):
-                    packed[kind, e, n] = (words[:, n * P : (n + 1) * P], scales[:, n * P : (n + 1) * P])
-                return
-            if e == LAST:
-                if (kind, s) == ("w3", 0):
-                    words = placed(start_of(("w1", e, 1)), [P, H], U32, "w_codes")
-                else:
-                    words = codes.tile([P, H], U32, name="w_codes", align_bytes=64)
-                scales = codes.tile([P, H], U8, name="w_scales", align_bytes=64)
-                nc.vector.quantize_mx(out=words[:].bitcast(FP8X4), scales=scales[:], in_=source[:, s, :])
-                packed[kind, e, s] = (words, scales)
-                return
+        def quantise_tokens(s):
+            nc.vector.quantize_mx(
+                out=x_codes[s][:].bitcast(FP8X4), scales=x_scales[SCALE_STEP * s : P, :], in_=grouped["x", 0, s][:, s, :]
+            )
+
+        def quantise_matrix(kind, e):
             words = codes.tile([P, PASSES, H], U32, name="w_codes", align_bytes=64)
             scales = codes.tile([P, PASSES, H], U8, name="w_scales", align_bytes=64)
             nc.vector.quantize_mx(
                 out=words[:].rearrange("p s w -> p (s w)").bitcast(FP8X4),
                 scales=scales[:].rearrange("p s w -> p (s w)"),
-                in_=source[:].rearrange("p s w -> p (s w)"),
+                in_=grouped[kind, e, 0][:].rearrange("p s w -> p (s w)"),
             )
-            for other in range(PASSES):
-                packed[kind, e, other] = (words[:, other, :], scales[:, other, :])
+            for s in range(PASSES):
+                packed[kind, e, s] = (words[:, s, :], scales[:, s, :])
 
-        def gather(tile, window, first, count):
-            nc.vector.tensor_copy(tile, window[:].indirect(offs_sb[:, first // 16 : (first + count) // 16]))
+        def quantise_last_pass(kind, s, words):
+            scales = codes.tile([P, H], U8, name="w_scales", align_bytes=64)
+            nc.vector.quantize_mx(out=words[:].bitcast(FP8X4), scales=scales[:], in_=grouped[kind, LAST, s][:, s, :])
+            packed[kind, LAST, s] = (words, scales)
+
+        def gather(target, window, first, count):
+            entries = offs_sb[:, first // LIST_ROWS : (first + count) // LIST_ROWS]
+            nc.vector.tensor_copy(target, window[:].indirect(entries))
 
         def gather_early(window, dtype, name):
-            tile = keep.tile([P, (E - HELD) * C], dtype, name=name, align_bytes=64)
-            for first in range(0, (E - HELD) * C, EARLY_ENTRIES):
+            tile = keep.tile([P, EARLY * C], dtype, name=name, align_bytes=64)
+            for first in range(0, EARLY * C, EARLY_ENTRIES):
                 gather(tile[:, first : first + EARLY_ENTRIES], window, first, EARLY_ENTRIES)
-            return [tile[:, e * C : (e + 1) * C] for e in range(E - HELD)]
+            return [tile[:, e * C : (e + 1) * C] for e in range(EARLY)]
 
         def gather_late(e, offset):
             for s in range(PASSES):
@@ -194,12 +184,12 @@ def tile_moe_tk_glu_relu_kernel(tc, xT, w1, w3, w2, gate, offs, pos1, pos2, pos3
             gather(slot_scales[e], x_scales, e * C, C)
 
         def first_product(kind, e):
-            for half in range(HALVES):
-                if kind == "w3" and e >= WOVEN:
-                    planes, cols = range(PACK), slice(half * P, (half + 1) * P)
+            for u in range(HALVES):
+                if kind == "w1":
+                    planes, cols = range(PAIR * u, PAIR * (u + 1)), slice(0, C)
                 else:
-                    planes, cols = range(2 * half, 2 * half + 2), slice(0, C)
-                bank = psum.tile([P, len(planes), cols.stop - cols.start], F32, name="bank", tag=f"{kind}_{half}")
+                    planes, cols = range(PACK), slice(u * P, (u + 1) * P)
+                bank = psum.tile([P, len(planes), cols.stop - cols.start], F32, name="bank", tag=f"{kind}_{u}")
                 for place, t in enumerate(planes):
                     rows = slice(t * P, (t + 1) * P)
                     for s in range(PASSES):
@@ -213,44 +203,29 @@ def tile_moe_tk_glu_relu_kernel(tc, xT, w1, w3, w2, gate, offs, pos1, pos2, pos3
                             start=(s == 0),
                             stop=(s == PASSES - 1),
                         )
-                banks[kind, e, half] = bank[:].rearrange("p t c -> p c t")
-
-        def like(flat, bank):
-            return flat.rearrange("p (c t) -> p c t", t=bank.shape[2])
+                banks[kind, e, u] = bank
 
         def take_relu(e, offset):
-            relu_a[e] = placed(offset, [P, HALVES, PASS], F32, "relu_a")
-            for half in range(HALVES):
-                bank = banks["w1", e, half]
-                nc.scalar.activation(like(relu_a[e][:, half, :], bank), bank, RELU)
+            relu_a[e] = placed(offset, [P, HALVES, C, PAIR], F32, "relu_a")
+            for u in range(HALVES):
+                nc.scalar.activation(relu_a[e][:, u], banks["w1", e, u][:].rearrange("p t c -> p c t"), RELU)
 
         def take_h(e, offset):
-            h_bf[e] = placed(offset, [P, HALVES, PASS], BF16, "h_bf")
+            h_bf[e] = placed(offset, [P, C, HALVES, PAIR], BF16, "h_bf")
             for half in range(HALVES):
-                bank = banks["w3", e, half]
-                if e < WOVEN:
-                    nc.vector.tensor_tensor(like(h_bf[e][:, half, :], bank), bank, like(relu_a[e][:, half, :], bank), MULT)
-                else:
-                    nc.vector.tensor_tensor(
-                        h_bf[e][:, half, :].rearrange("p (c u t) -> p c u t", u=HALVES, t=2),
-                        bank.rearrange("p c (u t) -> p c u t", t=2),
-                        relu_a[e][:].rearrange("p u (c t) -> p c u t", t=2)[:, half * P : (half + 1) * P],
-                        MULT,
-                    )
-
-        def weave_h(e, offset, engine_copy, words):
-            pairs = h_bf[e]
-            h_bf[e] = placed(offset, [P, HALVES, PASS], BF16, "h_woven")
-            engine_copy(
-                out=h_bf[e][:].rearrange("p a b -> p (a b)").bitcast(words).rearrange("p (c u) -> p c u", u=HALVES),
-                in_=pairs[:].bitcast(words).rearrange("p u c -> p c u"),
-            )
+                cols = slice(half * P, (half + 1) * P)
+                nc.vector.tensor_tensor(
+                    h_bf[e][:, cols],
+                    banks["w3", e, half][:].rearrange("p (u v) c -> p c u v", v=PAIR),
+                    relu_a[e][:].rearrange("p u c v -> p c u v")[:, cols],
+                    MULT,
+                )
 
         def quantise_h(e):
             words = keep.tile([P, C], U32, name=f"h_codes{e}", align_bytes=64)
             scales = keep.tile([P, C], U8, name=f"h_scales{e}", align_bytes=64)
             nc.vector.quantize_mx(
-                out=words[:].bitcast(FP8X4), scales=scales[:], in_=h_bf[e][:].rearrange("p a b -> p (a b)")
+                out=words[:].bitcast(FP8X4), scales=scales[:], in_=h_bf[e][:].rearrange("p c u v -> p (c u v)")
             )
             h_packed[e] = (words, scales)
 
@@ -267,24 +242,12 @@ def tile_moe_tk_glu_relu_kernel(tc, xT, w1, w3, w2, gate, offs, pos1, pos2, pos3
                 stop=True,
             )
 
-        def early_y(e):
+        def first_y():
             bank = psum.tile([P, HALVES, C], F32, name="bank_y", tag="w1_0")
             for n in range(HALVES):
-                second_product(e, n, bank[:, n, :])
+                second_product(0, n, bank[:, n, :])
             for n in range(HALVES):
-                nc.scalar.copy(out=y_sb[n][:, e * C : (e + 1) * C], in_=bank[:, n, :])
-
-        def spread_gates():
-            bank = psum.tile([P, T // P, P], F32, name="gate_bank", tag="y3")
-            for block in range(T // P):
-                nc.tensor.transpose(bank[:, block, :], gate_rows[:, block * P : (block + 1) * P], identity[:])
-            nc.scalar.copy(out=gate_columns[:], in_=bank[:, :, 0:TOP])
-            for r in range(TOP):
-                bank = psum.tile([P, T // P, P], F32, name="gate_bank", tag=f"y{r}")
-                for block in range(T // P):
-                    column = gate_columns[:, block, r : r + 1].to_broadcast([P, P])
-                    nc.tensor.transpose(bank[:, block, :], column, identity[:])
-                nc.scalar.copy(out=gate_sb[r][:], in_=bank[:].rearrange("q b p -> q (b p)"))
+                nc.scalar.copy(out=y_sb[n][:, 0:C], in_=bank[:, n, :])
 
         def late_y(experts, n, tag, engine_copy=nc.scalar.copy):
             bank = psum.tile([P, len(experts) * C], F32, name="bank_y", tag=tag)
@@ -292,45 +255,54 @@ def tile_moe_tk_glu_relu_kernel(tc, xT, w1, w3, w2, gate, offs, pos1, pos2, pos3
                 second_product(e, n, bank[:, place * C : (place + 1) * C])
             engine_copy(out=y_sb[n][:, experts[0] * C : (experts[-1] + 1) * C], in_=bank[:])
 
+        blocks = range(T // P)
+
+        def spread_gates():
+            bank = psum.tile([P, T // P, P], F32, name="gate_bank", tag="y3")
+            for block in blocks:
+                nc.tensor.transpose(bank[:, block, :], gate_rows[:, block * P : (block + 1) * P], identity[:])
+            nc.scalar.copy(out=gate_columns[:], in_=bank[:, :, 0:TOP])
+            for r in range(TOP):
+                bank = psum.tile([P, T // P, P], F32, name="gate_bank", tag=f"y{r}")
+                for block in blocks:
+                    column = gate_columns[:, block, r : r + 1].to_broadcast([P, P])
+                    nc.tensor.transpose(bank[:, block, :], column, identity[:])
+                nc.scalar.copy(out=gate_sb[r][:], in_=bank[:].rearrange("q b p -> q (b p)"))
+
         def work(chunk):
             kind, e, s = chunk
             interleave(chunk)
             if kind == "x":
-                quantise(chunk)
-                if s == 1:
+                quantise_tokens(s)
+                if s == PASSES - 1:
                     spread_gates()
                 for other, words in enumerate(gather_early(x_codes[s], U32, f"early_codes{s}")):
                     slot_words[other, s] = words
                 if s == PASSES - 1:
                     for other, scales in enumerate(gather_early(x_scales, U8, "early_scales")):
                         slot_scales[other] = scales
-            elif kind == "w2":
-                quantise(chunk)
-            elif e == LAST:
-                if (kind, s) != ("w3", 0):
-                    quantise(chunk)
-                if (kind, s) == ("w1", 0):
-                    take_h(e - 1, start_of(chunk))
-                    quantise_h(e - 1)
-                if (kind, s) == ("w1", 1):
-                    quantise(("w3", e, 0))
-                if s == 1:
-                    first_product(kind, e)
-            elif s == 0:
-                if kind == "w1" and e > 0:
-                    take_h(e - 1, start_of(chunk))
-            else:
-                quantise(chunk)
-                if kind == "w3":
-                    if chunk in held:
-                        gather_late(e + E - HELD, start_of(chunk) + BUFFER // 2)
-                    if e > 0:
-                        weave_h(e - 1, start_of(chunk) + BUFFER // 2 + (9 * C if chunk in held else 0), nc.scalar.copy, U32)
-                        quantise_h(e - 1)
-                    take_relu(e, start_of(chunk))
-                    if e == 2:
-                        early_y(0)
-                first_product(kind, e)
+                return
+            if kind == "w2":
+                quantise_w2([(e, n) for n in range(HALVES)], grouped[chunk][:])
+                return
+            if e == LAST and (kind, s) != ("w3", 0):
+                quantise_last_pass(kind, s, codes.tile([P, H], U32, name="w_codes", align_bytes=64))
+            if (kind, s) == ("w1", 0) and e > 0:
+                take_h(e - 1, start_of(chunk))
+                quantise_h(e - 1)
+            if s == 0:
+                return
+            if e < LAST:
+                quantise_matrix(kind, e)
+            elif kind == "w1":
+                quantise_last_pass("w3", 0, placed(start_of(chunk), [P, H], U32, "w_codes"))
+            if kind == "w3" and e < LAST:
+                if chunk in held:
+                    gather_late(e + EARLY, start_of(chunk) + BUFFER // 2)
+                take_relu(e, start_of(chunk))
+                if e == 2:
+                    first_y()
+            first_product(kind, e)
 
         for step in range(-AHEAD, len(chunks)):
             if step + AHEAD < len(chunks):
@@ -342,21 +314,23 @@ def tile_moe_tk_glu_relu_kernel(tc, xT, w1, w3, w2, gate, offs, pos1, pos2, pos3
             if step >= 0:
                 work(chunks[step])
 
-        width = PACK * P
-        first_free = len(in_turn) % ROTATING * BUFFER
-        second_free = (len(in_turn) + 1) % ROTATING * BUFFER
-        staging = start_of(held[0])
+        relu_place, other_place, fetch_place = [(len(in_turn) + turn) % ROTATING * BUFFER for turn in range(3)]
+        h_place = relu_place + 2 * HALF_BYTES
+
+        def in_y(first_expert):
+            return y_sb[0][:, first_expert * C : (first_expert + 2) * C].rearrange("p (j w) -> p j w", j=PACK)
+
         halves = {}
-        halves[1, 0] = placed(first_free, [P, PACK, P], F32, "raw_half")[:]
-        both = placed(first_free + 2 * HALF, [P, 2, PACK, P], F32, "raw_halves")
-        for e in (2, 3):
-            halves[e, 0] = both[:, e - 2]
-        halves[4, 0] = placed(second_free + 3 * HALF, [P, PACK, P], F32, "raw_half")[:]
-        halves[5, 0] = y_sb[0][:, C : 3 * C].rearrange("p (j w) -> p j w", j=PACK)
-        halves[1, 1] = y_sb[0][:, 3 * C : 5 * C].rearrange("p (j w) -> p j w", j=PACK)
+        halves[1, 0] = placed(relu_place, [P, PACK, P], F32, "raw_half")[:]
+        two_halves = placed(h_place, [P, 2, PACK, P], F32, "raw_halves")
+        halves[2, 0] = two_halves[:, 0]
+        halves[3, 0] = two_halves[:, 1]
+        halves[4, 0] = placed(other_place + 3 * HALF_BYTES, [P, PACK, P], F32, "raw_half")[:]
+        halves[5, 0] = in_y(1)
+        halves[1, 1] = in_y(3)
         for e in (2, 3, 4):
-            halves[e, 1] = placed(second_free + (e - 2) * HALF, [P, PACK, P], F32, "raw_half")[:]
-        halves[5, 1] = y_sb[1][:, C : 3 * C].rearrange("p (j w) -> p j w", j=PACK)
+            halves[e, 1] = placed(other_place + (e - 2) * HALF_BYTES, [P, PACK, P], F32, "raw_half")[:]
+        halves[5, 1] = placed(fetch_place + HALF_BYTES // 2, [P, PACK, P], F32, "raw_half")[:]
         for n in range(HALVES):
             for e in range(1, E):
                 rows = w2[e][:, n * P : (n + 1) * P]
@@ -365,60 +339,57 @@ def tile_moe_tk_glu_relu_kernel(tc, xT, w1, w3, w2, gate, offs, pos1, pos2, pos3
                 for r, pos in enumerate((pos1, pos2, pos3)):
                     nc.sync.dma_start(pos_sb[r][:], pos)
 
+        firsts = keep.tile([P, LAST, HALF_WIDTH], BF16, name="firsts", align_bytes=64)
+        staging = start_of(held[0])
+        seconds = [placed(staging + pair * HALF_BYTES, [P, 2, HALF_WIDTH], BF16, "seconds") for pair in range(2)]
+        last_second = placed(staging + 2 * HALF_BYTES, [P, HALF_WIDTH], BF16, "last_second")
+
         def interleave_half(e, n, target):
             source = halves[e, n].rearrange("p j (m i) -> p m j i", i=QUAD)
             nc.scalar.copy(out=target.rearrange("p (m i j) -> p m j i", i=QUAD, j=PACK), in_=source)
 
-        first = keep.tile([P, 4 * width], BF16, name="first", align_bytes=64)
-        first5 = keep.tile([P, width], BF16, name="first5", align_bytes=64)
-        second12 = placed(staging, [P, 2 * width], BF16, "second12")
-        second34 = placed(staging + 4 * width, [P, 2 * width], BF16, "second34")
-        second5 = placed(staging + 8 * width, [P, width], BF16, "second5")
-        interleave_half(1, 0, first[:, :width])
-        take_relu(LAST, first_free)
+        def quantise_firsts(experts):
+            source = firsts[:, experts[0] - 1 : experts[-1], :].rearrange("p e w -> p (e w)")
+            quantise_w2([(e, 0) for e in experts], source)
+
+        interleave_half(1, 0, firsts[:, 0, :])
+        take_relu(LAST, relu_place)
         nc.vector.tensor_copy(
-            out=first[:, width : 3 * width].rearrange("p (e m i j) -> p e m j i", e=2, i=QUAD, j=PACK),
-            in_=both[:].rearrange("p e j (m i) -> p e m j i", i=QUAD),
+            out=firsts[:, 1:3, :].rearrange("p e (m i j) -> p e m j i", i=QUAD, j=PACK),
+            in_=two_halves[:].rearrange("p e j (m i) -> p e m j i", i=QUAD),
         )
-        quantise_halves([1, 2], 0, first[:, : 2 * width])
-        take_h(LAST, first_free + 2 * HALF)
-        interleave_half(4, 0, first[:, 3 * width :])
-        quantise_halves([3, 4], 0, first[:, 2 * width :])
+        quantise_firsts([1])
+        quantise_firsts([2, 3])
+        take_h(LAST, h_place)
+        interleave_half(4, 0, firsts[:, 3, :])
+        interleave_half(5, 0, firsts[:, 4, :])
+        quantise_firsts([4, 5])
         quantise_h(LAST)
-        interleave_half(5, 0, first5[:])
-        quantise_halves([5], 0, first5[:])
-        late_y([1, 2], 0, "y0")
-        interleave_half(1, 1, second12[:, :width])
+        late_y([1, 2], 0, "y0", nc.vector.tensor_copy)
+        interleave_half(1, 1, seconds[0][:, 0, :])
         late_y([3, 4], 0, "y1")
         late_y([5], 0, "y2", nc.vector.tensor_copy)
-        interleave_half(2, 1, second12[:, width:])
-        quantise_halves([1, 2], 1, second12[:])
-        for place, e in enumerate((3, 4)):
-            interleave_half(e, 1, second34[:, place * width : (place + 1) * width])
-        quantise_halves([3, 4], 1, second34[:])
-        interleave_half(5, 1, second5[:])
+
+        interleave_half(2, 1, seconds[0][:, 1, :])
+        quantise_w2([(1, 1), (2, 1)], seconds[0][:].rearrange("p e w -> p (e w)"))
+        interleave_half(3, 1, seconds[1][:, 0, :])
+        interleave_half(4, 1, seconds[1][:, 1, :])
+        quantise_w2([(3, 1), (4, 1)], seconds[1][:].rearrange("p e w -> p (e w)"))
+        interleave_half(5, 1, last_second[:])
         late_y([1, 2], 1, "y3")
-        quantise_halves([5], 1, second5[:])
+        quantise_w2([(5, 1)], last_second[:])
         late_y([3, 4], 1, "y0")
         late_y([5], 1, "y2")
 
-        def fetch(n, r, cols):
-            name = f"part{n}_{r}_{cols.start}"
-            if n == 0 and r > 0:
-                part = placed(second_free + 2 * HALF if r == 1 else staging + 8 * width, [P, T], F32, name)
-            else:
-                part = keep.tile([P, cols.stop - cols.start], F32, name=name)
-            entries = pos_sb[r][:, cols.start // 16 : cols.stop // 16]
+        def fetch(n, r, cols, part):
+            entries = pos_sb[r][:, cols.start // LIST_ROWS : cols.stop // LIST_ROWS]
             nc.vector.tensor_tensor(part[:], y_sb[n][:].indirect(entries), gate_sb[r][:, cols], MULT)
-            return part
+            return [part[:, start : start + P] for start in range(0, cols.stop - cols.start, P)]
 
-        def add(name, first, second):
-            total = keep.tile([P, second.shape[1]], F32, name=name)
-            nc.vector.tensor_tensor(total[:], first, second[:], ADD)
-            return total
+        def new_part(n, r, cols):
+            return keep.tile([P, cols.stop - cols.start], F32, name=f"part{n}_{r}_{cols.start}")
 
-        blocks = range(T // P)
-        free_banks = [f"{kind}_{half}" for kind in ("w1", "w3") for half in range(HALVES)]
+        free_banks = [f"{kind}_{u}" for kind in ("w1", "w3") for u in range(HALVES)]
 
         def sum_in_psum(n, parts, targets):
             turned = [psum.tile([P, P], F32, name="turned", tag=free_banks[block]) for block in blocks]
@@ -438,24 +409,29 @@ def tile_moe_tk_glu_relu_kernel(tc, xT, w1, w3, w2, gate, offs, pos1, pos2, pos3
                 nc.tensor.transpose(targets[block], turned_sb[:], identity[:])
 
         tokens = slice(0, T)
-        parts = [fetch(0, r, tokens) for r in range(TOP)]
+        parts = [
+            fetch(0, 0, tokens, new_part(0, 0, tokens)),
+            fetch(0, 1, tokens, placed(fetch_place + HALF_BYTES, [P, T], F32, "second_part")),
+            fetch(0, 2, tokens, placed(fetch_place, [P, T], F32, "third_part")),
+        ]
         upright = psum.tile([P, T // P, P], F32, name="upright", tag="y1")
-        parts = [[part[:, block * P : (block + 1) * P] for block in blocks] for part in parts]
         sum_in_psum(0, parts, [upright[:, block, :] for block in blocks])
         result = keep.tile([P, T], F32, name="result0")
         nc.scalar.copy(out=result[:], in_=upright[:].rearrange("p b t -> p (b t)"))
         nc.sync.dma_start(out=out[0:P, :], in_=result[:])
 
-        token_halves = [slice(q * T // 2, (q + 1) * T // 2) for q in range(2)]
-        whole = fetch(1, 0, tokens)
-        cut = [fetch(1, 1, slice(start, stop)) for start, stop in ((0, 2 * P), (2 * P, 3 * P), (3 * P, T))]
+        pieces = [slice(0, 2 * P), slice(2 * P, 3 * P), slice(3 * P, T)]
         parts = [
-            [whole[:, block * P : (block + 1) * P] for block in blocks],
-            [cut[0][:, :P], cut[0][:, P:], cut[1][:], cut[2][:]],
+            fetch(1, 0, tokens, new_part(1, 0, tokens)),
+            [block for cols in pieces for block in fetch(1, 1, cols, new_part(1, 1, cols))],
         ]
-        pairs = [psum.tile([P, T // 2], F32, name="pair", tag=tag) for tag in ("y0", "y2")]
-        sum_in_psum(1, parts, [pairs[block // 2][:, block % 2 * P : (block % 2 + 1) * P] for block in blocks])
-        ends = [fetch(1, TOP - 1, cols) for cols in token_halves]
-        for cols, pair, end in zip(token_halves, pairs, ends):
-            result = add(f"result1_{cols.start}", pair[:], end)
+        sums = [psum.tile([P, T // 2], F32, name="sum_of_two", tag=tag) for tag in ("y0", "y2")]
+        sum_in_psum(1, parts, [sums[block // 2][:, block % 2 * P : (block % 2 + 1) * P] for block in blocks])
+        token_halves = [slice(q * T // 2, (q + 1) * T // 2) for q in range(2)]
+        thirds = [new_part(1, 2, cols) for cols in token_halves]
+        for cols, third in zip(token_halves, thirds):
+            fetch(1, 2, cols, third)
+        for cols, sum_of_two, third in zip(token_halves, sums, thirds):
+            result = keep.tile([P, T // 2], F32, name=f"result1_{cols.start}")
+            nc.vector.tensor_tensor(result[:], sum_of_two[:], third[:], ADD)
             nc.sync.dma_start(out=out[P : 2 * P, cols], in_=result[:])

@@ -336,8 +336,9 @@ def tile_moe_tk_glu_relu_kernel(tc, xT, w1, w3, w2, gate, offs, pos1, pos2, pos3
                 rows = w2[e][:, n * P : (n + 1) * P]
                 nc.sync.dma_start(out=halves[e, n], in_=rows.rearrange("(p j) w -> p j w", j=PACK))
             if n == 0:
-                for r, pos in enumerate((pos1, pos2, pos3)):
-                    nc.sync.dma_start(pos_sb[r][:], pos)
+                nc.sync.dma_start(pos_sb[0][:], pos1)
+        nc.sync.dma_start(pos_sb[1][:], pos2)
+        nc.sync.dma_start(pos_sb[2][:], pos3)
 
         firsts = keep.tile([P, LAST, HALF_WIDTH], BF16, name="firsts", align_bytes=64)
         staging = start_of(held[0])

@@ -17,6 +17,7 @@ FP8X4 = mybir.dt.float8_e4m3fn_x4
 MULT = mybir.AluOpType.mult
 ADD = mybir.AluOpType.add
 RELU = mybir.ActivationFunctionType.Relu
+COPY = mybir.ActivationFunctionType.Copy
 
 P = 128
 PACK = 4
@@ -33,31 +34,27 @@ BUFFER = PACK * PASS * 4
 ROTATING = 9
 AHEAD = ROTATING - 3
 EARLY = 3
+AMID = 2
 EARLY_ENTRIES = 384
-HALF_BYTES = PACK * P * 4
-HALF_WIDTH = PACK * P
 
 X_QUADS = 84
 W_QUADS = 96
 BEFORE_LAST_QUADS = 64
-LAST_QUADS = {("w1", 0): W_QUADS, ("w3", 0): 0, ("w1", 1): 84, ("w3", 1): 86}
+LAST_QUADS = {("w1", 0): W_QUADS, ("w1", 1): 24, ("w3", 0): 92, ("w3", 1): 86}
 
 
 def chunk_order():
     order = [("x", 0, s) for s in range(PASSES)]
-    for e in range(LAST):
-        order += [("w1", e, 0), ("w1", e, 1), ("w3", e, 0)]
-        if e == 1:
-            order.append(("w2", 0, 0))
-        order.append(("w3", e, 1))
-    return order + [(kind, LAST, s) for s in range(PASSES) for kind in ("w1", "w3")]
+    for e in range(E):
+        if 0 <= e - EARLY < AMID:
+            order.append(("w2", e - EARLY, 0))
+        order += [(kind, e, s) for kind in ("w1", "w3") for s in range(PASSES)]
+    return order
 
 
 def quads_on_vector(kind, e, s):
     if kind == "x":
         return X_QUADS if s == 0 else 0
-    if kind == "w2":
-        return 0
     if (kind, e) == ("w3", LAST - 1):
         return BEFORE_LAST_QUADS
     if e == LAST:
@@ -71,7 +68,7 @@ def tile_moe_tk_glu_relu_kernel(tc, xT, w1, w3, w2, gate, offs, pos1, pos2, pos3
         keep = ctx.enter_context(tc.tile_pool(name="keep", bufs=1))
         buffers = ctx.enter_context(tc.tile_pool(name="buffers", bufs=1))
         groups = ctx.enter_context(tc.tile_pool(name="groups", bufs=3))
-        codes = ctx.enter_context(tc.tile_pool(name="codes", bufs=4))
+        codes = ctx.enter_context(tc.tile_pool(name="codes", bufs=6))
         psum = ctx.enter_context(tc.psum_pool(name="psum", bufs=1))
 
         offs_sb = keep.tile([P, SLOTS // LIST_ROWS], U16, name="offs_sb")
@@ -85,7 +82,7 @@ def tile_moe_tk_glu_relu_kernel(tc, xT, w1, w3, w2, gate, offs, pos1, pos2, pos3
         make_identity(nc, identity[:])
         gate_columns = keep.tile([P, T // P, TOP], F32, name="gate_columns")
         gate_sb = [keep.tile([P, T], F32, name=f"gate_sb{r}") for r in range(TOP)]
-        y_sb = [keep.tile([P, SLOTS], F32, name=f"y_sb{n}") for n in range(HALVES)]
+        y_sb = [keep.tile([P, SLOTS], F32, name=f"y_sb{n}", align_bytes=64) for n in range(HALVES)]
 
         chunks = chunk_order()
         raw, grouped, packed, banks = {}, {}, {}, {}
@@ -102,29 +99,39 @@ def tile_moe_tk_glu_relu_kernel(tc, xT, w1, w3, w2, gate, offs, pos1, pos2, pos3
         def placed(offset, shape, dtype, name):
             return buffers.tile(shape, dtype, name=name, tag=f"{name}_{offset}", align_bytes=64, offset=offset)
 
+        raw2 = {}
+        grouped2 = [keep.tile([P, PACK * N], BF16, name=f"grouped2_{e}", align_bytes=64)[:] for e in range(LAST)]
+        grouped2.append(y_sb[0][:, AMID * C : (AMID + 2) * C].bitcast(BF16))
+        both, first, second = slice(0, HALVES), slice(0, 1), slice(1, 2)
+        on_vector, on_scalar = nc.vector.tensor_copy, nc.scalar.copy
+
+        def load_w2(e, target):
+            nc.sync.dma_start(out=target, in_=w2[e].rearrange("(p j) w -> p j w", j=PACK))
+            raw2[e] = target
+
+        def interleave_w2(e, halves, engine_copy):
+            source = raw2[e][:, :, halves.start * P : halves.stop * P].rearrange("p j (m i) -> p m j i", i=QUAD)
+            target = grouped2[e][:, halves.start * PACK * P : halves.stop * PACK * P]
+            engine_copy(out=target.rearrange("p (m i j) -> p m j i", i=QUAD, j=PACK), in_=source)
+
         def load(chunk):
             kind, e, s = chunk
             if kind == "w2":
-                tile = placed(start_of(chunk), [P, PACK, N], F32, "raw2")
-                rows = w2[e]
-            else:
-                tile = placed(start_of(chunk), [P, PACK, PASS], F32, "raw")
-                rows = {"x": xT, "w1": w1[e], "w3": w3[e]}[kind][s * PASS : (s + 1) * PASS, :]
+                load_w2(e, placed(start_of(chunk), [P, PACK, N], F32, "raw2")[:])
+                return
+            tile = placed(start_of(chunk), [P, PACK, PASS], F32, "raw")
+            rows = {"x": xT, "w1": w1[e], "w3": w3[e]}[kind][s * PASS : (s + 1) * PASS, :]
             nc.sync.dma_start(out=tile[:], in_=rows.rearrange("(p j) w -> p j w", j=PACK))
             raw[chunk] = tile
 
         def interleave(chunk):
             kind, e, s = chunk
             tile = raw.pop(chunk)
-            if kind == "w2":
-                target = groups.tile([P, PACK * N], BF16, name="grouped2", align_bytes=64)
-                flat = target[:]
+            if s == 0:
+                target = groups.tile([P, PASSES, PACK * PASS], BF16, name="grouped", align_bytes=64)
             else:
-                if s == 0:
-                    target = groups.tile([P, PASSES, PACK * PASS], BF16, name="grouped", align_bytes=64)
-                else:
-                    target = grouped[kind, e, 0]
-                flat = target[:, s, :]
+                target = grouped[kind, e, 0]
+            flat = target[:, s, :]
             grouped[chunk] = target
             source = tile[:].rearrange("p j (m i) -> p m j i", i=QUAD)
             if kind in ("w1", "w3"):
@@ -161,10 +168,11 @@ def tile_moe_tk_glu_relu_kernel(tc, xT, w1, w3, w2, gate, offs, pos1, pos2, pos3
             for s in range(PASSES):
                 packed[kind, e, s] = (words[:, s, :], scales[:, s, :])
 
-        def quantise_last_pass(kind, s, words):
+        def quantise_pass(kind, e, s):
+            words = codes.tile([P, H], U32, name="w_codes", align_bytes=64)
             scales = codes.tile([P, H], U8, name="w_scales", align_bytes=64)
-            nc.vector.quantize_mx(out=words[:].bitcast(FP8X4), scales=scales[:], in_=grouped[kind, LAST, s][:, s, :])
-            packed[kind, LAST, s] = (words, scales)
+            nc.vector.quantize_mx(out=words[:].bitcast(FP8X4), scales=scales[:], in_=grouped[kind, e, s][:, s, :])
+            packed[kind, e, s] = (words, scales)
 
         def gather(target, window, first, count):
             entries = offs_sb[:, first // LIST_ROWS : (first + count) // LIST_ROWS]
@@ -183,27 +191,28 @@ def tile_moe_tk_glu_relu_kernel(tc, xT, w1, w3, w2, gate, offs, pos1, pos2, pos3
             slot_scales[e] = placed(offset + PASSES * 4 * C, [P, C], U8, "slot_scales")[:]
             gather(slot_scales[e], x_scales, e * C, C)
 
-        def first_product(kind, e):
+        def first_product(kind, e, passes):
             for u in range(HALVES):
                 if kind == "w1":
                     planes, cols = range(PAIR * u, PAIR * (u + 1)), slice(0, C)
                 else:
                     planes, cols = range(PACK), slice(u * P, (u + 1) * P)
-                bank = psum.tile([P, len(planes), cols.stop - cols.start], F32, name="bank", tag=f"{kind}_{u}")
-                for place, t in enumerate(planes):
-                    rows = slice(t * P, (t + 1) * P)
-                    for s in range(PASSES):
-                        words, scales = packed[kind, e, s]
+                if passes[0] == 0:
+                    shape = [P, len(planes), cols.stop - cols.start]
+                    banks[kind, e, u] = psum.tile(shape, F32, name="bank", tag=f"{kind}_{u}")
+                for s in passes:
+                    words, scales = packed[kind, e, s]
+                    for place, t in enumerate(planes):
+                        rows = slice(t * P, (t + 1) * P)
                         nc.tensor.matmul_mx(
-                            out=bank[:, place, :],
+                            out=banks[kind, e, u][:, place, :],
                             lhsT=words[:, rows].bitcast(FP8X4),
                             lhsT_scale=scales[:, rows],
                             rhs=slot_words[e, s][:, cols].bitcast(FP8X4),
                             rhs_scale=slot_scales[e][SCALE_STEP * s : P, cols],
-                            start=(s == 0),
-                            stop=(s == PASSES - 1),
+                            start=(s == 0 and place == 0),
+                            stop=(s == PASSES - 1 and place == len(planes) - 1),
                         )
-                banks[kind, e, u] = bank
 
         def take_relu(e, offset):
             relu_a[e] = placed(offset, [P, HALVES, C, PAIR], F32, "relu_a")
@@ -242,18 +251,14 @@ def tile_moe_tk_glu_relu_kernel(tc, xT, w1, w3, w2, gate, offs, pos1, pos2, pos3
                 stop=True,
             )
 
-        def first_y():
-            bank = psum.tile([P, HALVES, C], F32, name="bank_y", tag="w1_0")
-            for n in range(HALVES):
-                second_product(0, n, bank[:, n, :])
-            for n in range(HALVES):
-                nc.scalar.copy(out=y_sb[n][:, 0:C], in_=bank[:, n, :])
-
-        def late_y(experts, n, tag, engine_copy=nc.scalar.copy):
+        def take_y(experts, n, tag, engine_copy):
             bank = psum.tile([P, len(experts) * C], F32, name="bank_y", tag=tag)
             for place, e in enumerate(experts):
                 second_product(e, n, bank[:, place * C : (place + 1) * C])
             engine_copy(out=y_sb[n][:, experts[0] * C : (experts[-1] + 1) * C], in_=bank[:])
+
+        def quantise_whole(e):
+            quantise_w2([(e, n) for n in range(HALVES)], grouped2[e])
 
         blocks = range(T // P)
 
@@ -271,6 +276,12 @@ def tile_moe_tk_glu_relu_kernel(tc, xT, w1, w3, w2, gate, offs, pos1, pos2, pos3
 
         def work(chunk):
             kind, e, s = chunk
+            if kind == "w2":
+                interleave_w2(e, both, on_vector)
+                quantise_whole(e)
+                for n in range(HALVES):
+                    take_y([e], n, f"y{n}", on_scalar)
+                return
             interleave(chunk)
             if kind == "x":
                 quantise_tokens(s)
@@ -282,27 +293,23 @@ def tile_moe_tk_glu_relu_kernel(tc, xT, w1, w3, w2, gate, offs, pos1, pos2, pos3
                     for other, scales in enumerate(gather_early(x_scales, U8, "early_scales")):
                         slot_scales[other] = scales
                 return
-            if kind == "w2":
-                quantise_w2([(e, n) for n in range(HALVES)], grouped[chunk][:])
-                return
-            if e == LAST and (kind, s) != ("w3", 0):
-                quantise_last_pass(kind, s, codes.tile([P, H], U32, name="w_codes", align_bytes=64))
             if (kind, s) == ("w1", 0) and e > 0:
                 take_h(e - 1, start_of(chunk))
                 quantise_h(e - 1)
+            if e == LAST or (kind, e) == ("w3", LAST - 1):
+                quantise_pass(kind, e, s)
+                if (kind, s) == ("w3", 1):
+                    take_relu(e, start_of(chunk))
+                first_product(kind, e, [s])
+                return
             if s == 0:
                 return
-            if e < LAST:
-                quantise_matrix(kind, e)
-            elif kind == "w1":
-                quantise_last_pass("w3", 0, placed(start_of(chunk), [P, H], U32, "w_codes"))
-            if kind == "w3" and e < LAST:
+            quantise_matrix(kind, e)
+            if kind == "w3":
                 if chunk in held:
                     gather_late(e + EARLY, start_of(chunk) + BUFFER // 2)
                 take_relu(e, start_of(chunk))
-                if e == 2:
-                    first_y()
-            first_product(kind, e)
+            first_product(kind, e, range(PASSES))
 
         for step in range(-AHEAD, len(chunks)):
             if step + AHEAD < len(chunks):
@@ -314,125 +321,88 @@ def tile_moe_tk_glu_relu_kernel(tc, xT, w1, w3, w2, gate, offs, pos1, pos2, pos3
             if step >= 0:
                 work(chunks[step])
 
-        relu_place, other_place, fetch_place = [(len(in_turn) + turn) % ROTATING * BUFFER for turn in range(3)]
-        h_place = relu_place + 2 * HALF_BYTES
+        places = [(len(in_turn) + turn) % ROTATING * BUFFER for turn in range(3)]
+        for e in range(AMID, LAST):
+            place = places[(e - AMID) // 2] + (e - AMID) % 2 * BUFFER // 2
+            load_w2(e, placed(place, [P, PACK, N], F32, "raw2")[:])
+            nc.sync.dma_start(pos_sb[e - AMID][:], (pos1, pos2, pos3)[e - AMID])
+        load_w2(LAST, y_sb[1][:, AMID * C :].rearrange("p (j w) -> p j w", j=PACK))
 
-        def in_y(first_expert):
-            return y_sb[0][:, first_expert * C : (first_expert + 2) * C].rearrange("p (j w) -> p j w", j=PACK)
-
-        halves = {}
-        halves[1, 0] = placed(relu_place, [P, PACK, P], F32, "raw_half")[:]
-        two_halves = placed(h_place, [P, 2, PACK, P], F32, "raw_halves")
-        halves[2, 0] = two_halves[:, 0]
-        halves[3, 0] = two_halves[:, 1]
-        halves[4, 0] = placed(other_place + 3 * HALF_BYTES, [P, PACK, P], F32, "raw_half")[:]
-        halves[5, 0] = in_y(1)
-        halves[1, 1] = in_y(3)
-        for e in (2, 3, 4):
-            halves[e, 1] = placed(other_place + (e - 2) * HALF_BYTES, [P, PACK, P], F32, "raw_half")[:]
-        halves[5, 1] = placed(fetch_place + HALF_BYTES // 2, [P, PACK, P], F32, "raw_half")[:]
-        for n in range(HALVES):
-            for e in range(1, E):
-                rows = w2[e][:, n * P : (n + 1) * P]
-                nc.sync.dma_start(out=halves[e, n], in_=rows.rearrange("(p j) w -> p j w", j=PACK))
-            if n == 0:
-                nc.sync.dma_start(pos_sb[0][:], pos1)
-        nc.sync.dma_start(pos_sb[1][:], pos2)
-        nc.sync.dma_start(pos_sb[2][:], pos3)
-
-        firsts = keep.tile([P, LAST, HALF_WIDTH], BF16, name="firsts", align_bytes=64)
-        staging = start_of(held[0])
-        seconds = [placed(staging + pair * HALF_BYTES, [P, 2, HALF_WIDTH], BF16, "seconds") for pair in range(2)]
-        last_second = placed(staging + 2 * HALF_BYTES, [P, HALF_WIDTH], BF16, "last_second")
-
-        def interleave_half(e, n, target):
-            source = halves[e, n].rearrange("p j (m i) -> p m j i", i=QUAD)
-            nc.scalar.copy(out=target.rearrange("p (m i j) -> p m j i", i=QUAD, j=PACK), in_=source)
-
-        def quantise_firsts(experts):
-            source = firsts[:, experts[0] - 1 : experts[-1], :].rearrange("p e w -> p (e w)")
-            quantise_w2([(e, 0) for e in experts], source)
-
-        interleave_half(1, 0, firsts[:, 0, :])
-        take_relu(LAST, relu_place)
-        nc.vector.tensor_copy(
-            out=firsts[:, 1:3, :].rearrange("p e (m i j) -> p e m j i", i=QUAD, j=PACK),
-            in_=two_halves[:].rearrange("p e j (m i) -> p e m j i", i=QUAD),
-        )
-        quantise_firsts([1])
-        quantise_firsts([2, 3])
-        take_h(LAST, h_place)
-        interleave_half(4, 0, firsts[:, 3, :])
-        interleave_half(5, 0, firsts[:, 4, :])
-        quantise_firsts([4, 5])
+        interleave_w2(2, both, on_vector)
+        take_h(LAST, places[-1])
+        interleave_w2(3, both, on_scalar)
+        quantise_whole(2)
+        quantise_whole(3)
         quantise_h(LAST)
-        late_y([1, 2], 0, "y0", nc.vector.tensor_copy)
-        interleave_half(1, 1, seconds[0][:, 0, :])
-        late_y([3, 4], 0, "y1")
-        late_y([5], 0, "y2", nc.vector.tensor_copy)
+        interleave_w2(4, both, on_scalar)
+        quantise_whole(4)
+        interleave_w2(LAST, both, on_scalar)
+        quantise_whole(LAST)
+        take_y([2, 3], 1, "y1", on_scalar)
+        take_y([2, 3], 0, "y0", on_vector)
+        take_y([4, 5], 1, "y3", on_scalar)
+        take_y([4, 5], 0, "y2", on_vector)
 
-        interleave_half(2, 1, seconds[0][:, 1, :])
-        quantise_w2([(1, 1), (2, 1)], seconds[0][:].rearrange("p e w -> p (e w)"))
-        interleave_half(3, 1, seconds[1][:, 0, :])
-        interleave_half(4, 1, seconds[1][:, 1, :])
-        quantise_w2([(3, 1), (4, 1)], seconds[1][:].rearrange("p e w -> p (e w)"))
-        interleave_half(5, 1, last_second[:])
-        late_y([1, 2], 1, "y3")
-        quantise_w2([(5, 1)], last_second[:])
-        late_y([3, 4], 1, "y0")
-        late_y([5], 1, "y2")
 
-        def fetch(n, r, cols, part):
-            entries = pos_sb[r][:, cols.start // LIST_ROWS : cols.stop // LIST_ROWS]
-            nc.vector.tensor_tensor(part[:], y_sb[n][:].indirect(entries), gate_sb[r][:, cols], MULT)
-            return [part[:, start : start + P] for start in range(0, cols.stop - cols.start, P)]
+        def entries(r, cols):
+            return pos_sb[r][:, cols.start // LIST_ROWS : cols.stop // LIST_ROWS]
 
-        def new_part(n, r, cols):
-            return keep.tile([P, cols.stop - cols.start], F32, name=f"part{n}_{r}_{cols.start}")
+        def new_part(name, cols):
+            return keep.tile([P, cols.stop - cols.start], F32, name=f"{name}_{cols.start}")
 
-        free_banks = [f"{kind}_{u}" for kind in ("w1", "w3") for u in range(HALVES)]
+        def in_blocks(part):
+            return [part[:, start : start + P] for start in range(0, part[:].shape[1], P)]
 
-        def sum_in_psum(n, parts, targets):
-            turned = [psum.tile([P, P], F32, name="turned", tag=free_banks[block]) for block in blocks]
-            for r, part in enumerate(parts):
-                for block in blocks:
-                    nc.tensor.matmul(
-                        turned[block][:],
-                        lhsT=part[block],
-                        rhs=identity[:],
-                        is_transpose=True,
-                        start=(r == 0),
-                        stop=(r == len(parts) - 1),
-                    )
-            for block in blocks:
-                turned_sb = keep.tile([P, P], F32, name=f"turned_sb{n}_{block}")
-                nc.scalar.copy(out=turned_sb[:], in_=turned[block][:])
-                nc.tensor.transpose(targets[block], turned_sb[:], identity[:])
+        def fetch(n, r, cols):
+            part = new_part(f"part{n}_{r}", cols)
+            nc.vector.tensor_tensor(part[:], y_sb[n][:].indirect(entries(r, cols)), gate_sb[r][:, cols], MULT)
+            return part
+
+        def fetch_plain(n, r, cols):
+            part = new_part(f"part{n}_{r}", cols)
+            nc.scalar.activation(part[:], y_sb[n][:].indirect(entries(r, cols)), COPY)
+            return part
+
+        def add_turned(target, source, first, last):
+            nc.tensor.matmul(target, lhsT=source, rhs=identity[:], is_transpose=True, start=first, stop=last)
 
         tokens = slice(0, T)
-        parts = [
-            fetch(0, 0, tokens, new_part(0, 0, tokens)),
-            fetch(0, 1, tokens, placed(fetch_place + HALF_BYTES, [P, T], F32, "second_part")),
-            fetch(0, 2, tokens, placed(fetch_place, [P, T], F32, "third_part")),
-        ]
-        upright = psum.tile([P, T // P, P], F32, name="upright", tag="y1")
-        sum_in_psum(0, parts, [upright[:, block, :] for block in blocks])
-        result = keep.tile([P, T], F32, name="result0")
-        nc.scalar.copy(out=result[:], in_=upright[:].rearrange("p b t -> p (b t)"))
-        nc.sync.dma_start(out=out[0:P, :], in_=result[:])
-
-        pieces = [slice(0, 2 * P), slice(2 * P, 3 * P), slice(3 * P, T)]
-        parts = [
-            fetch(1, 0, tokens, new_part(1, 0, tokens)),
-            [block for cols in pieces for block in fetch(1, 1, cols, new_part(1, 1, cols))],
-        ]
-        sums = [psum.tile([P, T // 2], F32, name="sum_of_two", tag=tag) for tag in ("y0", "y2")]
-        sum_in_psum(1, parts, [sums[block // 2][:, block % 2 * P : (block % 2 + 1) * P] for block in blocks])
         token_halves = [slice(q * T // 2, (q + 1) * T // 2) for q in range(2)]
-        thirds = [new_part(1, 2, cols) for cols in token_halves]
-        for cols, third in zip(token_halves, thirds):
-            fetch(1, 2, cols, third)
-        for cols, sum_of_two, third in zip(token_halves, sums, thirds):
-            result = keep.tile([P, T // 2], F32, name=f"result1_{cols.start}")
-            nc.vector.tensor_tensor(result[:], sum_of_two[:], third[:], ADD)
+
+        turned_plain = []
+        turned_sums = [psum.tile([P, P], F32, name="turned", tag=tag) for tag in ("y2", "y3", "w1_0", "w1_1")]
+        for r in range(TOP - 1):
+            plain = in_blocks(fetch_plain(1, r, tokens))
+            bank = psum.tile([P, T // P, P], F32, name="turned_plain", tag=f"y{r}")
+            for block in blocks:
+                nc.tensor.transpose(bank[:, block, :], plain[block], identity[:])
+            turned_plain.append(bank)
+            part = in_blocks(fetch(0, r, tokens))
+            for block in blocks:
+                add_turned(turned_sums[block][:], part[block], r == 0, False)
+        part = [block for cols in token_halves for block in in_blocks(fetch(0, TOP - 1, cols))]
+        scaled = [keep.tile([P, T // P, P], F32, name=f"scaled{r}") for r in range(TOP - 1)]
+        for r in range(TOP - 1):
+            for block in blocks:
+                nc.scalar.activation(
+                    scaled[r][:, block, :], turned_plain[r][:, block, :], COPY, scale=gate_columns[:, block, r : r + 1]
+                )
+        for block in blocks:
+            add_turned(turned_sums[block][:], part[block], False, True)
+        thirds = [fetch(1, TOP - 1, cols) for cols in token_halves]
+        sums = [psum.tile([P, 2, P], F32, name="sum_of_two", tag=tag) for tag in ("w3_0", "w3_1")]
+        for block in blocks:
+            for r in range(TOP - 1):
+                add_turned(sums[block // 2][:, block % 2, :], scaled[r][:, block, :], r == 0, r == TOP - 2)
+        upright = [psum.tile([P, 2, P], F32, name="upright", tag=tag) for tag in ("y0", "y1")]
+        for block in blocks:
+            turned_sb = keep.tile([P, P], F32, name=f"turned_sb{block}")
+            nc.scalar.copy(out=turned_sb[:], in_=turned_sums[block][:])
+            nc.tensor.transpose(upright[block // 2][:, block % 2, :], turned_sb[:], identity[:])
+        for q, cols in enumerate(token_halves):
+            result = new_part("result0", cols)
+            nc.scalar.copy(out=result[:], in_=upright[q][:].rearrange("p b t -> p (b t)"))
+            nc.sync.dma_start(out=out[0:P, cols], in_=result[:])
+            result = new_part("result1", cols)
+            nc.vector.tensor_tensor(result[:], sums[q][:].rearrange("p b t -> p (b t)"), thirds[q][:], ADD)
             nc.sync.dma_start(out=out[P : 2 * P, cols], in_=result[:])

@@ -336,13 +336,16 @@ def tile_moe_tk_glu_relu_kernel(tc, xT, w1, w3, w2, gate, offs, pos1, pos2, pos3
         quantise_h(LAST)
         interleave_w2(4, both, on_scalar)
         quantise_whole(4)
-        interleave_w2(LAST, both, on_scalar)
-        quantise_whole(LAST)
+        interleave_w2(LAST, first, on_scalar)
+        interleave_w2(LAST, second, on_vector)
+        for n in range(HALVES):
+            quantise_w2([(LAST, n)], grouped2[LAST][:, n * PACK * P : (n + 1) * PACK * P])
         take_y([2, 3], 1, "y1", on_scalar)
         take_y([2, 3], 0, "y0", on_vector)
-        take_y([4, 5], 1, "y3", on_scalar)
-        take_y([4, 5], 0, "y2", on_vector)
-
+        take_y([4], 0, "y2", on_scalar)
+        take_y([4], 1, "y3", on_scalar)
+        take_y([LAST], 0, "w1_0", on_vector)
+        take_y([LAST], 1, "w1_1", on_scalar)
 
         def entries(r, cols):
             return pos_sb[r][:, cols.start // LIST_ROWS : cols.stop // LIST_ROWS]
@@ -366,43 +369,49 @@ def tile_moe_tk_glu_relu_kernel(tc, xT, w1, w3, w2, gate, offs, pos1, pos2, pos3
         def add_turned(target, source, first, last):
             nc.tensor.matmul(target, lhsT=source, rhs=identity[:], is_transpose=True, start=first, stop=last)
 
-        tokens = slice(0, T)
         token_halves = [slice(q * T // 2, (q + 1) * T // 2) for q in range(2)]
 
-        turned_plain = []
-        turned_sums = [psum.tile([P, P], F32, name="turned", tag=tag) for tag in ("y2", "y3", "w1_0", "w1_1")]
-        for r in range(TOP - 1):
-            plain = in_blocks(fetch_plain(1, r, tokens))
-            bank = psum.tile([P, T // P, P], F32, name="turned_plain", tag=f"y{r}")
-            for block in blocks:
-                nc.tensor.transpose(bank[:, block, :], plain[block], identity[:])
-            turned_plain.append(bank)
-            part = in_blocks(fetch(0, r, tokens))
-            for block in blocks:
-                add_turned(turned_sums[block][:], part[block], r == 0, False)
-        part = [block for cols in token_halves for block in in_blocks(fetch(0, TOP - 1, cols))]
-        scaled = [keep.tile([P, T // P, P], F32, name=f"scaled{r}") for r in range(TOP - 1)]
-        for r in range(TOP - 1):
-            for block in blocks:
-                nc.scalar.activation(
-                    scaled[r][:, block, :], turned_plain[r][:, block, :], COPY, scale=gate_columns[:, block, r : r + 1]
-                )
-        for block in blocks:
-            add_turned(turned_sums[block][:], part[block], False, True)
-        thirds = [fetch(1, TOP - 1, cols) for cols in token_halves]
-        sums = [psum.tile([P, 2, P], F32, name="sum_of_two", tag=tag) for tag in ("w3_0", "w3_1")]
-        for block in blocks:
-            for r in range(TOP - 1):
-                add_turned(sums[block // 2][:, block % 2, :], scaled[r][:, block, :], r == 0, r == TOP - 2)
-        upright = [psum.tile([P, 2, P], F32, name="upright", tag=tag) for tag in ("y0", "y1")]
-        for block in blocks:
-            turned_sb = keep.tile([P, P], F32, name=f"turned_sb{block}")
-            nc.scalar.copy(out=turned_sb[:], in_=turned_sums[block][:])
-            nc.tensor.transpose(upright[block // 2][:, block % 2, :], turned_sb[:], identity[:])
+        pair = range(2)
+
+        turned_plain, turned_sums = {}, {}
         for q, cols in enumerate(token_halves):
-            result = new_part("result0", cols)
-            nc.scalar.copy(out=result[:], in_=upright[q][:].rearrange("p b t -> p (b t)"))
-            nc.sync.dma_start(out=out[0:P, cols], in_=result[:])
-            result = new_part("result1", cols)
-            nc.vector.tensor_tensor(result[:], sums[q][:].rearrange("p b t -> p (b t)"), thirds[q][:], ADD)
-            nc.sync.dma_start(out=out[P : 2 * P, cols], in_=result[:])
+            turned_plain[q] = psum.tile([P, 2, 2, P], F32, name="turned_plain", tag=f"y{q}")
+            turned_sums[q] = psum.tile([P, 2, P], F32, name="turned", tag=f"y{2 + q}")
+            for r in pair:
+                plain = in_blocks(fetch_plain(1, r, cols))
+                part = in_blocks(fetch(0, r, cols))
+                for place in pair:
+                    nc.tensor.transpose(turned_plain[q][:, r, place, :], plain[place], identity[:])
+                for place in pair:
+                    add_turned(turned_sums[q][:, place, :], part[place], (r, place) == (0, 0), (q, r, place) == (1, 1, 1))
+            if q == 0:
+                part = in_blocks(fetch(0, TOP - 1, cols))
+                for place in pair:
+                    add_turned(turned_sums[q][:, place, :], part[place], False, place == 1)
+        thirds = {(n, q): fetch(n, TOP - 1, token_halves[q]) for n, q in ((1, 0), (1, 1), (0, 1))}
+        sums = {}
+        for q in pair:
+            scaled = keep.tile([P, 2, 2, P], F32, name=f"scaled{q}")
+            for r in pair:
+                for place in pair:
+                    gates = gate_columns[:, 2 * q + place, r : r + 1]
+                    nc.scalar.activation(scaled[:, r, place, :], turned_plain[q][:, r, place, :], COPY, scale=gates)
+            turned_sb = keep.tile([P, 2, P], F32, name=f"turned_sb{q}")
+            nc.scalar.copy(out=turned_sb[:], in_=turned_sums[q][:])
+            sums[1, q] = psum.tile([P, 2, P], F32, name="sum_of_two", tag=f"w1_{q}")
+            sums[0, q] = psum.tile([P, 2, P], F32, name="sum_of_two", tag=f"w3_{q}")
+            for place in pair:
+                for r in pair:
+                    add_turned(sums[1, q][:, place, :], scaled[:, r, place, :], r == 0, r == 1)
+            for place in pair:
+                nc.tensor.transpose(sums[0, q][:, place, :], turned_sb[:, place, :], identity[:])
+
+        for n, q in ((0, 0), (1, 0), (1, 1), (0, 1)):
+            cols = token_halves[q]
+            result = new_part(f"result{n}", cols)
+            upright = sums[n, q][:].rearrange("p b t -> p (b t)")
+            if (n, q) in thirds:
+                nc.vector.tensor_tensor(result[:], upright, thirds[n, q][:], ADD)
+            else:
+                nc.scalar.copy(out=result[:], in_=upright)
+            nc.sync.dma_start(out=out[n * P : (n + 1) * P, cols], in_=result[:])

@@ -102,7 +102,7 @@ def tile_moe_tk_glu_relu_kernel(tc, xT, w1, w3, w2, gate, offs, pos1, pos2, pos3
         raw2 = {}
         grouped2 = [keep.tile([P, PACK * N], BF16, name=f"grouped2_{e}", align_bytes=64)[:] for e in range(LAST)]
         grouped2.append(y_sb[0][:, AMID * C : (AMID + 2) * C].bitcast(BF16))
-        both, first, second = slice(0, HALVES), slice(0, 1), slice(1, 2)
+        both = slice(0, HALVES)
         on_vector, on_scalar = nc.vector.tensor_copy, nc.scalar.copy
 
         def load_w2(e, target):
@@ -325,8 +325,9 @@ def tile_moe_tk_glu_relu_kernel(tc, xT, w1, w3, w2, gate, offs, pos1, pos2, pos3
         for e in range(AMID, LAST):
             place = places[(e - AMID) // 2] + (e - AMID) % 2 * BUFFER // 2
             load_w2(e, placed(place, [P, PACK, N], F32, "raw2")[:])
-            nc.sync.dma_start(pos_sb[e - AMID][:], (pos1, pos2, pos3)[e - AMID])
         load_w2(LAST, y_sb[1][:, AMID * C :].rearrange("p (j w) -> p j w", j=PACK))
+        for r, pos in enumerate((pos1, pos2, pos3)):
+            nc.sync.dma_start(pos_sb[r][:], pos)
 
         interleave_w2(2, both, on_vector)
         take_h(LAST, places[-1])
@@ -336,16 +337,12 @@ def tile_moe_tk_glu_relu_kernel(tc, xT, w1, w3, w2, gate, offs, pos1, pos2, pos3
         quantise_h(LAST)
         interleave_w2(4, both, on_scalar)
         quantise_whole(4)
-        interleave_w2(LAST, first, on_scalar)
-        interleave_w2(LAST, second, on_vector)
-        for n in range(HALVES):
-            quantise_w2([(LAST, n)], grouped2[LAST][:, n * PACK * P : (n + 1) * PACK * P])
+        interleave_w2(LAST, both, on_scalar)
+        quantise_whole(LAST)
         take_y([2, 3], 1, "y1", on_scalar)
         take_y([2, 3], 0, "y0", on_vector)
-        take_y([4], 0, "y2", on_scalar)
-        take_y([4], 1, "y3", on_scalar)
-        take_y([LAST], 0, "w1_0", on_vector)
-        take_y([LAST], 1, "w1_1", on_scalar)
+        take_y([4, 5], 1, "y3", on_scalar)
+        take_y([4, 5], 0, "y2", on_vector)
 
         def entries(r, cols):
             return pos_sb[r][:, cols.start // LIST_ROWS : cols.stop // LIST_ROWS]

@@ -40,7 +40,7 @@ EARLY_ENTRIES = 384
 X_QUADS = 84
 W_QUADS = 96
 BEFORE_LAST_QUADS = 64
-LAST_QUADS = {("w1", 0): W_QUADS, ("w1", 1): 24, ("w3", 0): 92, ("w3", 1): 86}
+LAST_QUADS = {("w1", 0): W_QUADS, ("w1", 1): 24, ("w3", 0): 60, ("w3", 1): 86}
 
 
 def chunk_order():
@@ -366,49 +366,71 @@ def tile_moe_tk_glu_relu_kernel(tc, xT, w1, w3, w2, gate, offs, pos1, pos2, pos3
         def add_turned(target, source, first, last):
             nc.tensor.matmul(target, lhsT=source, rhs=identity[:], is_transpose=True, start=first, stop=last)
 
-        token_halves = [slice(q * T // 2, (q + 1) * T // 2) for q in range(2)]
+        def tokens(first, last):
+            return slice(first * P, last * P)
 
         pair = range(2)
+        halves = [tokens(0, 2), tokens(2, 4)]
 
-        turned_plain, turned_sums = {}, {}
-        for q, cols in enumerate(token_halves):
-            turned_plain[q] = psum.tile([P, 2, 2, P], F32, name="turned_plain", tag=f"y{q}")
-            turned_sums[q] = psum.tile([P, 2, P], F32, name="turned", tag=f"y{2 + q}")
-            for r in pair:
-                plain = in_blocks(fetch_plain(1, r, cols))
-                part = in_blocks(fetch(0, r, cols))
-                for place in pair:
-                    nc.tensor.transpose(turned_plain[q][:, r, place, :], plain[place], identity[:])
-                for place in pair:
-                    add_turned(turned_sums[q][:, place, :], part[place], (r, place) == (0, 0), (q, r, place) == (1, 1, 1))
-            if q == 0:
-                part = in_blocks(fetch(0, TOP - 1, cols))
-                for place in pair:
-                    add_turned(turned_sums[q][:, place, :], part[place], False, place == 1)
-        thirds = {(n, q): fetch(n, TOP - 1, token_halves[q]) for n, q in ((1, 0), (1, 1), (0, 1))}
-        sums = {}
-        for q in pair:
-            scaled = keep.tile([P, 2, 2, P], F32, name=f"scaled{q}")
-            for r in pair:
-                for place in pair:
-                    gates = gate_columns[:, 2 * q + place, r : r + 1]
-                    nc.scalar.activation(scaled[:, r, place, :], turned_plain[q][:, r, place, :], COPY, scale=gates)
-            turned_sb = keep.tile([P, 2, P], F32, name=f"turned_sb{q}")
-            nc.scalar.copy(out=turned_sb[:], in_=turned_sums[q][:])
-            sums[1, q] = psum.tile([P, 2, P], F32, name="sum_of_two", tag=f"w1_{q}")
-            sums[0, q] = psum.tile([P, 2, P], F32, name="sum_of_two", tag=f"w3_{q}")
-            for place in pair:
+        def turn_plain(n, r, cols, targets):
+            for target, block in zip(targets, in_blocks(fetch_plain(n, r, cols))):
+                nc.tensor.transpose(target, block, identity[:])
+
+        turned = [psum.tile([P, 2, 2, P], F32, name="turned", tag=f"y{q}") for q in pair]
+        upper = psum.tile([P, 2, P], F32, name="upper", tag="y3")
+        turned_sum = psum.tile([P, P], F32, name="turned_sum", tag="y2")
+        gated = []
+        for r in pair:
+            turn_plain(1, r, halves[0], [turned[0][:, r, place, :] for place in pair])
+            gated.append(fetch(0, r, tokens(1, 4)))
+            add_turned(turned_sum[:], gated[r][:, 0:P], r == 0, False)
+        third_above = fetch(0, TOP - 1, tokens(0, 4))
+        add_turned(turned_sum[:], third_above[:, tokens(1, 2)], False, True)
+        for r in pair:
+            turn_plain(1, r, halves[1], [turned[1][:, r, place, :] for place in pair])
+        for r in pair:
+            turn_plain(0, r, tokens(0, 1), [upper[:, r, :]])
+
+        def store(n, cols, result):
+            nc.sync.dma_start(out=out[n * P : (n + 1) * P, cols], in_=result)
+
+        two = new_part("two", halves[1])
+        nc.vector.tensor_tensor(two[:], gated[0][:, P:], gated[1][:, P:], ADD)
+        thirds = [fetch(1, TOP - 1, halves[0])]
+        added = new_part("added", halves[1])
+        nc.vector.tensor_tensor(added[:], two[:], third_above[:, halves[1]], ADD)
+        store(0, halves[1], added[:])
+        thirds.append(fetch(1, TOP - 1, halves[1]))
+
+        def scale_and_turn_back(name, sources, first_block, tag):
+            places = range(len(sources[0]))
+            scaled = keep.tile([P, 2, len(places), P], F32, name=name)
+            for place in places:
                 for r in pair:
-                    add_turned(sums[1, q][:, place, :], scaled[:, r, place, :], r == 0, r == 1)
-            for place in pair:
-                nc.tensor.transpose(sums[0, q][:, place, :], turned_sb[:, place, :], identity[:])
+                    gates = gate_columns[:, first_block + place, r : r + 1]
+                    nc.scalar.activation(scaled[:, r, place, :], sources[r][place], COPY, scale=gates)
+            bank = psum.tile([P, len(places), P], F32, name="sum_of_two", tag=tag)
+            for place in places:
+                for r in pair:
+                    add_turned(bank[:, place, :], scaled[:, r, place, :], r == 0, r == 1)
+            return bank[:].rearrange("p b t -> p (b t)")
 
-        for n, q in ((0, 0), (1, 0), (1, 1), (0, 1)):
-            cols = token_halves[q]
-            result = new_part(f"result{n}", cols)
-            upright = sums[n, q][:].rearrange("p b t -> p (b t)")
-            if (n, q) in thirds:
-                nc.vector.tensor_tensor(result[:], upright, thirds[n, q][:], ADD)
-            else:
-                nc.scalar.copy(out=result[:], in_=upright)
-            nc.sync.dma_start(out=out[n * P : (n + 1) * P, cols], in_=result[:])
+        below = [[[turned[q][:, r, place, :] for place in pair] for r in pair] for q in pair]
+        first_below = scale_and_turn_back("scaled0", below[0], 0, "w1_0")
+        second_below = scale_and_turn_back("scaled1", below[1], 2, "w1_1")
+        above = scale_and_turn_back("scaled_above", [[upper[:, r, :]] for r in pair], 0, "w3_0")
+        turned_sb = keep.tile([P, P], F32, name="turned_sb")
+        nc.scalar.copy(out=turned_sb[:], in_=turned_sum[:])
+        upright = psum.tile([P, P], F32, name="upright", tag="w3_1")
+        nc.tensor.transpose(upright[:], turned_sb[:], identity[:])
+
+        result = new_part("result1", halves[0])
+        nc.vector.tensor_tensor(result[:], first_below, thirds[0][:], ADD)
+        store(1, halves[0], result[:])
+        result = new_part("result1", halves[1])
+        nc.vector.tensor_tensor(result[:], second_below, thirds[1][:], ADD)
+        store(1, halves[1], result[:])
+        result = new_part("result0", halves[0])
+        nc.vector.tensor_tensor(result[:, 0:P], above, third_above[:, 0:P], ADD)
+        nc.scalar.copy(out=result[:, P:], in_=upright[:])
+        store(0, halves[0], result[:])

@@ -34,13 +34,14 @@ BUFFER = PACK * PASS * 4
 ROTATING = 9
 AHEAD = ROTATING - 3
 EARLY = 3
-AMID = 2
 EARLY_ENTRIES = 384
+AMID = 2
 
 X_QUADS = 84
 W_QUADS = 96
 BEFORE_LAST_QUADS = 64
 LAST_QUADS = {("w1", 0): W_QUADS, ("w1", 1): 24, ("w3", 0): 60, ("w3", 1): 86}
+LAST_W2_QUADS = 26
 
 
 def chunk_order():
@@ -102,17 +103,17 @@ def tile_moe_tk_glu_relu_kernel(tc, xT, w1, w3, w2, gate, offs, pos1, pos2, pos3
         raw2 = {}
         grouped2 = [keep.tile([P, PACK * N], BF16, name=f"grouped2_{e}", align_bytes=64)[:] for e in range(LAST)]
         grouped2.append(y_sb[0][:, AMID * C : (AMID + 2) * C].bitcast(BF16))
-        both = slice(0, HALVES)
+        whole = slice(0, N // QUAD)
         on_vector, on_scalar = nc.vector.tensor_copy, nc.scalar.copy
 
         def load_w2(e, target):
             nc.sync.dma_start(out=target, in_=w2[e].rearrange("(p j) w -> p j w", j=PACK))
             raw2[e] = target
 
-        def interleave_w2(e, halves, engine_copy):
-            source = raw2[e][:, :, halves.start * P : halves.stop * P].rearrange("p j (m i) -> p m j i", i=QUAD)
-            target = grouped2[e][:, halves.start * PACK * P : halves.stop * PACK * P]
-            engine_copy(out=target.rearrange("p (m i j) -> p m j i", i=QUAD, j=PACK), in_=source)
+        def interleave_w2(e, quads, engine_copy):
+            source = raw2[e].rearrange("p j (m i) -> p m j i", i=QUAD)
+            target = grouped2[e].rearrange("p (m i j) -> p m j i", i=QUAD, j=PACK)
+            engine_copy(out=target[:, quads], in_=source[:, quads])
 
         def load(chunk):
             kind, e, s = chunk
@@ -143,13 +144,12 @@ def tile_moe_tk_glu_relu_kernel(tc, xT, w1, w3, w2, gate, offs, pos1, pos2, pos3
                 nc.vector.tensor_copy(out=flat[:, :cut], in_=source[:, :cut])
             nc.scalar.copy(out=flat[:, cut:], in_=source[:, cut:])
 
-        def quantise_w2(parts, source):
-            name = "%d_%d" % parts[0]
-            words = keep.tile([P, len(parts) * P], U32, name="w2_codes" + name, align_bytes=64)
-            scales = keep.tile([P, len(parts) * P], U8, name="w2_scales" + name, align_bytes=64)
-            nc.vector.quantize_mx(out=words[:].bitcast(FP8X4), scales=scales[:], in_=source)
-            for place, (e, n) in enumerate(parts):
-                cols = slice(place * P, (place + 1) * P)
+        def quantise_w2(e):
+            words = keep.tile([P, N], U32, name=f"w2_codes{e}", align_bytes=64)
+            scales = keep.tile([P, N], U8, name=f"w2_scales{e}", align_bytes=64)
+            nc.vector.quantize_mx(out=words[:].bitcast(FP8X4), scales=scales[:], in_=grouped2[e])
+            for n in range(HALVES):
+                cols = slice(n * P, (n + 1) * P)
                 packed["w2", e, n] = (words[:, cols], scales[:, cols])
 
         def quantise_tokens(s):
@@ -257,9 +257,6 @@ def tile_moe_tk_glu_relu_kernel(tc, xT, w1, w3, w2, gate, offs, pos1, pos2, pos3
                 second_product(e, n, bank[:, place * C : (place + 1) * C])
             engine_copy(out=y_sb[n][:, experts[0] * C : (experts[-1] + 1) * C], in_=bank[:])
 
-        def quantise_whole(e):
-            quantise_w2([(e, n) for n in range(HALVES)], grouped2[e])
-
         blocks = range(T // P)
 
         def spread_gates():
@@ -268,17 +265,18 @@ def tile_moe_tk_glu_relu_kernel(tc, xT, w1, w3, w2, gate, offs, pos1, pos2, pos3
                 nc.tensor.transpose(bank[:, block, :], gate_rows[:, block * P : (block + 1) * P], identity[:])
             nc.scalar.copy(out=gate_columns[:], in_=bank[:, :, 0:TOP])
             for r in range(TOP):
+                first = 0 if r == TOP - 1 else 1
                 bank = psum.tile([P, T // P, P], F32, name="gate_bank", tag=f"y{r}")
-                for block in blocks:
+                for block in blocks[first:]:
                     column = gate_columns[:, block, r : r + 1].to_broadcast([P, P])
                     nc.tensor.transpose(bank[:, block, :], column, identity[:])
-                nc.scalar.copy(out=gate_sb[r][:], in_=bank[:].rearrange("q b p -> q (b p)"))
+                nc.scalar.copy(out=gate_sb[r][:, first * P :], in_=bank[:, first:, :].rearrange("q b p -> q (b p)"))
 
         def work(chunk):
             kind, e, s = chunk
             if kind == "w2":
-                interleave_w2(e, both, on_vector)
-                quantise_whole(e)
+                interleave_w2(e, whole, on_vector)
+                quantise_w2(e)
                 for n in range(HALVES):
                     take_y([e], n, f"y{n}", on_scalar)
                 return
@@ -321,28 +319,34 @@ def tile_moe_tk_glu_relu_kernel(tc, xT, w1, w3, w2, gate, offs, pos1, pos2, pos3
             if step >= 0:
                 work(chunks[step])
 
-        places = [(len(in_turn) + turn) % ROTATING * BUFFER for turn in range(3)]
+        next_buffers = [(len(in_turn) + turn) % ROTATING * BUFFER for turn in range(3)]
         for e in range(AMID, LAST):
-            place = places[(e - AMID) // 2] + (e - AMID) % 2 * BUFFER // 2
-            load_w2(e, placed(place, [P, PACK, N], F32, "raw2")[:])
+            offset = next_buffers[(e - AMID) // 2] + (e - AMID) % 2 * BUFFER // 2
+            load_w2(e, placed(offset, [P, PACK, N], F32, "raw2")[:])
         load_w2(LAST, y_sb[1][:, AMID * C :].rearrange("p (j w) -> p j w", j=PACK))
         for r, pos in enumerate((pos1, pos2, pos3)):
             nc.sync.dma_start(pos_sb[r][:], pos)
 
-        interleave_w2(2, both, on_vector)
-        take_h(LAST, places[-1])
-        interleave_w2(3, both, on_scalar)
-        quantise_whole(2)
-        quantise_whole(3)
+        interleave_w2(2, whole, on_vector)
+        take_h(LAST, next_buffers[-1])
+        interleave_w2(3, whole, on_scalar)
+        quantise_w2(2)
+        quantise_w2(3)
         quantise_h(LAST)
-        interleave_w2(4, both, on_scalar)
-        quantise_whole(4)
-        interleave_w2(LAST, both, on_scalar)
-        quantise_whole(LAST)
+        interleave_w2(4, whole, on_scalar)
+        quantise_w2(4)
+        interleave_w2(LAST, slice(0, LAST_W2_QUADS), on_vector)
+        interleave_w2(LAST, slice(LAST_W2_QUADS, N // QUAD), on_scalar)
+        quantise_w2(LAST)
         take_y([2, 3], 1, "y1", on_scalar)
         take_y([2, 3], 0, "y0", on_vector)
-        take_y([4, 5], 1, "y3", on_scalar)
-        take_y([4, 5], 0, "y2", on_vector)
+        bank = psum.tile([P, HALVES, C], F32, name="bank_y", tag="y2")
+        for n in range(HALVES):
+            second_product(LAST - 1, n, bank[:, n, :])
+        for n, engine_copy in ((1, on_scalar), (0, on_vector)):
+            engine_copy(out=y_sb[n][:, (LAST - 1) * C : LAST * C], in_=bank[:, n, :])
+        take_y([LAST], 1, "y3", on_scalar)
+        take_y([LAST], 0, "y1", on_vector)
 
         def entries(r, cols):
             return pos_sb[r][:, cols.start // LIST_ROWS : cols.stop // LIST_ROWS]
@@ -370,7 +374,7 @@ def tile_moe_tk_glu_relu_kernel(tc, xT, w1, w3, w2, gate, offs, pos1, pos2, pos3
             return slice(first * P, last * P)
 
         pair = range(2)
-        halves = [tokens(0, 2), tokens(2, 4)]
+        token_halves = [tokens(0, 2), tokens(2, 4)]
 
         def turn_plain(n, r, cols, targets):
             for target, block in zip(targets, in_blocks(fetch_plain(n, r, cols))):
@@ -381,36 +385,36 @@ def tile_moe_tk_glu_relu_kernel(tc, xT, w1, w3, w2, gate, offs, pos1, pos2, pos3
         turned_sum = psum.tile([P, P], F32, name="turned_sum", tag="y2")
         gated = []
         for r in pair:
-            turn_plain(1, r, halves[0], [turned[0][:, r, place, :] for place in pair])
+            turn_plain(1, r, token_halves[0], [turned[0][:, r, place, :] for place in pair])
             gated.append(fetch(0, r, tokens(1, 4)))
             add_turned(turned_sum[:], gated[r][:, 0:P], r == 0, False)
         third_above = fetch(0, TOP - 1, tokens(0, 4))
         add_turned(turned_sum[:], third_above[:, tokens(1, 2)], False, True)
         for r in pair:
-            turn_plain(1, r, halves[1], [turned[1][:, r, place, :] for place in pair])
+            turn_plain(1, r, token_halves[1], [turned[1][:, r, place, :] for place in pair])
         for r in pair:
             turn_plain(0, r, tokens(0, 1), [upper[:, r, :]])
 
         def store(n, cols, result):
             nc.sync.dma_start(out=out[n * P : (n + 1) * P, cols], in_=result)
 
-        two = new_part("two", halves[1])
+        two = new_part("two", token_halves[1])
         nc.vector.tensor_tensor(two[:], gated[0][:, P:], gated[1][:, P:], ADD)
-        thirds = [fetch(1, TOP - 1, halves[0])]
-        added = new_part("added", halves[1])
-        nc.vector.tensor_tensor(added[:], two[:], third_above[:, halves[1]], ADD)
-        store(0, halves[1], added[:])
-        thirds.append(fetch(1, TOP - 1, halves[1]))
+        thirds = [fetch(1, TOP - 1, token_halves[0])]
+        added = new_part("added", token_halves[1])
+        nc.vector.tensor_tensor(added[:], two[:], third_above[:, token_halves[1]], ADD)
+        store(0, token_halves[1], added[:])
+        thirds.append(fetch(1, TOP - 1, token_halves[1]))
 
         def scale_and_turn_back(name, sources, first_block, tag):
-            places = range(len(sources[0]))
-            scaled = keep.tile([P, 2, len(places), P], F32, name=name)
-            for place in places:
+            spots = range(len(sources[0]))
+            scaled = keep.tile([P, 2, len(spots), P], F32, name=name)
+            for place in spots:
                 for r in pair:
                     gates = gate_columns[:, first_block + place, r : r + 1]
                     nc.scalar.activation(scaled[:, r, place, :], sources[r][place], COPY, scale=gates)
-            bank = psum.tile([P, len(places), P], F32, name="sum_of_two", tag=tag)
-            for place in places:
+            bank = psum.tile([P, len(spots), P], F32, name="sum_of_two", tag=tag)
+            for place in spots:
                 for r in pair:
                     add_turned(bank[:, place, :], scaled[:, r, place, :], r == 0, r == 1)
             return bank[:].rearrange("p b t -> p (b t)")
@@ -424,13 +428,13 @@ def tile_moe_tk_glu_relu_kernel(tc, xT, w1, w3, w2, gate, offs, pos1, pos2, pos3
         upright = psum.tile([P, P], F32, name="upright", tag="w3_1")
         nc.tensor.transpose(upright[:], turned_sb[:], identity[:])
 
-        result = new_part("result1", halves[0])
+        result = new_part("result1", token_halves[0])
         nc.vector.tensor_tensor(result[:], first_below, thirds[0][:], ADD)
-        store(1, halves[0], result[:])
-        result = new_part("result1", halves[1])
+        store(1, token_halves[0], result[:])
+        result = new_part("result1", token_halves[1])
         nc.vector.tensor_tensor(result[:], second_below, thirds[1][:], ADD)
-        store(1, halves[1], result[:])
-        result = new_part("result0", halves[0])
+        store(1, token_halves[1], result[:])
+        result = new_part("result0", token_halves[0])
         nc.vector.tensor_tensor(result[:, 0:P], above, third_above[:, 0:P], ADD)
         nc.scalar.copy(out=result[:, P:], in_=upright[:])
-        store(0, halves[0], result[:])
+        store(0, token_halves[0], result[:])

@@ -265,7 +265,7 @@ def tile_moe_tk_glu_relu_kernel(tc, xT, w1, w3, w2, gate, offs, pos1, pos2, pos3
                 nc.tensor.transpose(bank[:, block, :], gate_rows[:, block * P : (block + 1) * P], identity[:])
             nc.scalar.copy(out=gate_columns[:], in_=bank[:, :, 0:TOP])
             for r in range(TOP):
-                first = 0 if r == TOP - 1 else 1
+                first = 0 if r == TOP - 1 else 2
                 bank = psum.tile([P, T // P, P], F32, name="gate_bank", tag=f"y{r}")
                 for block in blocks[first:]:
                     column = gate_columns[:, block, r : r + 1].to_broadcast([P, P])
@@ -380,61 +380,56 @@ def tile_moe_tk_glu_relu_kernel(tc, xT, w1, w3, w2, gate, offs, pos1, pos2, pos3
             for target, block in zip(targets, in_blocks(fetch_plain(n, r, cols))):
                 nc.tensor.transpose(target, block, identity[:])
 
-        turned = [psum.tile([P, 2, 2, P], F32, name="turned", tag=f"y{q}") for q in pair]
-        upper = psum.tile([P, 2, P], F32, name="upper", tag="y3")
-        turned_sum = psum.tile([P, P], F32, name="turned_sum", tag="y2")
-        gated = []
-        for r in pair:
-            turn_plain(1, r, token_halves[0], [turned[0][:, r, place, :] for place in pair])
-            gated.append(fetch(0, r, tokens(1, 4)))
-            add_turned(turned_sum[:], gated[r][:, 0:P], r == 0, False)
-        third_above = fetch(0, TOP - 1, tokens(0, 4))
-        add_turned(turned_sum[:], third_above[:, tokens(1, 2)], False, True)
-        for r in pair:
-            turn_plain(1, r, token_halves[1], [turned[1][:, r, place, :] for place in pair])
-        for r in pair:
-            turn_plain(0, r, tokens(0, 1), [upper[:, r, :]])
-
         def store(n, cols, result):
             nc.sync.dma_start(out=out[n * P : (n + 1) * P, cols], in_=result)
 
-        two = new_part("two", token_halves[1])
-        nc.vector.tensor_tensor(two[:], gated[0][:, P:], gated[1][:, P:], ADD)
-        thirds = [fetch(1, TOP - 1, token_halves[0])]
-        added = new_part("added", token_halves[1])
-        nc.vector.tensor_tensor(added[:], two[:], third_above[:, token_halves[1]], ADD)
-        store(0, token_halves[1], added[:])
-        thirds.append(fetch(1, TOP - 1, token_halves[1]))
+        def add(name, cols, first, second):
+            result = new_part(name, cols)
+            nc.vector.tensor_tensor(result[:], first, second, ADD)
+            return result
 
-        def scale_and_turn_back(name, sources, first_block, tag):
-            spots = range(len(sources[0]))
-            scaled = keep.tile([P, 2, len(spots), P], F32, name=name)
-            for place in spots:
-                for r in pair:
-                    gates = gate_columns[:, first_block + place, r : r + 1]
-                    nc.scalar.activation(scaled[:, r, place, :], sources[r][place], COPY, scale=gates)
-            bank = psum.tile([P, len(spots), P], F32, name="sum_of_two", tag=tag)
-            for place in spots:
-                for r in pair:
-                    add_turned(bank[:, place, :], scaled[:, r, place, :], r == 0, r == 1)
-            return bank[:].rearrange("p b t -> p (b t)")
+        turned = [psum.tile([P, 2, HALVES, P], F32, name="turned", tag=f"y{b}") for b in pair]
+        lone = psum.tile([P, 2, P], F32, name="lone", tag="y3")
+        turned_sum = psum.tile([P, P], F32, name="turned_sum", tag="y2")
+        for n in (1, 0):
+            for r in pair:
+                turn_plain(n, r, token_halves[0], [turned[b][:, r, n, :] for b in pair])
+        for r in pair:
+            turn_plain(1, r, tokens(2, 3), [lone[:, r, :]])
 
-        below = [[[turned[q][:, r, place, :] for place in pair] for r in pair] for q in pair]
-        first_below = scale_and_turn_back("scaled0", below[0], 0, "w1_0")
-        second_below = scale_and_turn_back("scaled1", below[1], 2, "w1_1")
-        above = scale_and_turn_back("scaled_above", [[upper[:, r, :]] for r in pair], 0, "w3_0")
+        for r in pair:
+            add_turned(turned_sum[:], fetch(1, r, tokens(3, 4))[:], r == 0, False)
+        third_below = fetch(1, TOP - 1, tokens(0, 4))
+        add_turned(turned_sum[:], third_below[:, tokens(3, 4)], False, True)
+        gated = [fetch(0, r, token_halves[1]) for r in range(TOP)]
+        two = add("two", token_halves[1], gated[0][:], gated[1][:])
+        third_above = fetch(0, TOP - 1, token_halves[0])
+        store(0, token_halves[1], add("added", token_halves[1], two[:], gated[2][:])[:])
+
+        def scale(name, source, block, r):
+            scaled = keep.tile([P, source.shape[1]], F32, name=f"{name}{block}_{r}")
+            nc.scalar.activation(scaled[:], source, COPY, scale=gate_columns[:, block, r : r + 1])
+            return scaled
+
+        sums = [psum.tile([P, 2, P], F32, name="sum_of_two", tag=f"w1_{n}") for n in range(HALVES)]
+        for b in pair:
+            scaled = [scale("scaled", turned[b][:, r].rearrange("p n t -> p (n t)"), b, r) for r in pair]
+            for n in (1, 0):
+                for r in pair:
+                    add_turned(sums[n][:, b, :], scaled[r][:, n * P : (n + 1) * P], r == 0, r == 1)
+        lone_sum = psum.tile([P, P], F32, name="lone_sum", tag="w3_0")
+        for r in pair:
+            add_turned(lone_sum[:], scale("scaled", lone[:, r, :], 2, r)[:], r == 0, r == 1)
+
         turned_sb = keep.tile([P, P], F32, name="turned_sb")
         nc.scalar.copy(out=turned_sb[:], in_=turned_sum[:])
         upright = psum.tile([P, P], F32, name="upright", tag="w3_1")
         nc.tensor.transpose(upright[:], turned_sb[:], identity[:])
 
-        result = new_part("result1", token_halves[0])
-        nc.vector.tensor_tensor(result[:], first_below, thirds[0][:], ADD)
-        store(1, token_halves[0], result[:])
+        for n, third in ((1, third_below[:, token_halves[0]]), (0, third_above[:])):
+            result = add(f"result{n}", token_halves[0], sums[n][:].rearrange("p b t -> p (b t)"), third)
+            store(n, token_halves[0], result[:])
         result = new_part("result1", token_halves[1])
-        nc.vector.tensor_tensor(result[:], second_below, thirds[1][:], ADD)
-        store(1, token_halves[1], result[:])
-        result = new_part("result0", token_halves[0])
-        nc.vector.tensor_tensor(result[:, 0:P], above, third_above[:, 0:P], ADD)
         nc.scalar.copy(out=result[:, P:], in_=upright[:])
-        store(0, token_halves[0], result[:])
+        nc.vector.tensor_tensor(result[:, 0:P], lone_sum[:], third_below[:, tokens(2, 3)], ADD)
+        store(1, token_halves[1], result[:])

from contextlib import ExitStack

import concourse.mybir as mybir
from concourse.masks import make_identity

K, T, E, C, H, N = 1024, 512, 6, 256, 512, 256
TOP = 3
SLOTS = E * C
FLOPS = 2 * SLOTS * (2 * K * H + H * N)

F32 = mybir.dt.float32
BF16 = mybir.dt.bfloat16
U32 = mybir.dt.uint32
U16 = mybir.dt.uint16
U8 = mybir.dt.uint8
FP8X4 = mybir.dt.float8_e4m3fn_x4
MULT = mybir.AluOpType.mult
ADD = mybir.AluOpType.add
RELU = mybir.ActivationFunctionType.Relu
COPY = mybir.ActivationFunctionType.Copy

P = 128
PACK = 4
PAIR = 2
PASS = P * PACK
PASSES = K // PASS
HALVES = 2
QUAD = 4
SCALE_STEP = 4
LIST_ROWS = 16
LAST = E - 1

BUFFER = PACK * PASS * 4
ROTATING = 9
AHEAD = ROTATING - 3
EARLY = 3
EARLY_ENTRIES = 384
AMID = 2

X_QUADS = 84
W_QUADS = 96
BEFORE_LAST_QUADS = 64
LAST_QUADS = {("w1", 0): W_QUADS, ("w1", 1): 24, ("w3", 0): 60, ("w3", 1): 86}
LAST_W2_QUADS = 26


def chunk_order():
    order = [("x", 0, s) for s in range(PASSES)]
    for e in range(E):
        if 0 <= e - EARLY < AMID:
            order.append(("w2", e - EARLY, 0))
        order += [(kind, e, s) for kind in ("w1", "w3") for s in range(PASSES)]
    return order


def quads_on_vector(kind, e, s):
    if kind == "x":
        return X_QUADS if s == 0 else 0
    if (kind, e) == ("w3", LAST - 1):
        return BEFORE_LAST_QUADS
    if e == LAST:
        return LAST_QUADS[kind, s]
    return W_QUADS if s == 0 else 0


def tile_moe_tk_glu_relu_kernel(tc, xT, w1, w3, w2, gate, offs, pos1, pos2, pos3, out):
    nc = tc.nc
    with ExitStack() as ctx:
        keep = ctx.enter_context(tc.tile_pool(name="keep", bufs=1))
        buffers = ctx.enter_context(tc.tile_pool(name="buffers", bufs=1))
        groups = ctx.enter_context(tc.tile_pool(name="groups", bufs=3))
        codes = ctx.enter_context(tc.tile_pool(name="codes", bufs=6))
        psum = ctx.enter_context(tc.psum_pool(name="psum", bufs=1))

        offs_sb = keep.tile([P, SLOTS // LIST_ROWS], U16, name="offs_sb")
        pos_sb = [keep.tile([P, T // LIST_ROWS], U16, name=f"pos_sb{r}") for r in range(TOP)]
        x_codes = [keep.tile([P, T], U32, name=f"x_codes{s}", align_bytes=64) for s in range(PASSES)]
        x_scales = keep.tile([P, T], U8, name="x_scales", align_bytes=64)
        gate_rows = keep.tile([P, T], F32, name="gate_rows")
        nc.gpsimd.memset(gate_rows[:], 0.0)
        nc.gpsimd.memset(x_scales[:], 0)
        identity = keep.tile([P, P], F32, name="identity")
        make_identity(nc, identity[:])
        gate_columns = keep.tile([P, T // P, TOP], F32, name="gate_columns")
        gate_sb = [keep.tile([P, T], F32, name=f"gate_sb{r}") for r in range(TOP)]
        y_sb = [keep.tile([P, SLOTS], F32, name=f"y_sb{n}", align_bytes=64) for n in range(HALVES)]

        chunks = chunk_order()
        raw, grouped, packed, banks = {}, {}, {}, {}
        slot_words, slot_scales, relu_a, h_bf, h_packed = {}, {}, {}, {}, {}

        held = [("w3", e, 1) for e in range(E - EARLY)]
        in_turn = [chunk for chunk in chunks if chunk not in held]

        def start_of(chunk):
            if chunk in held:
                return (ROTATING + held.index(chunk)) * BUFFER
            return in_turn.index(chunk) % ROTATING * BUFFER

        def placed(offset, shape, dtype, name):
            return buffers.tile(shape, dtype, name=name, tag=f"{name}_{offset}", align_bytes=64, offset=offset)

        raw2 = {}
        grouped2 = [keep.tile([P, PACK * N], BF16, name=f"grouped2_{e}", align_bytes=64)[:] for e in range(LAST)]
        grouped2.append(y_sb[0][:, AMID * C : (AMID + 2) * C].bitcast(BF16))
        whole = slice(0, N // QUAD)
        on_vector, on_scalar = nc.vector.tensor_copy, nc.scalar.copy

        def load_w2(e, target):
            nc.sync.dma_start(out=target, in_=w2[e].rearrange("(p j) w -> p j w", j=PACK))
            raw2[e] = target

        def interleave_w2(e, quads, engine_copy):
            source = raw2[e].rearrange("p j (m i) -> p m j i", i=QUAD)
            target = grouped2[e].rearrange("p (m i j) -> p m j i", i=QUAD, j=PACK)
            engine_copy(out=target[:, quads], in_=source[:, quads])

        def load(chunk):
            kind, e, s = chunk
            if kind == "w2":
                load_w2(e, placed(start_of(chunk), [P, PACK, N], F32, "raw2")[:])
                return
            tile = placed(start_of(chunk), [P, PACK, PASS], F32, "raw")
            rows = {"x": xT, "w1": w1[e], "w3": w3[e]}[kind][s * PASS : (s + 1) * PASS, :]
            nc.sync.dma_start(out=tile[:], in_=rows.rearrange("(p j) w -> p j w", j=PACK))
            raw[chunk] = tile

        def interleave(chunk):
            kind, e, s = chunk
            tile = raw.pop(chunk)
            if s == 0:
                target = groups.tile([P, PASSES, PACK * PASS], BF16, name="grouped", align_bytes=64)
            else:
                target = grouped[kind, e, 0]
            flat = target[:, s, :]
            grouped[chunk] = target
            source = tile[:].rearrange("p j (m i) -> p m j i", i=QUAD)
            if kind in ("w1", "w3"):
                flat = flat.rearrange("p (i m j) -> p m j i", i=QUAD, j=PACK)
            else:
                flat = flat.rearrange("p (m i j) -> p m j i", i=QUAD, j=PACK)
            cut = quads_on_vector(kind, e, s)
            if cut > 0:
                nc.vector.tensor_copy(out=flat[:, :cut], in_=source[:, :cut])
            nc.scalar.copy(out=flat[:, cut:], in_=source[:, cut:])

        def quantise_w2(e):
            words = keep.tile([P, N], U32, name=f"w2_codes{e}", align_bytes=64)
            scales = keep.tile([P, N], U8, name=f"w2_scales{e}", align_bytes=64)
            nc.vector.quantize_mx(out=words[:].bitcast(FP8X4), scales=scales[:], in_=grouped2[e])
            for n in range(HALVES):
                cols = slice(n * P, (n + 1) * P)
                packed["w2", e, n] = (words[:, cols], scales[:, cols])

        def quantise_tokens(s):
            nc.vector.quantize_mx(
                out=x_codes[s][:].bitcast(FP8X4), scales=x_scales[SCALE_STEP * s : P, :], in_=grouped["x", 0, s][:, s, :]
            )

        def quantise_matrix(kind, e):
            words = codes.tile([P, PASSES, H], U32, name="w_codes", align_bytes=64)
            scales = codes.tile([P, PASSES, H], U8, name="w_scales", align_bytes=64)
            nc.vector.quantize_mx(
                out=words[:].rearrange("p s w -> p (s w)").bitcast(FP8X4),
                scales=scales[:].rearrange("p s w -> p (s w)"),
                in_=grouped[kind, e, 0][:].rearrange("p s w -> p (s w)"),
            )
            for s in range(PASSES):
                packed[kind, e, s] = (words[:, s, :], scales[:, s, :])

        def quantise_pass(kind, e, s):
            words = codes.tile([P, H], U32, name="w_codes", align_bytes=64)
            scales = codes.tile([P, H], U8, name="w_scales", align_bytes=64)
            nc.vector.quantize_mx(out=words[:].bitcast(FP8X4), scales=scales[:], in_=grouped[kind, e, s][:, s, :])
            packed[kind, e, s] = (words, scales)

        def gather(target, window, first, count):
            entries = offs_sb[:, first // LIST_ROWS : (first + count) // LIST_ROWS]
            nc.vector.tensor_copy(target, window[:].indirect(entries))

        def gather_early(window, dtype, name):
            tile = keep.tile([P, EARLY * C], dtype, name=name, align_bytes=64)
            for first in range(0, EARLY * C, EARLY_ENTRIES):
                gather(tile[:, first : first + EARLY_ENTRIES], window, first, EARLY_ENTRIES)
            return [tile[:, e * C : (e + 1) * C] for e in range(EARLY)]

        def gather_late(e, offset):
            for s in range(PASSES):
                slot_words[e, s] = placed(offset + s * 4 * C, [P, C], U32, "slot_codes")[:]
                gather(slot_words[e, s], x_codes[s], e * C, C)
            slot_scales[e] = placed(offset + PASSES * 4 * C, [P, C], U8, "slot_scales")[:]
            gather(slot_scales[e], x_scales, e * C, C)

        def first_product(kind, e, passes):
            for u in range(HALVES):
                if kind == "w1":
                    planes, cols = range(PAIR * u, PAIR * (u + 1)), slice(0, C)
                else:
                    planes, cols = range(PACK), slice(u * P, (u + 1) * P)
                if passes[0] == 0:
                    shape = [P, len(planes), cols.stop - cols.start]
                    banks[kind, e, u] = psum.tile(shape, F32, name="bank", tag=f"{kind}_{u}")
                for s in passes:
                    words, scales = packed[kind, e, s]
                    for place, t in enumerate(planes):
                        rows = slice(t * P, (t + 1) * P)
                        nc.tensor.matmul_mx(
                            out=banks[kind, e, u][:, place, :],
                            lhsT=words[:, rows].bitcast(FP8X4),
                            lhsT_scale=scales[:, rows],
                            rhs=slot_words[e, s][:, cols].bitcast(FP8X4),
                            rhs_scale=slot_scales[e][SCALE_STEP * s : P, cols],
                            start=(s == 0 and place == 0),
                            stop=(s == PASSES - 1 and place == len(planes) - 1),
                        )

        def take_relu(e, offset):
            relu_a[e] = placed(offset, [P, HALVES, C, PAIR], F32, "relu_a")
            for u in range(HALVES):
                nc.scalar.activation(relu_a[e][:, u], banks["w1", e, u][:].rearrange("p t c -> p c t"), RELU)

        def take_h(e, offset):
            h_bf[e] = placed(offset, [P, C, HALVES, PAIR], BF16, "h_bf")
            for half in range(HALVES):
                cols = slice(half * P, (half + 1) * P)
                nc.vector.tensor_tensor(
                    h_bf[e][:, cols],
                    banks["w3", e, half][:].rearrange("p (u v) c -> p c u v", v=PAIR),
                    relu_a[e][:].rearrange("p u c v -> p c u v")[:, cols],
                    MULT,
                )

        def quantise_h(e):
            words = keep.tile([P, C], U32, name=f"h_codes{e}", align_bytes=64)
            scales = keep.tile([P, C], U8, name=f"h_scales{e}", align_bytes=64)
            nc.vector.quantize_mx(
                out=words[:].bitcast(FP8X4), scales=scales[:], in_=h_bf[e][:].rearrange("p c u v -> p (c u v)")
            )
            h_packed[e] = (words, scales)

        def second_product(e, n, target):
            words, scales = packed["w2", e, n]
            h_words, h_scales = h_packed[e]
            nc.tensor.matmul_mx(
                out=target,
                lhsT=words.bitcast(FP8X4),
                lhsT_scale=scales,
                rhs=h_words[:].bitcast(FP8X4),
                rhs_scale=h_scales[:],
                start=True,
                stop=True,
            )

        def take_y(experts, n, tag, engine_copy):
            bank = psum.tile([P, len(experts) * C], F32, name="bank_y", tag=tag)
            for place, e in enumerate(experts):
                second_product(e, n, bank[:, place * C : (place + 1) * C])
            engine_copy(out=y_sb[n][:, experts[0] * C : (experts[-1] + 1) * C], in_=bank[:])

        blocks = range(T // P)

        def spread_gates():
            bank = psum.tile([P, T // P, P], F32, name="gate_bank", tag="y3")
            for block in blocks:
                nc.tensor.transpose(bank[:, block, :], gate_rows[:, block * P : (block + 1) * P], identity[:])
            nc.scalar.copy(out=gate_columns[:], in_=bank[:, :, 0:TOP])
            for r in range(TOP):
                first = 0 if r == TOP - 1 else 2
                bank = psum.tile([P, T // P, P], F32, name="gate_bank", tag=f"y{r}")
                for block in blocks[first:]:
                    column = gate_columns[:, block, r : r + 1].to_broadcast([P, P])
                    nc.tensor.transpose(bank[:, block, :], column, identity[:])
                nc.scalar.copy(out=gate_sb[r][:, first * P :], in_=bank[:, first:, :].rearrange("q b p -> q (b p)"))

        def work(chunk):
            kind, e, s = chunk
            if kind == "w2":
                interleave_w2(e, whole, on_vector)
                quantise_w2(e)
                for n in range(HALVES):
                    take_y([e], n, f"y{n}", on_scalar)
                return
            interleave(chunk)
            if kind == "x":
                quantise_tokens(s)
                if s == PASSES - 1:
                    spread_gates()
                for other, words in enumerate(gather_early(x_codes[s], U32, f"early_codes{s}")):
                    slot_words[other, s] = words
                if s == PASSES - 1:
                    for other, scales in enumerate(gather_early(x_scales, U8, "early_scales")):
                        slot_scales[other] = scales
                return
            if (kind, s) == ("w1", 0) and e > 0:
                take_h(e - 1, start_of(chunk))
                quantise_h(e - 1)
            if e == LAST or (kind, e) == ("w3", LAST - 1):
                quantise_pass(kind, e, s)
                if (kind, s) == ("w3", 1):
                    take_relu(e, start_of(chunk))
                first_product(kind, e, [s])
                return
            if s == 0:
                return
            quantise_matrix(kind, e)
            if kind == "w3":
                if chunk in held:
                    gather_late(e + EARLY, start_of(chunk) + BUFFER // 2)
                take_relu(e, start_of(chunk))
            first_product(kind, e, range(PASSES))

        for step in range(-AHEAD, len(chunks)):
            if step + AHEAD < len(chunks):
                load(chunks[step + AHEAD])
                if step + AHEAD == 0:
                    nc.sync.dma_start(offs_sb[:], offs)
                if step + AHEAD == 1:
                    nc.sync.dma_start(out=gate_rows[0:TOP, :], in_=gate[:, 0, :])
            if step >= 0:
                work(chunks[step])

        next_buffers = [(len(in_turn) + turn) % ROTATING * BUFFER for turn in range(3)]
        for e in range(AMID, LAST):
            offset = next_buffers[(e - AMID) // 2] + (e - AMID) % 2 * BUFFER // 2
            load_w2(e, placed(offset, [P, PACK, N], F32, "raw2")[:])
        load_w2(LAST, y_sb[1][:, AMID * C :].rearrange("p (j w) -> p j w", j=PACK))
        for r, pos in enumerate((pos1, pos2, pos3)):
            nc.sync.dma_start(pos_sb[r][:], pos)

        interleave_w2(2, whole, on_vector)
        take_h(LAST, next_buffers[-1])
        interleave_w2(3, whole, on_scalar)
        quantise_w2(2)
        quantise_w2(3)
        quantise_h(LAST)
        interleave_w2(4, whole, on_scalar)
        quantise_w2(4)
        interleave_w2(LAST, slice(0, LAST_W2_QUADS), on_vector)
        interleave_w2(LAST, slice(LAST_W2_QUADS, N // QUAD), on_scalar)
        quantise_w2(LAST)
        take_y([2, 3], 1, "y1", on_scalar)
        take_y([2, 3], 0, "y0", on_vector)
        bank = psum.tile([P, HALVES, C], F32, name="bank_y", tag="y2")
        for n in range(HALVES):
            second_product(LAST - 1, n, bank[:, n, :])
        for n, engine_copy in ((1, on_scalar), (0, on_vector)):
            engine_copy(out=y_sb[n][:, (LAST - 1) * C : LAST * C], in_=bank[:, n, :])
        take_y([LAST], 1, "y3", on_scalar)
        take_y([LAST], 0, "y1", on_vector)

        def entries(r, cols):
            return pos_sb[r][:, cols.start // LIST_ROWS : cols.stop // LIST_ROWS]

        def new_part(name, cols):
            return keep.tile([P, cols.stop - cols.start], F32, name=f"{name}_{cols.start}")

        def in_blocks(part):
            return [part[:, start : start + P] for start in range(0, part[:].shape[1], P)]

        def fetch(n, r, cols):
            part = new_part(f"part{n}_{r}", cols)
            nc.vector.tensor_tensor(part[:], y_sb[n][:].indirect(entries(r, cols)), gate_sb[r][:, cols], MULT)
            return part

        def fetch_plain(n, r, cols):
            part = new_part(f"part{n}_{r}", cols)
            nc.scalar.activation(part[:], y_sb[n][:].indirect(entries(r, cols)), COPY)
            return part

        def add_turned(target, source, first, last):
            nc.tensor.matmul(target, lhsT=source, rhs=identity[:], is_transpose=True, start=first, stop=last)

        def tokens(first, last):
            return slice(first * P, last * P)

        pair = range(2)
        token_halves = [tokens(0, 2), tokens(2, 4)]

        def turn_plain(n, r, cols, targets):
            for target, block in zip(targets, in_blocks(fetch_plain(n, r, cols))):
                nc.tensor.transpose(target, block, identity[:])

        def store(n, cols, result):
            nc.sync.dma_start(out=out[n * P : (n + 1) * P, cols], in_=result)

        def add(name, cols, first, second):
            result = new_part(name, cols)
            nc.vector.tensor_tensor(result[:], first, second, ADD)
            return result

        turned = [psum.tile([P, 2, HALVES, P], F32, name="turned", tag=f"y{b}") for b in pair]
        lone = psum.tile([P, 2, P], F32, name="lone", tag="y3")
        turned_sum = psum.tile([P, P], F32, name="turned_sum", tag="y2")
        for n in (1, 0):
            for r in pair:
                turn_plain(n, r, token_halves[0], [turned[b][:, r, n, :] for b in pair])
        for r in pair:
            turn_plain(1, r, tokens(2, 3), [lone[:, r, :]])

        for r in pair:
            add_turned(turned_sum[:], fetch(1, r, tokens(3, 4))[:], r == 0, False)
        third_below = fetch(1, TOP - 1, tokens(0, 4))
        add_turned(turned_sum[:], third_below[:, tokens(3, 4)], False, True)
        gated = [fetch(0, r, token_halves[1]) for r in range(TOP)]
        two = add("two", token_halves[1], gated[0][:], gated[1][:])
        third_above = fetch(0, TOP - 1, token_halves[0])
        store(0, token_halves[1], add("added", token_halves[1], two[:], gated[2][:])[:])

        def scale(name, source, block, r):
            scaled = keep.tile([P, source.shape[1]], F32, name=f"{name}{block}_{r}")
            nc.scalar.activation(scaled[:], source, COPY, scale=gate_columns[:, block, r : r + 1])
            return scaled

        sums = [psum.tile([P, 2, P], F32, name="sum_of_two", tag=f"w1_{n}") for n in range(HALVES)]
        for b in pair:
            scaled = [scale("scaled", turned[b][:, r].rearrange("p n t -> p (n t)"), b, r) for r in pair]
            for n in (1, 0):
                for r in pair:
                    add_turned(sums[n][:, b, :], scaled[r][:, n * P : (n + 1) * P], r == 0, r == 1)
        lone_sum = psum.tile([P, P], F32, name="lone_sum", tag="w3_0")
        for r in pair:
            add_turned(lone_sum[:], scale("scaled", lone[:, r, :], 2, r)[:], r == 0, r == 1)

        turned_sb = keep.tile([P, P], F32, name="turned_sb")
        nc.scalar.copy(out=turned_sb[:], in_=turned_sum[:])
        upright = psum.tile([P, P], F32, name="upright", tag="w3_1")
        nc.tensor.transpose(upright[:], turned_sb[:], identity[:])

        for n, third in ((1, third_below[:, token_halves[0]]), (0, third_above[:])):
            result = add(f"result{n}", token_halves[0], sums[n][:].rearrange("p b t -> p (b t)"), third)
            store(n, token_halves[0], result[:])
        result = new_part("result1", token_halves[1])
        nc.scalar.copy(out=result[:, P:], in_=upright[:])
        nc.vector.tensor_tensor(result[:, 0:P], lone_sum[:], third_below[:, tokens(2, 3)], ADD)
        store(1, token_halves[1], result[:])
